import numpy as np
import ml_dtypes


def mxq(x, axis, fmt="e4m3"):
    dtype, down = {"e4m3": (ml_dtypes.float8_e4m3fn, 7), "e5m2": (ml_dtypes.float8_e5m2, 14)}[fmt]
    v = np.moveaxis(np.asarray(x, np.float32).astype(ml_dtypes.bfloat16).astype(np.float64), axis, -1)
    blocks = v.reshape(v.shape[:-1] + (-1, 32))
    amax = np.abs(blocks).max(-1, keepdims=True)
    byte = np.maximum(np.where(amax > 0, np.frexp(amax)[1] - 1 + 127, 0) - down, 1)
    scale = np.exp2(byte - 127.0)
    codes = (blocks / scale).astype(np.float32).astype(dtype).astype(np.float64)
    return np.moveaxis((codes * scale).reshape(v.shape), -1, axis)


WIDE = False


def mx_kscale(k):
    if not WIDE:
        return np.ones(k)
    levels = np.array([10, -10, 5, -5, 0])
    if k % 512:
        return np.exp2(np.random.permutation(np.resize(levels, k // 32))).repeat(32)
    a = np.empty((k // 512, 16))
    for p in range(k // 512):
        a[p, :8] = np.random.permutation(np.resize(levels, 8))
        for g in range(8):
            far = levels[np.abs(levels - a[p, g]) >= 10]
            a[p, g + 8] = far[np.random.randint(len(far))]
    return np.exp2(a.ravel()).repeat(32)


def f64(x):
    return np.asarray(x).astype(np.float64)


def striped(idx):
    return np.tile(idx.reshape(-1, 16).T, (8, 1)).astype(np.uint16)


def unstriped(offs):
    return offs[:16].T.reshape(-1).astype(np.int64)


E2M1 = np.array([0.0, 0.5, 1.0, 1.5, 2.0, 3.0, 4.0, 6.0, -0.0, -0.5, -1.0, -1.5, -2.0, -3.0, -4.0, -6.0])


def pack_weight(w, fmt):
    k, n = w.shape
    w = f64(np.asarray(w, np.float32).astype(ml_dtypes.bfloat16)).reshape(k // 32, 32, n)
    amax = np.abs(w).max(1)
    if fmt == "e4m3":
        byte = np.frexp(amax)[1] - 1 + 127 - 7
    else:
        mant, ex = np.frexp(amax / 6.0)
        byte = np.where(mant > 0.5, ex, ex - 1) + 127
    byte = np.clip(np.where(amax > 0, byte, 1), 1, 254)
    scaled = (w * np.exp2(127.0 - byte)[:, None, :]).reshape(k, n).astype(np.float32)
    by_word = np.ascontiguousarray(scaled.reshape(k // 512, 128, 4, n).transpose(0, 1, 3, 2))
    if fmt == "e4m3":
        words = by_word.astype(ml_dtypes.float8_e4m3fn).view(np.uint8)
    else:
        c = by_word.astype(ml_dtypes.float4_e2m1fn).view(np.uint8) & 0xF
        words = (c[..., 0::2] | (c[..., 1::2] << 4)).reshape(k // 512, 128, 2 * n)
    return np.ascontiguousarray(words), np.ascontiguousarray(byte.astype(np.uint8).reshape(k // 512, 16, n))


def unpack_weight(words, scales, fmt):
    g, _, n = scales.shape
    words = np.ascontiguousarray(words).reshape(g, 128, n, -1)
    if fmt == "e4m3":
        vals = words.view(ml_dtypes.float8_e4m3fn).astype(np.float64)
    else:
        nib = np.empty((g, 128, n, 4), np.uint8)
        nib[..., 0::2] = words & 0xF
        nib[..., 1::2] = words >> 4
        vals = E2M1[nib]
    vals = vals * np.repeat(np.exp2(scales.astype(np.float64) - 127.0), 8, axis=1)[..., None]
    return vals.transpose(0, 1, 3, 2).reshape(g * 512, n)


def relu(v):
    return np.maximum(v, 0.0)


K, T, E, C, H, N = 1536, 512, 4, 256, 512, 256


def by_expert(wq, xq):
    return np.concatenate([wq[e].T @ xq[:, e * C:(e + 1) * C] for e in range(E)], axis=1)


def setup_inputs():
    n = np.random.standard_normal
    s = mx_kscale(K)[:, None]
    u = mx_kscale(H)
    first = np.random.permutation(np.repeat(np.arange(E), T // E))
    second = (first + 1 + np.random.permutation(np.repeat(np.arange(E - 1), -(-T // (E - 1)))[:T])) % E
    while np.bincount(second, minlength=E).max() != T // E:
        load = np.bincount(second, minlength=E); hi, lo = int(load.argmax()), int(load.argmin())
        t = np.flatnonzero((second == hi) & (first != lo))[0]; second[t] = lo
    slot_token = np.empty(E * C, np.int64); pos = np.empty((2, T), np.int64); fill = np.zeros(E, np.int64)
    place = np.stack([np.random.permutation(C) for _ in range(E)])
    for r, deal in enumerate((first, second)):
        for t in np.random.permutation(T):
            e = deal[t]; j = e * C + place[e, fill[e]]; fill[e] += 1; slot_token[j] = t; pos[r, t] = j
    g = np.random.uniform(0.2, 0.8, T)
    w1 = [pack_weight(m, "e2m1") for m in n((E, K, H)) / np.sqrt(K) / s[None]]
    w3 = [pack_weight(m, "e2m1") for m in n((E, K, H)) / np.sqrt(K) / s[None] * u[None, None, :]]
    w2 = [pack_weight(m, "e2m1") for m in n((E, H, N)) / np.sqrt(H) / u[None, :, None]]
    w_slot = np.empty(E * C); w_slot[pos[0]] = g; w_slot[pos[1]] = 1.0 - g
    return {
        "xT": (n((K, T)) * s).astype(np.float32),
        "w1_words": np.stack([m[0] for m in w1]),
        "w1_scales": np.stack([m[1] for m in w1]),
        "w3_words": np.stack([m[0] for m in w3]),
        "w3_scales": np.stack([m[1] for m in w3]),
        "w2_words": np.stack([m[0] for m in w2]),
        "w2_scales": np.stack([m[1] for m in w2]),
        "gate": np.tile(w_slot, (K, 1)).astype(np.float32),
        "offs": striped(slot_token),
        "pos1": striped(pos[0]),
        "pos2": striped(pos[1]),
    }


def reference(xT, w1_words, w1_scales, w3_words, w3_scales, w2_words, w2_scales, gate, offs, pos1, pos2):
    idx = unstriped(offs)
    w1 = np.stack([unpack_weight(w1_words[e], w1_scales[e], "e2m1") for e in range(E)])
    w3 = np.stack([unpack_weight(w3_words[e], w3_scales[e], "e2m1") for e in range(E)])
    w2 = np.stack([unpack_weight(w2_words[e], w2_scales[e], "e2m1") for e in range(E)])
    xq = mxq(f64(gate) * f64(xT)[:, idx], 0, "e4m3")
    h = relu(by_expert(w1, xq))
    h = h * by_expert(w3, xq)
    y = by_expert(w2, mxq(h, 0, "e4m3"))
    return y[:, unstriped(pos1)] + y[:, unstriped(pos2)]

@@ -1,0 +1,238 @@
+from contextlib import ExitStack
+
+import concourse.mybir as mybir
+from concourse.masks import make_identity
+
+K, T, E, C, H, N = 1536, 512, 4, 256, 512, 256
+S = E * C
+P = 128
+PACK = 4
+PASSES = K // (P * PACK)
+TILES = S // P
+
+FLOPS = 2 * S * (2 * K * H + H * N)
+BYTES = 4 * K * T + E * (2 * K * H + H * N) // 2 + E * (2 * K * H + H * N) // 32 + 4 * P * S + 2 * P * (S + 2 * T) // 16 + 4 * N * T
+
+F32 = mybir.dt.float32
+BF16 = mybir.dt.bfloat16
+I32 = mybir.dt.int32
+U32 = mybir.dt.uint32
+U16 = mybir.dt.uint16
+U8 = mybir.dt.uint8
+FP8X4 = mybir.dt.float8_e4m3fn_x4
+FP4X4 = mybir.dt.float4_e2m1fn_x4
+MULT = mybir.AluOpType.mult
+ADD = mybir.AluOpType.add
+RELU = mybir.ActivationFunctionType.Relu
+
+QUANT_WORDS = (256, 128)
+FIRST = 384
+
+
+def tile_moe_pre_glu_relu_kernel(
+    tc, xT, w1_words, w1_scales, w3_words, w3_scales, w2_words, w2_scales, gate, offs, pos1, pos2, out
+):
+    nc = tc.nc
+    with ExitStack() as ctx:
+        keep = ctx.enter_context(tc.tile_pool(name="keep", bufs=1))
+        stage = ctx.enter_context(tc.tile_pool(name="stage", bufs=3))
+        psum = ctx.enter_context(tc.psum_pool(name="psum", bufs=1))
+
+        offs_sb = keep.tile([P, S // 16], U16, name="offs_sb")
+        pos1_sb = keep.tile([P, T // 16], U16, name="pos1_sb")
+        pos2_sb = keep.tile([P, T // 16], U16, name="pos2_sb")
+        gate_sb = keep.tile([P, S], F32, name="gate_sb")
+        planes = [[keep.tile([P, T], F32, name=f"x{s}{t}") for t in range(PACK)] for s in range(PASSES)]
+        w1c = keep.tile([P, E, PASSES, 2 * H], U8, name="w1c", align_bytes=64)
+        w3c = keep.tile([P, E, PASSES, 2 * H], U8, name="w3c", align_bytes=64)
+        w2c = keep.tile([P, E, 2 * N], U8, name="w2c", align_bytes=64)
+        w1s = keep.tile([P, E * PASSES, H], U8, name="w1s", align_bytes=64)
+        w3s = keep.tile([P, E * PASSES, H], U8, name="w3s", align_bytes=64)
+        w2s = keep.tile([P, E, N], U8, name="w2s", align_bytes=64)
+        xq = keep.tile([P, PASSES, S], U32, name="xq", align_bytes=64)
+        xs = keep.tile([P, PASSES, S], U8, name="xs", align_bytes=64)
+        hq = keep.tile([P, S], U32, name="hq", align_bytes=64)
+        hs = keep.tile([P, S], U8, name="hs", align_bytes=64)
+        y = keep.tile([P, N // P, S], F32, name="y")
+        ident = keep.tile([P, P], F32, name="ident")
+
+        make_identity(nc, ident[:])
+        for plane in (w1s, w3s, w2s):
+            nc.vector.memset(plane[:].bitcast(I32), 0)
+
+        nc.sync.dma_start(offs_sb[:], offs)
+        nc.sync.dma_start(gate_sb[:, :FIRST], gate[:P, :FIRST])
+        x_rows = xT.rearrange("(s p t) c -> s t p c", p=P, t=PACK)
+        for s in range(PASSES):
+            for t in range(PACK):
+                nc.sync.dma_start(planes[s][t][:], x_rows[s, t])
+        nc.sync.dma_start(gate_sb[:, FIRST:], gate[:P, FIRST:])
+        for plane, scales in ((w1s, w1_scales), (w3s, w3_scales), (w2s, w2_scales)):
+            for r in range(4):
+                nc.sync.dma_start(
+                    plane[r:P:32].bitcast(I32),
+                    scales.rearrange("e s (q r) n -> r q (e s) n", r=4)[r].bitcast(I32),
+                )
+        for e in range(E):
+            for codes, words in ((w1c, w1_words), (w3c, w3_words)):
+                nc.sync.dma_start(codes[:, e].bitcast(I32), words[e].rearrange("s p b -> p s b").bitcast(I32))
+            if e == 0:
+                nc.sync.dma_start(w2c[:].bitcast(I32), w2_words.rearrange("e s p b -> p (e s) b").bitcast(I32))
+        nc.sync.dma_start(pos1_sb[:], pos1)
+        nc.sync.dma_start(pos2_sb[:], pos2)
+
+        rounded = {}
+        banks = {}
+        relu_a = {}
+        turned = {}
+
+        def gather(s, lo, hi):
+            n = hi - lo
+            g4 = stage.tile([P, PACK, n], F32, name="g4")
+            for t in range(PACK):
+                nc.vector.tensor_tensor(
+                    g4[:, t, :], planes[s][t][:].indirect(offs_sb[:, lo // 16 : hi // 16]), gate_sb[:, lo:hi], MULT
+                )
+            xb = stage.tile([P, n * PACK], BF16, name="xb", align_bytes=64)
+            nc.scalar.copy(xb[:].rearrange("p (c t) -> p c t", t=PACK), g4[:].rearrange("p t c -> p c t"))
+            rounded[s, lo] = xb
+
+        def quantize_x(s, lo, hi):
+            xb = rounded[s, lo]
+            c = lo
+            while c < hi:
+                w = max(q for q in QUANT_WORDS if q <= hi - c)
+                nc.vector.quantize_mx(
+                    out=xq[:, s, c : c + w].bitcast(FP8X4),
+                    scales=xs[:, s, c : c + w],
+                    in_=xb[:, (c - lo) * PACK : (c - lo + w) * PACK],
+                )
+                c += w
+
+        def first_layer(j, passes):
+            e = j * P // C
+            cols = slice(j * P, (j + 1) * P)
+            if j not in banks:
+                banks[j] = (
+                    psum.tile([P, H], F32, name="acc_a", bufs=2),
+                    psum.tile([P, H], F32, name="acc_b", bufs=4),
+                )
+            for s in passes:
+                for acc, codes, plane in zip(banks[j], (w1c, w3c), (w1s, w3s)):
+                    nc.tensor.matmul_mx(
+                        out=acc[:],
+                        lhsT=xq[:, s, cols].bitcast(FP8X4),
+                        lhsT_scale=xs[:, s, cols],
+                        rhs=codes[:, e, s, :].bitcast(FP4X4),
+                        rhs_scale=plane[:, e * PASSES + s, :],
+                        start=(s == 0),
+                        stop=(s == PASSES - 1),
+                    )
+            if passes[-1] == PASSES - 1:
+                r = stage.tile([P, H], F32, name="r", bufs=4)
+                nc.scalar.activation(
+                    r[:].rearrange("j (u p d) -> j u p d", u=2, d=2),
+                    banks[j][0][:].rearrange("j (p u d) -> j u p d", u=2, d=2),
+                    RELU,
+                )
+                relu_a[j] = r
+
+        def hidden(j):
+            hb = stage.tile([P, H], BF16, name="hb")
+            nc.vector.tensor_tensor(
+                hb[:].rearrange("j (u p d) -> j u p d", u=2, d=2),
+                banks[j][1][:].rearrange("j (p u d) -> j u p d", u=2, d=2),
+                relu_a[j][:].rearrange("j (u p d) -> j u p d", u=2, d=2),
+                MULT,
+            )
+            words = hb[:].bitcast(F32)
+            ht = psum.tile([P, 2, P], F32, name="ht")
+            for u in range(2):
+                nc.tensor.transpose(ht[:, u, :], words[:, u * P : (u + 1) * P], ident[:])
+            hi4 = stage.tile([P, P * PACK], BF16, name="hi4", align_bytes=64)
+            nc.scalar.copy(hi4[:].bitcast(F32).rearrange("p (j u) -> p j u", u=2), ht[:].rearrange("p u j -> p j u"))
+            turned[j] = hi4
+
+        def second_layer(j):
+            e = j * P // C
+            cols = slice(j * P, (j + 1) * P)
+            nc.vector.quantize_mx(out=hq[:, cols].bitcast(FP8X4), scales=hs[:, cols], in_=turned[j][:])
+            acc_y = psum.tile([P, N // P, P], F32, name="acc_y")
+            for m in range(N // P):
+                nc.tensor.matmul_mx(
+                    out=acc_y[:, m, :],
+                    lhsT=w2c[:, e, 2 * m * P : 2 * (m + 1) * P].bitcast(FP4X4),
+                    lhsT_scale=w2s[:, e, m * P : (m + 1) * P],
+                    rhs=hq[:, cols].bitcast(FP8X4),
+                    rhs_scale=hs[:, cols],
+                    start=True,
+                    stop=True,
+                )
+            nc.scalar.copy(y[:, :, cols], acc_y[:])
+
+        all_passes = list(range(PASSES))
+        A, B = (0, 384), (384, 768)
+        gather(0, *A)
+        gather(1, *A)
+        quantize_x(0, *A)
+        gather(2, *A)
+        quantize_x(1, *A)
+        gather(0, *B)
+        quantize_x(2, *A)
+        for j in (0, 1, 2):
+            first_layer(j, all_passes)
+        gather(1, *B)
+        quantize_x(0, *B)
+        gather(2, *B)
+        quantize_x(1, *B)
+        hidden(0)
+        hidden(1)
+        gather(0, 768, 1024)
+        quantize_x(2, *B)
+        for j in (3, 4, 5):
+            first_layer(j, all_passes)
+        hidden(2)
+        second_layer(0)
+        second_layer(1)
+        gather(1, 768, 1024)
+        quantize_x(0, 768, 1024)
+        hidden(3)
+        second_layer(2)
+        gather(2, 768, 896)
+        quantize_x(1, 768, 1024)
+        first_layer(6, [0, 1])
+        first_layer(7, [0, 1])
+        gather(2, 896, 1024)
+        quantize_x(2, 768, 896)
+        first_layer(6, [2])
+        second_layer(3)
+        hidden(4)
+        quantize_x(2, 896, 1024)
+        first_layer(7, [2])
+        hidden(5)
+        hidden(6)
+        second_layer(4)
+        hidden(7)
+        second_layer(5)
+        second_layer(6)
+        second_layer(7)
+
+        pieces = ((0, 0, T), (1, 0, T // 2), (1, T // 2, T))
+        pending = None
+        for m, lo, hi in pieces:
+            got = []
+            for pos in (pos1_sb, pos2_sb):
+                g = stage.tile([P, hi - lo], F32, name="g", bufs=6)
+                nc.vector.tensor_copy(g[:], y[:, m, :].indirect(pos[:, lo // 16 : hi // 16]))
+                got.append(g)
+                if pending is not None:
+                    pending()
+                    pending = None
+
+            def finish(m=m, lo=lo, hi=hi, got=got):
+                res = stage.tile([P, hi - lo], F32, name="res")
+                nc.vector.tensor_tensor(res[:], got[0][:], got[1][:], ADD)
+                nc.sync.dma_start(out[m * P : (m + 1) * P, lo:hi], res[:])
+
+            pending = finish
+        pending()

@@ -25,8 +25,10 @@ MULT = mybir.AluOpType.mult
 ADD = mybir.AluOpType.add
 RELU = mybir.ActivationFunctionType.Relu
 
-QUANT_WORDS = (256, 128)
-FIRST = 384
+GROUPS = ((0, 512), (512, 768), (768, 1024))
+FIRST = GROUPS[0][1]
+PAD = 32
+HEAD = 128
 
 
 def tile_moe_pre_glu_relu_kernel(
@@ -36,36 +38,42 @@ def tile_moe_pre_glu_relu_kernel(
     with ExitStack() as ctx:
         keep = ctx.enter_context(tc.tile_pool(name="keep", bufs=1))
         stage = ctx.enter_context(tc.tile_pool(name="stage", bufs=3))
-        psum = ctx.enter_context(tc.psum_pool(name="psum", bufs=1))
+        psum = ctx.enter_context(tc.psum_pool(name="psum", bufs=8))
 
         offs_sb = keep.tile([P, S // 16], U16, name="offs_sb")
         pos1_sb = keep.tile([P, T // 16], U16, name="pos1_sb")
         pos2_sb = keep.tile([P, T // 16], U16, name="pos2_sb")
         gate_sb = keep.tile([P, S], F32, name="gate_sb")
-        planes = [[keep.tile([P, T], F32, name=f"x{s}{t}") for t in range(PACK)] for s in range(PASSES)]
+        planes = [[keep.tile([P, T + PAD], F32, name=f"x{s}{t}") for t in range(PACK)] for s in range(PASSES)]
         w1c = keep.tile([P, E, PASSES, 2 * H], U8, name="w1c", align_bytes=64)
         w3c = keep.tile([P, E, PASSES, 2 * H], U8, name="w3c", align_bytes=64)
         w2c = keep.tile([P, E, 2 * N], U8, name="w2c", align_bytes=64)
         w1s = keep.tile([P, E * PASSES, H], U8, name="w1s", align_bytes=64)
         w3s = keep.tile([P, E * PASSES, H], U8, name="w3s", align_bytes=64)
         w2s = keep.tile([P, E, N], U8, name="w2s", align_bytes=64)
-        xq = keep.tile([P, PASSES, S], U32, name="xq", align_bytes=64)
-        xs = keep.tile([P, PASSES, S], U8, name="xs", align_bytes=64)
+        xb = keep.tile([P, PASSES * S * PACK + H // 2], BF16, name="xb", align_bytes=64)
+        xq = keep.tile([P, PASSES * S], U32, name="xq", align_bytes=64)
+        xs = keep.tile([P, PASSES * S], U8, name="xs", align_bytes=64)
         hq = keep.tile([P, S], U32, name="hq", align_bytes=64)
         hs = keep.tile([P, S], U8, name="hs", align_bytes=64)
         y = keep.tile([P, N // P, S], F32, name="y")
         ident = keep.tile([P, P], F32, name="ident")
 
+        ring = keep.tile([P, 2, PACK, FIRST], F32, name="ring")
+
+        nc.vector.memset(w1s[:].bitcast(I32), 0)
+        nc.gpsimd.memset(w3s[:].bitcast(I32), 0)
+        nc.vector.memset(w2s[:].bitcast(I32), 0)
         make_identity(nc, ident[:])
-        for plane in (w1s, w3s, w2s):
-            nc.vector.memset(plane[:].bitcast(I32), 0)
 
         nc.sync.dma_start(offs_sb[:], offs)
-        nc.sync.dma_start(gate_sb[:, :FIRST], gate[:P, :FIRST])
         x_rows = xT.rearrange("(s p t) c -> s t p c", p=P, t=PACK)
         for s in range(PASSES):
             for t in range(PACK):
-                nc.sync.dma_start(planes[s][t][:], x_rows[s, t])
+                nc.sync.dma_start(planes[s][t][:, :T], x_rows[s, t])
+                if (s, t) == (0, 0):
+                    nc.sync.dma_start(gate_sb[:, :HEAD], gate[:P, :HEAD])
+                    nc.sync.dma_start(gate_sb[:, HEAD:FIRST], gate[:P, HEAD:FIRST])
         nc.sync.dma_start(gate_sb[:, FIRST:], gate[:P, FIRST:])
         for plane, scales in ((w1s, w1_scales), (w3s, w3_scales), (w2s, w2_scales)):
             for r in range(4):
@@ -81,86 +89,103 @@ def tile_moe_pre_glu_relu_kernel(
         nc.sync.dma_start(pos1_sb[:], pos1)
         nc.sync.dma_start(pos2_sb[:], pos2)
 
-        rounded = {}
         banks = {}
         relu_a = {}
+        turning = {}
         turned = {}
+        gathered = []
+        results = {}
 
-        def gather(s, lo, hi):
+        def word(s, slot):
+            lo, hi = [g for g in GROUPS if g[0] <= slot < g[1]][0]
+            return PASSES * lo + s * (hi - lo) + slot - lo
+
+        def gather(s, lo, hi, on_vector=False):
             n = hi - lo
-            g4 = stage.tile([P, PACK, n], F32, name="g4")
+            g4 = ring[:, len(gathered) % 2, :, :n]
+            gathered.append((s, lo))
             for t in range(PACK):
-                nc.vector.tensor_tensor(
-                    g4[:, t, :], planes[s][t][:].indirect(offs_sb[:, lo // 16 : hi // 16]), gate_sb[:, lo:hi], MULT
-                )
-            xb = stage.tile([P, n * PACK], BF16, name="xb", align_bytes=64)
-            nc.scalar.copy(xb[:].rearrange("p (c t) -> p c t", t=PACK), g4[:].rearrange("p t c -> p c t"))
-            rounded[s, lo] = xb
+                for a, b in ((0, HEAD), (HEAD, hi)) if (s, t, lo) == (0, 0, 0) else ((lo, hi),):
+                    nc.vector.tensor_tensor(
+                        g4[:, t, a - lo : b - lo],
+                        planes[s][t][:].indirect(offs_sb[:, a // 16 : b // 16]),
+                        gate_sb[:, a:b],
+                        MULT,
+                    )
+            w = word(s, lo)
+            (nc.vector.tensor_copy if on_vector else nc.scalar.copy)(
+                xb[:, w * PACK : (w + n) * PACK].rearrange("p (c t) -> p c t", t=PACK), g4.rearrange("p t c -> p c t")
+            )
 
-        def quantize_x(s, lo, hi):
-            xb = rounded[s, lo]
-            c = lo
-            while c < hi:
-                w = max(q for q in QUANT_WORDS if q <= hi - c)
-                nc.vector.quantize_mx(
-                    out=xq[:, s, c : c + w].bitcast(FP8X4),
-                    scales=xs[:, s, c : c + w],
-                    in_=xb[:, (c - lo) * PACK : (c - lo + w) * PACK],
-                )
-                c += w
+        def quantize_x(s, lo, n):
+            w = word(s, lo)
+            nc.vector.quantize_mx(
+                out=xq[:, w : w + n].bitcast(FP8X4), scales=xs[:, w : w + n], in_=xb[:, w * PACK : (w + n) * PACK]
+            )
 
-        def first_layer(j, passes):
+        def first_layer(j, passes, in_ring=False):
             e = j * P // C
-            cols = slice(j * P, (j + 1) * P)
             if j not in banks:
                 banks[j] = (
-                    psum.tile([P, H], F32, name="acc_a", bufs=2),
-                    psum.tile([P, H], F32, name="acc_b", bufs=4),
+                    psum.tile([P, H], F32, name="bank"),
+                    psum.tile([P, H], F32, name="bank"),
                 )
             for s in passes:
+                cols = slice(word(s, j * P), word(s, j * P) + P)
                 for acc, codes, plane in zip(banks[j], (w1c, w3c), (w1s, w3s)):
                     nc.tensor.matmul_mx(
                         out=acc[:],
-                        lhsT=xq[:, s, cols].bitcast(FP8X4),
-                        lhsT_scale=xs[:, s, cols],
+                        lhsT=xq[:, cols].bitcast(FP8X4),
+                        lhsT_scale=xs[:, cols],
                         rhs=codes[:, e, s, :].bitcast(FP4X4),
                         rhs_scale=plane[:, e * PASSES + s, :],
                         start=(s == 0),
                         stop=(s == PASSES - 1),
                     )
             if passes[-1] == PASSES - 1:
-                r = stage.tile([P, H], F32, name="r", bufs=4)
+                if in_ring:
+                    r = ring[:, (len(gathered) - 1) % 2, 1, :]
+                else:
+                    r = stage.tile([P, H], F32, name="r", bufs=4)[:]
                 nc.scalar.activation(
-                    r[:].rearrange("j (u p d) -> j u p d", u=2, d=2),
+                    r.rearrange("j (u p d) -> j u p d", u=2, d=2),
                     banks[j][0][:].rearrange("j (p u d) -> j u p d", u=2, d=2),
                     RELU,
                 )
                 relu_a[j] = r
 
-        def hidden(j):
-            hb = stage.tile([P, H], BF16, name="hb")
+        def hidden(j, unit, words=None, on_vector=False):
+            if words is None:
+                words = stage.tile([P, H // 2], F32, name="hb")[:]
+            hb = words.bitcast(BF16)
             nc.vector.tensor_tensor(
-                hb[:].rearrange("j (u p d) -> j u p d", u=2, d=2),
+                hb.rearrange("j (u p d) -> j u p d", u=2, d=2),
                 banks[j][1][:].rearrange("j (p u d) -> j u p d", u=2, d=2),
-                relu_a[j][:].rearrange("j (u p d) -> j u p d", u=2, d=2),
+                relu_a[j].rearrange("j (u p d) -> j u p d", u=2, d=2),
                 MULT,
             )
-            words = hb[:].bitcast(F32)
-            ht = psum.tile([P, 2, P], F32, name="ht")
+            if unit not in turning:
+                turning[unit] = psum.tile([P, 2, len(unit) * P], F32, name="bank")
+            ht = turning[unit]
+            at = (j - unit[0]) * P
             for u in range(2):
-                nc.tensor.transpose(ht[:, u, :], words[:, u * P : (u + 1) * P], ident[:])
-            hi4 = stage.tile([P, P * PACK], BF16, name="hi4", align_bytes=64)
-            nc.scalar.copy(hi4[:].bitcast(F32).rearrange("p (j u) -> p j u", u=2), ht[:].rearrange("p u j -> p j u"))
-            turned[j] = hi4
+                nc.tensor.transpose(ht[:, u, at : at + P], words[:, u * P : (u + 1) * P], ident[:])
+            if j == unit[-1]:
+                hi4 = stage.tile([P, len(unit) * P * PACK], BF16, name="hi4", align_bytes=64, bufs=4)
+                (nc.vector.tensor_copy if on_vector else nc.scalar.copy)(
+                    hi4[:].bitcast(F32).rearrange("p (j u) -> p j u", u=2), ht[:].rearrange("p u j -> p j u")
+                )
+                turned[unit] = hi4
 
-        def second_layer(j):
-            e = j * P // C
-            cols = slice(j * P, (j + 1) * P)
-            nc.vector.quantize_mx(out=hq[:, cols].bitcast(FP8X4), scales=hs[:, cols], in_=turned[j][:])
-            acc_y = psum.tile([P, N // P, P], F32, name="acc_y")
+        def second_layer(unit, split=False):
+            e = unit[0] * P // C
+            cols = slice(unit[0] * P, (unit[-1] + 1) * P)
+            nc.vector.quantize_mx(out=hq[:, cols].bitcast(FP8X4), scales=hs[:, cols], in_=turned[unit][:])
+            acc_y = [psum.tile([P, N // P, len(unit) * P], F32, name="bank")]
+            acc_y.append(psum.tile([P, N // P, len(unit) * P], F32, name="bank") if split else acc_y[0])
             for m in range(N // P):
                 nc.tensor.matmul_mx(
-                    out=acc_y[:, m, :],
+                    out=acc_y[m][:, m, :],
                     lhsT=w2c[:, e, 2 * m * P : 2 * (m + 1) * P].bitcast(FP4X4),
                     lhsT_scale=w2s[:, e, m * P : (m + 1) * P],
                     rhs=hq[:, cols].bitcast(FP8X4),
@@ -168,56 +193,76 @@ def tile_moe_pre_glu_relu_kernel(
                     start=True,
                     stop=True,
                 )
-            nc.scalar.copy(y[:, :, cols], acc_y[:])
+            results[unit] = acc_y
 
-        all_passes = list(range(PASSES))
-        A, B = (0, 384), (384, 768)
+        def keep_y(unit, how="s"):
+            cols = slice(unit[0] * P, (unit[-1] + 1) * P)
+            copies = {"s": nc.scalar.copy, "v": nc.vector.tensor_copy}
+            if len(how) == 1:
+                copies[how](y[:, :, cols], results[unit][0][:])
+            else:
+                for m in range(N // P):
+                    copies[how[m]](y[:, m, cols], results[unit][m][:, m, :])
+
+        A, B, Z = GROUPS
         gather(0, *A)
         gather(1, *A)
-        quantize_x(0, *A)
+        quantize_x(0, 0, 512)
         gather(2, *A)
-        quantize_x(1, *A)
+        quantize_x(1, 0, 512)
+        first_layer(0, [0, 1])
+        first_layer(1, [0, 1])
+        first_layer(2, [0, 1])
         gather(0, *B)
-        quantize_x(2, *A)
-        for j in (0, 1, 2):
-            first_layer(j, all_passes)
+        quantize_x(2, 0, 512)
+        first_layer(0, [2])
+        first_layer(1, [2], in_ring=True)
+        first_layer(2, [2])
         gather(1, *B)
-        quantize_x(0, *B)
+        first_layer(3, [0, 1, 2], in_ring=True)
+        hidden(0, (0, 1))
+        hidden(1, (0, 1))
         gather(2, *B)
-        quantize_x(1, *B)
-        hidden(0)
-        hidden(1)
-        gather(0, 768, 1024)
-        quantize_x(2, *B)
-        for j in (3, 4, 5):
-            first_layer(j, all_passes)
-        hidden(2)
-        second_layer(0)
-        second_layer(1)
-        gather(1, 768, 1024)
-        quantize_x(0, 768, 1024)
-        hidden(3)
-        second_layer(2)
+        quantize_x(0, 512, 512)
+        hidden(2, (2, 3))
+        hidden(3, (2, 3))
+        first_layer(4, [0, 1])
+        first_layer(5, [0, 1])
+        second_layer((0, 1))
+        second_layer((2, 3))
+        gather(0, *Z)
+        quantize_x(2, 512, 256)
+        first_layer(4, [2])
+        first_layer(5, [2])
+        gather(1, *Z)
+        quantize_x(0, 768, 256)
+        first_layer(6, [0])
+        first_layer(7, [0])
+        keep_y((0, 1))
+        quantize_x(1, 768, 256)
         gather(2, 768, 896)
-        quantize_x(1, 768, 1024)
-        first_layer(6, [0, 1])
-        first_layer(7, [0, 1])
-        gather(2, 896, 1024)
-        quantize_x(2, 768, 896)
+        first_layer(6, [1])
+        keep_y((2, 3))
+        first_layer(7, [1])
+        quantize_x(2, 768, 128)
         first_layer(6, [2])
-        second_layer(3)
-        hidden(4)
-        quantize_x(2, 896, 1024)
+        gather(2, 896, 1024, on_vector=True)
+        quantize_x(2, 896, 128)
         first_layer(7, [2])
-        hidden(5)
-        hidden(6)
-        second_layer(4)
-        hidden(7)
-        second_layer(5)
-        second_layer(6)
-        second_layer(7)
+        hidden(4, (4,), xb[:, PASSES * S * PACK - 768 : PASSES * S * PACK - 256].bitcast(F32))
+        hidden(5, (5,), ring[:, 1, 0, :256])
+        hidden(6, (6,), on_vector=False)
+        hidden(7, (7,), on_vector=True)
+        second_layer((7,), split=True)
+        keep_y((7,), "vs")
+        second_layer((6,), split=True)
+        keep_y((6,), "ss")
+        second_layer((4,), split=True)
+        keep_y((4,), "vs")
+        second_layer((5,), split=False)
+        keep_y((5,), "s")
 
-        pieces = ((0, 0, T), (1, 0, T // 2), (1, T // 2, T))
+        pieces = ((0, 0, T), (1, 0, 384), (1, 384, T))
         pending = None
         for m, lo, hi in pieces:
             got = []
@@ -231,7 +276,7 @@ def tile_moe_pre_glu_relu_kernel(
 
             def finish(m=m, lo=lo, hi=hi, got=got):
                 res = stage.tile([P, hi - lo], F32, name="res")
-                nc.vector.tensor_tensor(res[:], got[0][:], got[1][:], ADD)
+                (nc.vector if (m, hi) == (1, T) else nc.gpsimd).tensor_tensor(res[:], got[0][:], got[1][:], ADD)
                 nc.sync.dma_start(out[m * P : (m + 1) * P, lo:hi], res[:])
 
             pending = finish

@@ -62,16 +62,16 @@ def tile_moe_pre_glu_relu_kernel(
         ring = keep.tile([P, 2, PACK, FIRST], F32, name="ring")
 
         nc.vector.memset(w1s[:].bitcast(I32), 0)
-        nc.gpsimd.memset(w3s[:].bitcast(I32), 0)
+        nc.vector.memset(w3s[:].bitcast(I32), 0)
         nc.vector.memset(w2s[:].bitcast(I32), 0)
         make_identity(nc, ident[:])
 
-        nc.sync.dma_start(offs_sb[:], offs)
         x_rows = xT.rearrange("(s p t) c -> s t p c", p=P, t=PACK)
         for s in range(PASSES):
             for t in range(PACK):
                 nc.sync.dma_start(planes[s][t][:, :T], x_rows[s, t])
                 if (s, t) == (0, 0):
+                    nc.sync.dma_start(offs_sb[:], offs)
                     nc.sync.dma_start(gate_sb[:, :HEAD], gate[:P, :HEAD])
                     nc.sync.dma_start(gate_sb[:, HEAD:FIRST], gate[:P, HEAD:FIRST])
         nc.sync.dma_start(gate_sb[:, FIRST:], gate[:P, FIRST:])
@@ -100,9 +100,12 @@ def tile_moe_pre_glu_relu_kernel(
             lo, hi = [g for g in GROUPS if g[0] <= slot < g[1]][0]
             return PASSES * lo + s * (hi - lo) + slot - lo
 
-        def gather(s, lo, hi, on_vector=False):
+        def gather(s, lo, hi, on_vector=False, late=None):
             n = hi - lo
             g4 = ring[:, len(gathered) % 2, :, :n]
+            if late is not None:
+                end = word(s, lo - n) * PACK + late * 2 * n
+                g4 = xb[:, end - 2 * PACK * n : end].bitcast(F32).rearrange("p (t c) -> p t c", t=PACK)
             gathered.append((s, lo))
             for t in range(PACK):
                 for a, b in ((0, HEAD), (HEAD, hi)) if (s, t, lo) == (0, 0, 0) else ((lo, hi),):
@@ -114,7 +117,8 @@ def tile_moe_pre_glu_relu_kernel(
                     )
             w = word(s, lo)
             (nc.vector.tensor_copy if on_vector else nc.scalar.copy)(
-                xb[:, w * PACK : (w + n) * PACK].rearrange("p (c t) -> p c t", t=PACK), g4.rearrange("p t c -> p c t")
+                xb[:, w * PACK : (w + n) * PACK].rearrange("p (c i t) -> p c t i", i=4, t=PACK),
+                g4.rearrange("p t (c i) -> p c t i", i=4),
             )
 
         def quantize_x(s, lo, n):
@@ -213,54 +217,54 @@ def tile_moe_pre_glu_relu_kernel(
         first_layer(0, [0, 1])
         first_layer(1, [0, 1])
         first_layer(2, [0, 1])
-        gather(0, *B)
         quantize_x(2, 0, 512)
-        first_layer(0, [2])
+        gather(0, *B)
         first_layer(1, [2], in_ring=True)
-        first_layer(2, [2])
+        first_layer(0, [2])
         gather(1, *B)
-        first_layer(3, [0, 1, 2], in_ring=True)
-        hidden(0, (0, 1))
-        hidden(1, (0, 1))
-        gather(2, *B)
         quantize_x(0, 512, 512)
-        hidden(2, (2, 3))
-        hidden(3, (2, 3))
-        first_layer(4, [0, 1])
+        first_layer(2, [2])
+        hidden(0, (0, 1))
+        first_layer(3, [0, 1, 2], in_ring=True)
+        hidden(1, (0, 1))
         first_layer(5, [0, 1])
-        second_layer((0, 1))
-        second_layer((2, 3))
+        hidden(2, (2, 3))
+        gather(2, *B)
+        hidden(3, (2, 3))
         gather(0, *Z)
         quantize_x(2, 512, 256)
-        first_layer(4, [2])
-        first_layer(5, [2])
-        gather(1, *Z)
+        first_layer(4, [0, 1])
+        second_layer((0, 1))
         quantize_x(0, 768, 256)
-        first_layer(6, [0])
-        first_layer(7, [0])
         keep_y((0, 1))
+        first_layer(6, [0])
+        first_layer(4, [2])
+        gather(1, *Z)
+        second_layer((2, 3))
+        first_layer(5, [2])
         quantize_x(1, 768, 256)
+        first_layer(7, [0])
         gather(2, 768, 896)
-        first_layer(6, [1])
-        keep_y((2, 3))
-        first_layer(7, [1])
         quantize_x(2, 768, 128)
-        first_layer(6, [2])
-        gather(2, 896, 1024, on_vector=True)
+        first_layer(6, [1])
+        first_layer(7, [1])
+        gather(2, 896, 1024, on_vector=True, late=1)
+        keep_y((2, 3))
         quantize_x(2, 896, 128)
+        hidden(4, (4,), xb[:, PASSES * S * PACK - 768 : PASSES * S * PACK - 256].bitcast(F32), on_vector=False)
+        first_layer(6, [2])
+        hidden(5, (5,), xb[:, PASSES * S * PACK - 256 :].bitcast(F32), on_vector=False)
+        hidden(6, (6,), on_vector=True)
         first_layer(7, [2])
-        hidden(4, (4,), xb[:, PASSES * S * PACK - 768 : PASSES * S * PACK - 256].bitcast(F32))
-        hidden(5, (5,), ring[:, 1, 0, :256])
-        hidden(6, (6,), on_vector=False)
         hidden(7, (7,), on_vector=True)
-        second_layer((7,), split=True)
-        keep_y((7,), "vs")
+        second_layer((4,), split=False)
         second_layer((6,), split=True)
-        keep_y((6,), "ss")
-        second_layer((4,), split=True)
-        keep_y((4,), "vs")
-        second_layer((5,), split=False)
-        keep_y((5,), "s")
+        second_layer((7,), split=True)
+        second_layer((5,), split=True)
+        keep_y((6,), "sv")
+        keep_y((4,), "s")
+        keep_y((5,), "sv")
+        keep_y((7,), "vs")
 
         pieces = ((0, 0, T), (1, 0, 384), (1, 384, T))
         pending = None
@@ -276,7 +280,7 @@ def tile_moe_pre_glu_relu_kernel(
 
             def finish(m=m, lo=lo, hi=hi, got=got):
                 res = stage.tile([P, hi - lo], F32, name="res")
-                (nc.vector if (m, hi) == (1, T) else nc.gpsimd).tensor_tensor(res[:], got[0][:], got[1][:], ADD)
+                nc.vector.tensor_tensor(res[:], got[0][:], got[1][:], ADD)
                 nc.sync.dma_start(out[m * P : (m + 1) * P, lo:hi], res[:])
 
             pending = finish

@@ -67,25 +67,42 @@ def tile_moe_pre_glu_relu_kernel(
         make_identity(nc, ident[:])
 
         x_rows = xT.rearrange("(s p t) c -> s t p c", p=P, t=PACK)
-        for s in range(PASSES):
-            for t in range(PACK):
+
+        def load_x(s, ts):
+            for t in ts:
                 nc.sync.dma_start(planes[s][t][:, :T], x_rows[s, t])
-                if (s, t) == (0, 0):
-                    nc.sync.dma_start(offs_sb[:], offs)
-                    nc.sync.dma_start(gate_sb[:, :HEAD], gate[:P, :HEAD])
-                    nc.sync.dma_start(gate_sb[:, HEAD:FIRST], gate[:P, HEAD:FIRST])
-        nc.sync.dma_start(gate_sb[:, FIRST:], gate[:P, FIRST:])
-        for plane, scales in ((w1s, w1_scales), (w3s, w3_scales), (w2s, w2_scales)):
+
+        def load_gate(lo, hi):
+            nc.sync.dma_start(gate_sb[:, lo:hi], gate[:P, lo:hi])
+
+        def load_scales(plane, scales, e0, e1):
+            per = scales.shape[1]
             for r in range(4):
                 nc.sync.dma_start(
-                    plane[r:P:32].bitcast(I32),
-                    scales.rearrange("e s (q r) n -> r q (e s) n", r=4)[r].bitcast(I32),
+                    plane[r:P:32, e0 * per : e1 * per].bitcast(I32),
+                    scales[e0:e1].rearrange("e s (q r) n -> r q (e s) n", r=4)[r].bitcast(I32),
                 )
-        for e in range(E):
+
+        def load_words(e):
             for codes, words in ((w1c, w1_words), (w3c, w3_words)):
                 nc.sync.dma_start(codes[:, e].bitcast(I32), words[e].rearrange("s p b -> p s b").bitcast(I32))
-            if e == 0:
-                nc.sync.dma_start(w2c[:].bitcast(I32), w2_words.rearrange("e s p b -> p (e s) b").bitcast(I32))
+
+        load_x(0, [0])
+        nc.sync.dma_start(offs_sb[:], offs)
+        load_gate(0, HEAD)
+        load_gate(HEAD, FIRST)
+        load_x(0, [1, 2, 3])
+        load_x(1, [0, 1, 2, 3])
+        load_x(2, [0, 1, 2, 3])
+        load_gate(FIRST, S)
+        load_scales(w1s, w1_scales, 0, E)
+        load_scales(w3s, w3_scales, 0, E)
+        load_scales(w2s, w2_scales, 0, E)
+        load_words(0)
+        load_words(1)
+        nc.sync.dma_start(w2c[:].bitcast(I32), w2_words.rearrange("e s p b -> p (e s) b").bitcast(I32))
+        load_words(2)
+        load_words(3)
         nc.sync.dma_start(pos1_sb[:], pos1)
         nc.sync.dma_start(pos2_sb[:], pos2)
 
@@ -93,20 +110,18 @@ def tile_moe_pre_glu_relu_kernel(
         relu_a = {}
         turning = {}
         turned = {}
-        gathered = []
         results = {}
 
         def word(s, slot):
             lo, hi = [g for g in GROUPS if g[0] <= slot < g[1]][0]
             return PASSES * lo + s * (hi - lo) + slot - lo
 
-        def gather(s, lo, hi, on_vector=False, late=None):
+        def gather(s, lo, hi, slot, at=0, on_vector=False, late=None):
             n = hi - lo
-            g4 = ring[:, len(gathered) % 2, :, :n]
+            g4 = ring[:, slot, :, at : at + n]
             if late is not None:
                 end = word(s, lo - n) * PACK + late * 2 * n
                 g4 = xb[:, end - 2 * PACK * n : end].bitcast(F32).rearrange("p (t c) -> p t c", t=PACK)
-            gathered.append((s, lo))
             for t in range(PACK):
                 for a, b in ((0, HEAD), (HEAD, hi)) if (s, t, lo) == (0, 0, 0) else ((lo, hi),):
                     nc.vector.tensor_tensor(
@@ -127,7 +142,7 @@ def tile_moe_pre_glu_relu_kernel(
                 out=xq[:, w : w + n].bitcast(FP8X4), scales=xs[:, w : w + n], in_=xb[:, w * PACK : (w + n) * PACK]
             )
 
-        def first_layer(j, passes, in_ring=False):
+        def first_layer(j, passes, in_ring=None):
             e = j * P // C
             if j not in banks:
                 banks[j] = (
@@ -147,12 +162,12 @@ def tile_moe_pre_glu_relu_kernel(
                         stop=(s == PASSES - 1),
                     )
             if passes[-1] == PASSES - 1:
-                if in_ring:
-                    r = ring[:, (len(gathered) - 1) % 2, 1, :]
+                if in_ring is not None:
+                    r = in_ring.rearrange("j (u c) -> j u c", u=2)
                 else:
-                    r = stage.tile([P, H], F32, name="r", bufs=4)[:]
+                    r = stage.tile([P, 2, H // 2], F32, name="r", bufs=4)[:]
                 nc.scalar.activation(
-                    r.rearrange("j (u p d) -> j u p d", u=2, d=2),
+                    r.rearrange("j u (p d) -> j u p d", d=2),
                     banks[j][0][:].rearrange("j (p u d) -> j u p d", u=2, d=2),
                     RELU,
                 )
@@ -165,7 +180,7 @@ def tile_moe_pre_glu_relu_kernel(
             nc.vector.tensor_tensor(
                 hb.rearrange("j (u p d) -> j u p d", u=2, d=2),
                 banks[j][1][:].rearrange("j (p u d) -> j u p d", u=2, d=2),
-                relu_a[j].rearrange("j (u p d) -> j u p d", u=2, d=2),
+                relu_a[j].rearrange("j u (p d) -> j u p d", d=2),
                 MULT,
             )
             if unit not in turning:
@@ -209,46 +224,51 @@ def tile_moe_pre_glu_relu_kernel(
                     copies[how[m]](y[:, m, cols], results[unit][m][:, m, :])
 
         A, B, Z = GROUPS
-        gather(0, *A)
-        gather(1, *A)
+        gather(0, *A, 0)
+        gather(1, *A, 1)
         quantize_x(0, 0, 512)
-        gather(2, *A)
+        first_layer(0, [0])
+        first_layer(1, [0])
+        first_layer(2, [0])
+        first_layer(3, [0])
+        gather(2, *A, 0)
         quantize_x(1, 0, 512)
-        first_layer(0, [0, 1])
-        first_layer(1, [0, 1])
-        first_layer(2, [0, 1])
+        first_layer(0, [1])
+        first_layer(1, [1])
+        first_layer(2, [1])
+        first_layer(3, [1])
+        gather(0, *B, 1)
         quantize_x(2, 0, 512)
-        gather(0, *B)
-        first_layer(1, [2], in_ring=True)
         first_layer(0, [2])
-        gather(1, *B)
+        first_layer(1, [2])
+        first_layer(3, [2], in_ring=ring[:, 1, 2, :])
+        gather(1, *B, 0)
+        first_layer(2, [2], in_ring=ring[:, 0, 3, :])
         quantize_x(0, 512, 512)
-        first_layer(2, [2])
         hidden(0, (0, 1))
-        first_layer(3, [0, 1, 2], in_ring=True)
         hidden(1, (0, 1))
-        first_layer(5, [0, 1])
         hidden(2, (2, 3))
-        gather(2, *B)
         hidden(3, (2, 3))
-        gather(0, *Z)
+        gather(2, *B, 1)
+        first_layer(5, [0, 1])
+        gather(0, *Z, 0)
         quantize_x(2, 512, 256)
         first_layer(4, [0, 1])
         second_layer((0, 1))
         quantize_x(0, 768, 256)
         keep_y((0, 1))
         first_layer(6, [0])
-        first_layer(4, [2])
-        gather(1, *Z)
+        gather(1, *Z, 1)
+        first_layer(4, [2], in_ring=ring[:, 1, 1, :])
         second_layer((2, 3))
-        first_layer(5, [2])
         quantize_x(1, 768, 256)
         first_layer(7, [0])
-        gather(2, 768, 896)
+        gather(2, 768, 896, 0)
+        first_layer(5, [2], in_ring=ring[:, 0, 1, :])
         quantize_x(2, 768, 128)
         first_layer(6, [1])
         first_layer(7, [1])
-        gather(2, 896, 1024, on_vector=True, late=1)
+        gather(2, 896, 1024, 0, on_vector=True, late=1)
         keep_y((2, 3))
         quantize_x(2, 896, 128)
         hidden(4, (4,), xb[:, PASSES * S * PACK - 768 : PASSES * S * PACK - 256].bitcast(F32), on_vector=False)
@@ -258,12 +278,12 @@ def tile_moe_pre_glu_relu_kernel(
         first_layer(7, [2])
         hidden(7, (7,), on_vector=True)
         second_layer((4,), split=False)
+        second_layer((5,), split=False)
         second_layer((6,), split=True)
         second_layer((7,), split=True)
-        second_layer((5,), split=True)
-        keep_y((6,), "sv")
-        keep_y((4,), "s")
-        keep_y((5,), "sv")
+        keep_y((4,), "ss")
+        keep_y((5,), "ss")
+        keep_y((6,), "vs")
         keep_y((7,), "vs")
 
         pieces = ((0, 0, T), (1, 0, 384), (1, 384, T))

@@ -250,39 +250,39 @@ def tile_moe_pre_glu_relu_kernel(
         hidden(2, (2, 3))
         hidden(3, (2, 3))
         gather(2, *B, 1)
-        first_layer(5, [0, 1])
+        second_layer((0, 1))
         gather(0, *Z, 0)
         quantize_x(2, 512, 256)
-        first_layer(4, [0, 1])
-        second_layer((0, 1))
-        quantize_x(0, 768, 256)
+        first_layer(5, [0, 1])
         keep_y((0, 1))
-        first_layer(6, [0])
         gather(1, *Z, 1)
+        first_layer(4, [0, 1])
+        quantize_x(0, 768, 256)
         first_layer(4, [2], in_ring=ring[:, 1, 1, :])
         second_layer((2, 3))
-        quantize_x(1, 768, 256)
-        first_layer(7, [0])
         gather(2, 768, 896, 0)
+        quantize_x(1, 768, 256)
+        first_layer(6, [0])
         first_layer(5, [2], in_ring=ring[:, 0, 1, :])
         quantize_x(2, 768, 128)
-        first_layer(6, [1])
-        first_layer(7, [1])
         gather(2, 896, 1024, 0, on_vector=True, late=1)
+        first_layer(7, [0])
+        first_layer(7, [1])
+        first_layer(6, [1])
+        first_layer(6, [2])
         keep_y((2, 3))
         quantize_x(2, 896, 128)
-        hidden(4, (4,), xb[:, PASSES * S * PACK - 768 : PASSES * S * PACK - 256].bitcast(F32), on_vector=False)
-        first_layer(6, [2])
-        hidden(5, (5,), xb[:, PASSES * S * PACK - 256 :].bitcast(F32), on_vector=False)
-        hidden(6, (6,), on_vector=True)
         first_layer(7, [2])
+        hidden(5, (5,), gate_sb[:, 640:896], on_vector=False)
+        hidden(4, (4,), xb[:, PASSES * S * PACK - 768 : PASSES * S * PACK - 256].bitcast(F32), on_vector=False)
+        hidden(6, (6,), on_vector=False)
         hidden(7, (7,), on_vector=True)
-        second_layer((4,), split=False)
         second_layer((5,), split=False)
+        second_layer((4,), split=True)
         second_layer((6,), split=True)
+        keep_y((5,), "s")
+        keep_y((4,), "sv")
         second_layer((7,), split=True)
-        keep_y((4,), "ss")
-        keep_y((5,), "ss")
         keep_y((6,), "vs")
         keep_y((7,), "vs")
 

@@ -8,7 +8,6 @@ S = E * C
 P = 128
 PACK = 4
 PASSES = K // (P * PACK)
-TILES = S // P
 
 FLOPS = 2 * S * (2 * K * H + H * N)
 BYTES = 4 * K * T + E * (2 * K * H + H * N) // 2 + E * (2 * K * H + H * N) // 32 + 4 * P * S + 2 * P * (S + 2 * T) // 16 + 4 * N * T
@@ -26,9 +25,10 @@ ADD = mybir.AluOpType.add
 RELU = mybir.ActivationFunctionType.Relu
 
 GROUPS = ((0, 512), (512, 768), (768, 1024))
-FIRST = GROUPS[0][1]
 PAD = 32
 HEAD = 128
+ARENA = 18176
+AB = ((0, 1), (2, 3), (4, 5), (6, 7), (0, 2), (4, 6), (1, 3), (5, 7))
 
 
 def tile_moe_pre_glu_relu_kernel(
@@ -37,13 +37,12 @@ def tile_moe_pre_glu_relu_kernel(
     nc = tc.nc
     with ExitStack() as ctx:
         keep = ctx.enter_context(tc.tile_pool(name="keep", bufs=1))
-        stage = ctx.enter_context(tc.tile_pool(name="stage", bufs=3))
-        psum = ctx.enter_context(tc.psum_pool(name="psum", bufs=8))
+        psum = ctx.enter_context(tc.psum_pool(name="psum", bufs=1))
 
         offs_sb = keep.tile([P, S // 16], U16, name="offs_sb")
         pos1_sb = keep.tile([P, T // 16], U16, name="pos1_sb")
         pos2_sb = keep.tile([P, T // 16], U16, name="pos2_sb")
-        gate_sb = keep.tile([P, S], F32, name="gate_sb")
+        gate_sb = keep.tile([P, S + 256], F32, name="gate_sb", align_bytes=64)
         planes = [[keep.tile([P, T + PAD], F32, name=f"x{s}{t}") for t in range(PACK)] for s in range(PASSES)]
         w1c = keep.tile([P, E, PASSES, 2 * H], U8, name="w1c", align_bytes=64)
         w3c = keep.tile([P, E, PASSES, 2 * H], U8, name="w3c", align_bytes=64)
@@ -51,20 +50,19 @@ def tile_moe_pre_glu_relu_kernel(
         w1s = keep.tile([P, E * PASSES, H], U8, name="w1s", align_bytes=64)
         w3s = keep.tile([P, E * PASSES, H], U8, name="w3s", align_bytes=64)
         w2s = keep.tile([P, E, N], U8, name="w2s", align_bytes=64)
-        xb = keep.tile([P, PASSES * S * PACK + H // 2], BF16, name="xb", align_bytes=64)
         xq = keep.tile([P, PASSES * S], U32, name="xq", align_bytes=64)
         xs = keep.tile([P, PASSES * S], U8, name="xs", align_bytes=64)
         hq = keep.tile([P, S], U32, name="hq", align_bytes=64)
         hs = keep.tile([P, S], U8, name="hs", align_bytes=64)
-        y = keep.tile([P, N // P, S], F32, name="y")
+        y = [keep.tile([P, S], F32, name=f"y{m}") for m in range(N // P)]
         ident = keep.tile([P, P], F32, name="ident")
-
-        ring = keep.tile([P, 2, PACK, FIRST], F32, name="ring")
+        arena = keep.tile([P, ARENA], F32, name="arena", align_bytes=64)
+        bank = [psum.tile([P, H], F32, name=f"bank{b}") for b in range(8)]
 
         nc.vector.memset(w1s[:].bitcast(I32), 0)
-        nc.vector.memset(w3s[:].bitcast(I32), 0)
-        nc.vector.memset(w2s[:].bitcast(I32), 0)
         make_identity(nc, ident[:])
+        nc.gpsimd.memset(w3s[:].bitcast(I32), 0)
+        nc.gpsimd.memset(w2s[:].bitcast(I32), 0)
 
         x_rows = xT.rearrange("(s p t) c -> s t p c", p=P, t=PACK)
 
@@ -75,12 +73,11 @@ def tile_moe_pre_glu_relu_kernel(
         def load_gate(lo, hi):
             nc.sync.dma_start(gate_sb[:, lo:hi], gate[:P, lo:hi])
 
-        def load_scales(plane, scales, e0, e1):
-            per = scales.shape[1]
+        def load_scales(plane, scales):
             for r in range(4):
                 nc.sync.dma_start(
-                    plane[r:P:32, e0 * per : e1 * per].bitcast(I32),
-                    scales[e0:e1].rearrange("e s (q r) n -> r q (e s) n", r=4)[r].bitcast(I32),
+                    plane[r:P:32].bitcast(I32),
+                    scales.rearrange("e s (q r) n -> r q (e s) n", r=4)[r].bitcast(I32),
                 )
 
         def load_words(e):
@@ -90,14 +87,14 @@ def tile_moe_pre_glu_relu_kernel(
         load_x(0, [0])
         nc.sync.dma_start(offs_sb[:], offs)
         load_gate(0, HEAD)
-        load_gate(HEAD, FIRST)
+        load_gate(HEAD, 512)
         load_x(0, [1, 2, 3])
         load_x(1, [0, 1, 2, 3])
         load_x(2, [0, 1, 2, 3])
-        load_gate(FIRST, S)
-        load_scales(w1s, w1_scales, 0, E)
-        load_scales(w3s, w3_scales, 0, E)
-        load_scales(w2s, w2_scales, 0, E)
+        load_gate(512, S)
+        load_scales(w1s, w1_scales)
+        load_scales(w3s, w3_scales)
+        load_scales(w2s, w2_scales)
         load_words(0)
         load_words(1)
         nc.sync.dma_start(w2c[:].bitcast(I32), w2_words.rearrange("e s p b -> p (e s) b").bitcast(I32))
@@ -106,202 +103,214 @@ def tile_moe_pre_glu_relu_kernel(
         nc.sync.dma_start(pos1_sb[:], pos1)
         nc.sync.dma_start(pos2_sb[:], pos2)
 
-        banks = {}
-        relu_a = {}
-        turning = {}
-        turned = {}
-        results = {}
-
         def word(s, slot):
             lo, hi = [g for g in GROUPS if g[0] <= slot < g[1]][0]
             return PASSES * lo + s * (hi - lo) + slot - lo
 
-        def gather(s, lo, hi, slot, at=0, on_vector=False, late=None):
-            n = hi - lo
-            g4 = ring[:, slot, :, at : at + n]
-            if late is not None:
-                end = word(s, lo - n) * PACK + late * 2 * n
-                g4 = xb[:, end - 2 * PACK * n : end].bitcast(F32).rearrange("p (t c) -> p t c", t=PACK)
-            for t in range(PACK):
+        def room(at, words):
+            return arena[:, at : at + words]
+
+        def halves(at, step=256):
+            return room(at, 2 * step).rearrange("p (u c) -> p u c", u=2)[:, :, :256]
+
+        def gather(s, lo, hi, place, ts):
+            base, stride = place
+            for t in ts:
                 for a, b in ((0, HEAD), (HEAD, hi)) if (s, t, lo) == (0, 0, 0) else ((lo, hi),):
                     nc.vector.tensor_tensor(
-                        g4[:, t, a - lo : b - lo],
+                        room(base + t * stride + a - lo, b - a),
                         planes[s][t][:].indirect(offs_sb[:, a // 16 : b // 16]),
                         gate_sb[:, a:b],
                         MULT,
                     )
-            w = word(s, lo)
-            (nc.vector.tensor_copy if on_vector else nc.scalar.copy)(
-                xb[:, w * PACK : (w + n) * PACK].rearrange("p (c i t) -> p c t i", i=4, t=PACK),
+
+        def weave(n, place, at, lo=0):
+            base, stride = place
+            g4 = room(base, PACK * stride).rearrange("p (t c) -> p t c", t=PACK)[:, :, lo : lo + n]
+            nc.scalar.copy(
+                room(at, 2 * n).bitcast(BF16).rearrange("p (c i t) -> p c t i", i=4, t=PACK),
                 g4.rearrange("p t (c i) -> p c t i", i=4),
             )
 
-        def quantize_x(s, lo, n):
+        def quantize_x(s, lo, n, at):
             w = word(s, lo)
-            nc.vector.quantize_mx(
-                out=xq[:, w : w + n].bitcast(FP8X4), scales=xs[:, w : w + n], in_=xb[:, w * PACK : (w + n) * PACK]
+            nc.vector.quantize_mx(out=xq[:, w : w + n].bitcast(FP8X4), scales=xs[:, w : w + n], in_=room(at, 2 * n).bitcast(BF16))
+
+        def first_layer(j, s, which):
+            e = j * P // C
+            cols = slice(word(s, j * P), word(s, j * P) + P)
+            codes, plane = ((w1c, w1s), (w3c, w3s))[which]
+            nc.tensor.matmul_mx(
+                out=bank[AB[j][which]][:],
+                lhsT=xq[:, cols].bitcast(FP8X4),
+                lhsT_scale=xs[:, cols],
+                rhs=codes[:, e, s, :].bitcast(FP4X4),
+                rhs_scale=plane[:, e * PASSES + s, :],
+                start=(s == 0),
+                stop=(s == PASSES - 1),
             )
 
-        def first_layer(j, passes, in_ring=None):
-            e = j * P // C
-            if j not in banks:
-                banks[j] = (
-                    psum.tile([P, H], F32, name="bank"),
-                    psum.tile([P, H], F32, name="bank"),
-                )
-            for s in passes:
-                cols = slice(word(s, j * P), word(s, j * P) + P)
-                for acc, codes, plane in zip(banks[j], (w1c, w3c), (w1s, w3s)):
-                    nc.tensor.matmul_mx(
-                        out=acc[:],
-                        lhsT=xq[:, cols].bitcast(FP8X4),
-                        lhsT_scale=xs[:, cols],
-                        rhs=codes[:, e, s, :].bitcast(FP4X4),
-                        rhs_scale=plane[:, e * PASSES + s, :],
-                        start=(s == 0),
-                        stop=(s == PASSES - 1),
-                    )
-            if passes[-1] == PASSES - 1:
-                if in_ring is not None:
-                    r = in_ring.rearrange("j (u c) -> j u c", u=2)
-                else:
-                    r = stage.tile([P, 2, H // 2], F32, name="r", bufs=4)[:]
-                nc.scalar.activation(
-                    r.rearrange("j u (p d) -> j u p d", d=2),
-                    banks[j][0][:].rearrange("j (p u d) -> j u p d", u=2, d=2),
-                    RELU,
-                )
-                relu_a[j] = r
+        def both(js, ss):
+            for s in ss:
+                for which in range(2):
+                    for j in js:
+                        first_layer(j, s, which)
 
-        def hidden(j, unit, words=None, on_vector=False):
-            if words is None:
-                words = stage.tile([P, H // 2], F32, name="hb")[:]
-            hb = words.bitcast(BF16)
+        def relu(j, r):
+            nc.scalar.activation(
+                r.rearrange("j u (p d) -> j u p d", d=2),
+                bank[AB[j][0]][:].rearrange("j (p u d) -> j u p d", u=2, d=2),
+                RELU,
+            )
+
+        def product(j, r, words):
             nc.vector.tensor_tensor(
-                hb.rearrange("j (u p d) -> j u p d", u=2, d=2),
-                banks[j][1][:].rearrange("j (p u d) -> j u p d", u=2, d=2),
-                relu_a[j].rearrange("j u (p d) -> j u p d", d=2),
+                words.bitcast(BF16).rearrange("j (u p d) -> j u p d", u=2, d=2),
+                bank[AB[j][1]][:].rearrange("j (p u d) -> j u p d", u=2, d=2),
+                r.rearrange("j u (p d) -> j u p d", d=2),
                 MULT,
             )
-            if unit not in turning:
-                turning[unit] = psum.tile([P, 2, len(unit) * P], F32, name="bank")
-            ht = turning[unit]
-            at = (j - unit[0]) * P
+
+        def turn(words, b, n, at):
+            ht = bank[b][:, : 2 * n].rearrange("p (u j) -> p u j", u=2)
             for u in range(2):
                 nc.tensor.transpose(ht[:, u, at : at + P], words[:, u * P : (u + 1) * P], ident[:])
-            if j == unit[-1]:
-                hi4 = stage.tile([P, len(unit) * P * PACK], BF16, name="hi4", align_bytes=64, bufs=4)
-                (nc.vector.tensor_copy if on_vector else nc.scalar.copy)(
-                    hi4[:].bitcast(F32).rearrange("p (j u) -> p j u", u=2), ht[:].rearrange("p u j -> p j u")
-                )
-                turned[unit] = hi4
 
-        def second_layer(unit, split=False):
-            e = unit[0] * P // C
-            cols = slice(unit[0] * P, (unit[-1] + 1) * P)
-            nc.vector.quantize_mx(out=hq[:, cols].bitcast(FP8X4), scales=hs[:, cols], in_=turned[unit][:])
-            acc_y = [psum.tile([P, N // P, len(unit) * P], F32, name="bank")]
-            acc_y.append(psum.tile([P, N // P, len(unit) * P], F32, name="bank") if split else acc_y[0])
-            for m in range(N // P):
-                nc.tensor.matmul_mx(
-                    out=acc_y[m][:, m, :],
-                    lhsT=w2c[:, e, 2 * m * P : 2 * (m + 1) * P].bitcast(FP4X4),
-                    lhsT_scale=w2s[:, e, m * P : (m + 1) * P],
-                    rhs=hq[:, cols].bitcast(FP8X4),
-                    rhs_scale=hs[:, cols],
-                    start=True,
-                    stop=True,
-                )
-            results[unit] = acc_y
+        def turned(b, n, hi4):
+            nc.scalar.copy(
+                hi4.rearrange("p (j u) -> p j u", u=2),
+                bank[b][:, : 2 * n].rearrange("p (u j) -> p j u", u=2),
+            )
 
-        def keep_y(unit, how="s"):
-            cols = slice(unit[0] * P, (unit[-1] + 1) * P)
-            copies = {"s": nc.scalar.copy, "v": nc.vector.tensor_copy}
-            if len(how) == 1:
-                copies[how](y[:, :, cols], results[unit][0][:])
-            else:
-                for m in range(N // P):
-                    copies[how[m]](y[:, m, cols], results[unit][m][:, m, :])
+        def quantize_h(lo, n, hi4):
+            nc.vector.quantize_mx(out=hq[:, lo : lo + n].bitcast(FP8X4), scales=hs[:, lo : lo + n], in_=hi4.bitcast(BF16))
 
-        A, B, Z = GROUPS
-        gather(0, *A, 0)
-        gather(1, *A, 1)
-        quantize_x(0, 0, 512)
-        first_layer(0, [0])
-        first_layer(1, [0])
-        first_layer(2, [0])
-        first_layer(3, [0])
-        gather(2, *A, 0)
-        quantize_x(1, 0, 512)
-        first_layer(0, [1])
-        first_layer(1, [1])
-        first_layer(2, [1])
-        first_layer(3, [1])
-        gather(0, *B, 1)
-        quantize_x(2, 0, 512)
-        first_layer(0, [2])
-        first_layer(1, [2])
-        first_layer(3, [2], in_ring=ring[:, 1, 2, :])
-        gather(1, *B, 0)
-        first_layer(2, [2], in_ring=ring[:, 0, 3, :])
-        quantize_x(0, 512, 512)
-        hidden(0, (0, 1))
-        hidden(1, (0, 1))
-        hidden(2, (2, 3))
-        hidden(3, (2, 3))
-        gather(2, *B, 1)
-        second_layer((0, 1))
-        gather(0, *Z, 0)
-        quantize_x(2, 512, 256)
-        first_layer(5, [0, 1])
-        keep_y((0, 1))
-        gather(1, *Z, 1)
-        first_layer(4, [0, 1])
-        quantize_x(0, 768, 256)
-        first_layer(4, [2], in_ring=ring[:, 1, 1, :])
-        second_layer((2, 3))
-        gather(2, 768, 896, 0)
-        quantize_x(1, 768, 256)
-        first_layer(6, [0])
-        first_layer(5, [2], in_ring=ring[:, 0, 1, :])
-        quantize_x(2, 768, 128)
-        gather(2, 896, 1024, 0, on_vector=True, late=1)
-        first_layer(7, [0])
-        first_layer(7, [1])
-        first_layer(6, [1])
-        first_layer(6, [2])
-        keep_y((2, 3))
-        quantize_x(2, 896, 128)
-        first_layer(7, [2])
-        hidden(5, (5,), gate_sb[:, 640:896], on_vector=False)
-        hidden(4, (4,), xb[:, PASSES * S * PACK - 768 : PASSES * S * PACK - 256].bitcast(F32), on_vector=False)
-        hidden(6, (6,), on_vector=False)
-        hidden(7, (7,), on_vector=True)
-        second_layer((5,), split=False)
-        second_layer((4,), split=True)
-        second_layer((6,), split=True)
-        keep_y((5,), "s")
-        keep_y((4,), "sv")
-        second_layer((7,), split=True)
-        keep_y((6,), "vs")
-        keep_y((7,), "vs")
+        def second_layer(lo, n, m, acc):
+            e = lo // C
+            nc.tensor.matmul_mx(
+                out=acc,
+                lhsT=w2c[:, e, 2 * m * P : 2 * (m + 1) * P].bitcast(FP4X4),
+                lhsT_scale=w2s[:, e, m * P : (m + 1) * P],
+                rhs=hq[:, lo : lo + n].bitcast(FP8X4),
+                rhs_scale=hs[:, lo : lo + n],
+                start=True,
+                stop=True,
+            )
 
-        pieces = ((0, 0, T), (1, 0, 384), (1, 384, T))
-        pending = None
-        for m, lo, hi in pieces:
-            got = []
-            for pos in (pos1_sb, pos2_sb):
-                g = stage.tile([P, hi - lo], F32, name="g", bufs=6)
-                nc.vector.tensor_copy(g[:], y[:, m, :].indirect(pos[:, lo // 16 : hi // 16]))
-                got.append(g)
-                if pending is not None:
-                    pending()
-                    pending = None
+        def results(lo, n, banks):
+            for m in range(2):
+                second_layer(lo, n, m, bank[banks[m]][:, m * n : (m + 1) * n])
 
-            def finish(m=m, lo=lo, hi=hi, got=got):
-                res = stage.tile([P, hi - lo], F32, name="res")
-                nc.vector.tensor_tensor(res[:], got[0][:], got[1][:], ADD)
-                nc.sync.dma_start(out[m * P : (m + 1) * P, lo:hi], res[:])
+        def keep_y(lo, n, banks, m):
+            nc.scalar.copy(y[m][:, lo : lo + n], bank[banks[m]][:, m * n : (m + 1) * n])
 
-            pending = finish
-        pending()
+        gA0, gA1, gA2 = (4608, 512), (2048, 512), (4608, 512)
+        gB0, gB1, gB2 = (2048, 256), (3072, 256), (9472, 512)
+        gZ0, gZ1, gZa, gZb = (12544, 256), (11008, 256), (12032, 128), (12544, 256)
+        xA0, xA1, xA2a, xA2b, xB0, xB1, xB2, xZ0, xZ1, xZa, xZb = 3584, 6144, 2816, 3328, 0, 11008, 12800, 12016, 12800, 13312, 768
+        r = [halves(3840)] + [halves(9472 + 512 * j) for j in range(3)] + [halves(11392, 1152)] + [halves(7168 + 512 * j) for j in range(3)]
+        hb = [room(14336 + 256 * j, 256) for j in range(5)]
+        hb = hb + [gate_sb[:, 960:1216], room(15616, 256), room(15872, 256)]
+        hi03, hi4, hi5, hi6, hi7 = room(13312, 1024), room(1024, 256), room(1280, 256), room(1536, 256), room(1792, 256)
+        ALL = range(PACK)
+
+        gather(0, 0, 512, gA0, ALL)
+        weave(512, gA0, xA0)
+        quantize_x(0, 0, 512, xA0)
+        both(range(4), [0])
+        gather(1, 0, 512, gA1, ALL)
+        weave(512, gA1, xA1)
+        quantize_x(1, 0, 512, xA1)
+        both(range(4), [1])
+        gather(2, 0, 512, gA2, ALL)
+        weave(256, gA2, xA2a)
+        weave(256, gA2, xA2b, 256)
+        quantize_x(2, 0, 256, xA2a)
+        both((0, 1), [2])
+        gather(0, 512, 768, gB0, ALL)
+        quantize_x(2, 256, 256, xA2b)
+        both((2, 3), [2])
+        for j in range(4):
+            relu(j, r[j])
+        weave(256, gB0, xB0)
+        for j in range(4):
+            product(j, r[j], hb[j])
+            turn(hb[j], 1 + 4 * (j // 2), 256, (j % 2) * P)
+        quantize_x(0, 512, 256, xB0)
+        both((4, 5), [0])
+        gather(1, 512, 768, gB1, ALL)
+        turned(1, 256, hi03[:, :512])
+        turned(5, 256, hi03[:, 512:])
+        weave(256, gB1, xB1)
+        quantize_x(1, 512, 256, xB1)
+        both((4, 5), [1])
+        gather(2, 512, 768, gB2, ALL)
+        weave(256, gB2, xB2)
+        quantize_h(0, 512, hi03)
+        quantize_x(2, 512, 256, xB2)
+        both((4, 5), [2])
+        relu(4, r[4])
+        relu(5, r[5])
+        results(0, 256, (3, 3))
+        results(256, 256, (7, 7))
+        for m in range(2):
+            keep_y(0, 256, (3, 3), m)
+        for m in range(2):
+            keep_y(256, 256, (7, 7), m)
+        product(4, r[4], hb[4])
+        turn(hb[4], 0, P, 0)
+        gather(0, 768, S, gZ0, (3, 2, 1, 0))
+        weave(256, gZ0, xZ0)
+        turned(0, P, hi4)
+        quantize_x(0, 768, 256, xZ0)
+        both((6, 7), [0])
+        quantize_h(512, P, hi4)
+        results(512, P, (0, 0))
+        gather(1, 768, S, gZ1, ALL)
+        weave(256, gZ1, xZ1)
+        quantize_x(1, 768, 256, xZ1)
+        both((6,), [1])
+        gather(2, 768, 896, gZa, ALL)
+        weave(128, gZa, xZa)
+        quantize_x(2, 768, 128, xZa)
+        both((6,), [2])
+        both((7,), [1])
+        for m in range(2):
+            keep_y(512, P, (0, 0), m)
+        gather(2, 896, S, gZb, ALL)
+        weave(128, gZb, xZb)
+        quantize_x(2, 896, 128, xZb)
+        both((7,), [2])
+        relu(6, r[6])
+        relu(7, r[7])
+        product(7, r[7], hb[7])
+        turn(hb[7], 1, P, 0)
+        turned(1, P, hi7)
+        quantize_h(896, P, hi7)
+        product(6, r[6], hb[6])
+        results(896, P, (5, 3))
+        keep_y(896, P, (5, 3), 0)
+        turn(hb[6], 2, P, 0)
+        turned(2, P, hi6)
+        quantize_h(768, P, hi6)
+        product(5, r[5], hb[5])
+        results(768, P, (6, 6))
+        keep_y(768, P, (6, 6), 0)
+        turn(hb[5], 4, P, 0)
+        turned(4, P, hi5)
+        quantize_h(640, P, hi5)
+        results(640, P, (0, 0))
+        keep_y(640, P, (0, 0), 0)
+        keep_y(896, P, (5, 3), 1)
+        keep_y(768, P, (6, 6), 1)
+        keep_y(640, P, (0, 0), 1)
+
+        first = [room(16128 + 512 * m, 512) for m in range(2)]
+        total = [room(17152 + 512 * m, 512) for m in range(2)]
+        for m in range(2):
+            nc.vector.tensor_copy(first[m], y[m][:].indirect(pos1_sb[:]))
+        for m, lo, hi in ((0, 0, T), (1, 0, 384), (1, 384, T)):
+            nc.vector.tensor_tensor(
+                total[m][:, lo:hi], y[m][:].indirect(pos2_sb[:, lo // 16 : hi // 16]), first[m][:, lo:hi], ADD
+            )
+            nc.sync.dma_start(out[m * P : (m + 1) * P, lo:hi], total[m][:, lo:hi])

@@ -47,8 +47,8 @@ def tile_moe_pre_glu_relu_kernel(
         w1c = keep.tile([P, E, PASSES, 2 * H], U8, name="w1c", align_bytes=64)
         w3c = keep.tile([P, E, PASSES, 2 * H], U8, name="w3c", align_bytes=64)
         w2c = keep.tile([P, E, 2 * N], U8, name="w2c", align_bytes=64)
-        w1s = keep.tile([P, E * PASSES, H], U8, name="w1s", align_bytes=64)
-        w3s = keep.tile([P, E * PASSES, H], U8, name="w3s", align_bytes=64)
+        w1s = [keep.tile([P, 2 * PASSES, H], U8, name=f"w1s{h}", align_bytes=64) for h in range(2)]
+        w3s = [keep.tile([P, 2 * PASSES, H], U8, name=f"w3s{h}", align_bytes=64) for h in range(2)]
         w2s = keep.tile([P, E, N], U8, name="w2s", align_bytes=64)
         xq = keep.tile([P, PASSES * S], U32, name="xq", align_bytes=64)
         xs = keep.tile([P, PASSES * S], U8, name="xs", align_bytes=64)
@@ -59,9 +59,11 @@ def tile_moe_pre_glu_relu_kernel(
         arena = keep.tile([P, ARENA], F32, name="arena", align_bytes=64)
         bank = [psum.tile([P, H], F32, name=f"bank{b}") for b in range(8)]
 
-        nc.vector.memset(w1s[:].bitcast(I32), 0)
+        nc.vector.memset(w1s[0][:].bitcast(I32), 0)
+        nc.vector.memset(w3s[0][:].bitcast(I32), 0)
         make_identity(nc, ident[:])
-        nc.gpsimd.memset(w3s[:].bitcast(I32), 0)
+        nc.gpsimd.memset(w1s[1][:].bitcast(I32), 0)
+        nc.gpsimd.memset(w3s[1][:].bitcast(I32), 0)
         nc.gpsimd.memset(w2s[:].bitcast(I32), 0)
 
         x_rows = xT.rearrange("(s p t) c -> s t p c", p=P, t=PACK)
@@ -92,13 +94,15 @@ def tile_moe_pre_glu_relu_kernel(
         load_x(1, [0, 1, 2, 3])
         load_x(2, [0, 1, 2, 3])
         load_gate(512, S)
-        load_scales(w1s, w1_scales)
-        load_scales(w3s, w3_scales)
-        load_scales(w2s, w2_scales)
+        load_scales(w1s[0], w1_scales[:2])
+        load_scales(w3s[0], w3_scales[:2])
         load_words(0)
         load_words(1)
-        nc.sync.dma_start(w2c[:].bitcast(I32), w2_words.rearrange("e s p b -> p (e s) b").bitcast(I32))
+        load_scales(w1s[1], w1_scales[2:])
+        load_scales(w3s[1], w3_scales[2:])
+        load_scales(w2s, w2_scales)
         load_words(2)
+        nc.sync.dma_start(w2c[:].bitcast(I32), w2_words.rearrange("e s p b -> p (e s) b").bitcast(I32))
         load_words(3)
         nc.sync.dma_start(pos1_sb[:], pos1)
         nc.sync.dma_start(pos2_sb[:], pos2)
@@ -145,7 +149,7 @@ def tile_moe_pre_glu_relu_kernel(
                 lhsT=xq[:, cols].bitcast(FP8X4),
                 lhsT_scale=xs[:, cols],
                 rhs=codes[:, e, s, :].bitcast(FP4X4),
-                rhs_scale=plane[:, e * PASSES + s, :],
+                rhs_scale=plane[e // 2][:, (e % 2) * PASSES + s, :],
                 start=(s == 0),
                 stop=(s == PASSES - 1),
             )
@@ -217,11 +221,11 @@ def tile_moe_pre_glu_relu_kernel(
         gather(0, 0, 512, gA0, ALL)
         weave(512, gA0, xA0)
         quantize_x(0, 0, 512, xA0)
-        both(range(4), [0])
         gather(1, 0, 512, gA1, ALL)
         weave(512, gA1, xA1)
         quantize_x(1, 0, 512, xA1)
-        both(range(4), [1])
+        both((0, 1), [0, 1])
+        both((2, 3), [0, 1])
         gather(2, 0, 512, gA2, ALL)
         weave(256, gA2, xA2a)
         weave(256, gA2, xA2b, 256)

@@ -27,7 +27,7 @@ RELU = mybir.ActivationFunctionType.Relu
 GROUPS = ((0, 512), (512, 768), (768, 1024))
 PAD = 32
 HEAD = 128
-ARENA = 18176
+ARENA = 21760
 AB = ((0, 1), (2, 3), (4, 5), (6, 7), (0, 2), (4, 6), (1, 3), (5, 7))
 
 
@@ -42,7 +42,7 @@ def tile_moe_pre_glu_relu_kernel(
         offs_sb = keep.tile([P, S // 16], U16, name="offs_sb")
         pos1_sb = keep.tile([P, T // 16], U16, name="pos1_sb")
         pos2_sb = keep.tile([P, T // 16], U16, name="pos2_sb")
-        gate_sb = keep.tile([P, S + 256], F32, name="gate_sb", align_bytes=64)
+        gate_sb = keep.tile([P, S], F32, name="gate_sb")
         planes = [[keep.tile([P, T + PAD], F32, name=f"x{s}{t}") for t in range(PACK)] for s in range(PASSES)]
         w1c = keep.tile([P, E, PASSES, 2 * H], U8, name="w1c", align_bytes=64)
         w3c = keep.tile([P, E, PASSES, 2 * H], U8, name="w3c", align_bytes=64)
@@ -61,8 +61,8 @@ def tile_moe_pre_glu_relu_kernel(
 
         nc.vector.memset(w1s[0][:].bitcast(I32), 0)
         nc.vector.memset(w3s[0][:].bitcast(I32), 0)
+        nc.vector.memset(w1s[1][:].bitcast(I32), 0)
         make_identity(nc, ident[:])
-        nc.gpsimd.memset(w1s[1][:].bitcast(I32), 0)
         nc.gpsimd.memset(w3s[1][:].bitcast(I32), 0)
         nc.gpsimd.memset(w2s[:].bitcast(I32), 0)
 
@@ -208,14 +208,14 @@ def tile_moe_pre_glu_relu_kernel(
         def keep_y(lo, n, banks, m):
             nc.scalar.copy(y[m][:, lo : lo + n], bank[banks[m]][:, m * n : (m + 1) * n])
 
-        gA0, gA1, gA2 = (4608, 512), (2048, 512), (4608, 512)
-        gB0, gB1, gB2 = (2048, 256), (3072, 256), (9472, 512)
-        gZ0, gZ1, gZa, gZb = (12544, 256), (11008, 256), (12032, 128), (12544, 256)
-        xA0, xA1, xA2a, xA2b, xB0, xB1, xB2, xZ0, xZ1, xZa, xZb = 3584, 6144, 2816, 3328, 0, 11008, 12800, 12016, 12800, 13312, 768
-        r = [halves(3840)] + [halves(9472 + 512 * j) for j in range(3)] + [halves(11392, 1152)] + [halves(7168 + 512 * j) for j in range(3)]
+        gA0, gA1, gA2 = (4608, 512), (3072, 512), (4608, 512)
+        gB0, gB1, gB2 = (3840, 256), (4864, 256), (5632, 256)
+        gZ0, gZ1, gZa, gZb = (5376, 256), (6144, 256), (5376, 128), (5632, 256)
+        xA0, xA1, xA2a, xA2b, xB0, xB1, xB2, xZ0, xZ1, xZa, xZb = 0, 1024, 11008, 11520, 12032, 12544, 13056, 13568, 18176, 18688, 18944
+        r = [halves(5632), halves(19200), halves(6144), halves(19712), halves(6272, 512)] + [halves(20224 + 512 * j) for j in range(3)]
         hb = [room(14336 + 256 * j, 256) for j in range(5)]
-        hb = hb + [gate_sb[:, 960:1216], room(15616, 256), room(15872, 256)]
-        hi03, hi4, hi5, hi6, hi7 = room(13312, 1024), room(1024, 256), room(1280, 256), room(1536, 256), room(1792, 256)
+        hb = hb + [room(5376, 256), room(15616, 256), room(15872, 256)]
+        hi03, hi4, hi5, hi6, hi7 = room(2048, 1024), room(9984, 256), room(10240, 256), room(10496, 256), room(10752, 256)
         ALL = range(PACK)
 
         gather(0, 0, 512, gA0, ALL)
@@ -226,7 +226,7 @@ def tile_moe_pre_glu_relu_kernel(
         quantize_x(1, 0, 512, xA1)
         both((0, 1), [0, 1])
         both((2, 3), [0, 1])
-        gather(2, 0, 512, gA2, ALL)
+        gather(2, 0, 512, gA2, (3, 2, 1, 0))
         weave(256, gA2, xA2a)
         weave(256, gA2, xA2b, 256)
         quantize_x(2, 0, 256, xA2a)
@@ -248,7 +248,7 @@ def tile_moe_pre_glu_relu_kernel(
         weave(256, gB1, xB1)
         quantize_x(1, 512, 256, xB1)
         both((4, 5), [1])
-        gather(2, 512, 768, gB2, ALL)
+        gather(2, 512, 768, gB2, (1, 2, 3, 0))
         weave(256, gB2, xB2)
         quantize_h(0, 512, hi03)
         quantize_x(2, 512, 256, xB2)
@@ -263,14 +263,14 @@ def tile_moe_pre_glu_relu_kernel(
             keep_y(256, 256, (7, 7), m)
         product(4, r[4], hb[4])
         turn(hb[4], 0, P, 0)
-        gather(0, 768, S, gZ0, (3, 2, 1, 0))
+        gather(0, 768, S, gZ0, ALL)
         weave(256, gZ0, xZ0)
         turned(0, P, hi4)
         quantize_x(0, 768, 256, xZ0)
         both((6, 7), [0])
         quantize_h(512, P, hi4)
         results(512, P, (0, 0))
-        gather(1, 768, S, gZ1, ALL)
+        gather(1, 768, S, gZ1, (1, 2, 3, 0))
         weave(256, gZ1, xZ1)
         quantize_x(1, 768, 256, xZ1)
         both((6,), [1])
@@ -281,7 +281,7 @@ def tile_moe_pre_glu_relu_kernel(
         both((7,), [1])
         for m in range(2):
             keep_y(512, P, (0, 0), m)
-        gather(2, 896, S, gZb, ALL)
+        gather(2, 896, S, gZb, (1, 2, 3, 0))
         weave(128, gZb, xZb)
         quantize_x(2, 896, 128, xZb)
         both((7,), [2])

@@ -114,8 +114,8 @@ def tile_moe_pre_glu_relu_kernel(
         def room(at, words):
             return arena[:, at : at + words]
 
-        def halves(at, step=256):
-            return room(at, 2 * step).rearrange("p (u c) -> p u c", u=2)[:, :, :256]
+        def halves(at, step=256, n=256):
+            return room(at, 2 * step).rearrange("p (u c) -> p u c", u=2)[:, :, :n]
 
         def gather(s, lo, hi, place, ts):
             base, stride = place
@@ -160,25 +160,25 @@ def tile_moe_pre_glu_relu_kernel(
                     for j in js:
                         first_layer(j, s, which)
 
-        def relu(j, r):
+        def relu(j, r, u0=0, u1=2):
             nc.scalar.activation(
-                r.rearrange("j u (p d) -> j u p d", d=2),
-                bank[AB[j][0]][:].rearrange("j (p u d) -> j u p d", u=2, d=2),
+                r.rearrange("j u (p d) -> j u p d", d=2)[:, u0:u1],
+                bank[AB[j][0]][:].rearrange("j (p u d) -> j u p d", u=2, d=2)[:, u0:u1],
                 RELU,
             )
 
-        def product(j, r, words):
+        def product(j, r, words, u0=0, u1=2):
             nc.vector.tensor_tensor(
-                words.bitcast(BF16).rearrange("j (u p d) -> j u p d", u=2, d=2),
-                bank[AB[j][1]][:].rearrange("j (p u d) -> j u p d", u=2, d=2),
-                r.rearrange("j u (p d) -> j u p d", d=2),
+                words.bitcast(BF16).rearrange("j u (p d) -> j u p d", d=2)[:, u0:u1],
+                bank[AB[j][1]][:].rearrange("j (p u d) -> j u p d", u=2, d=2)[:, u0:u1],
+                r.rearrange("j u (p d) -> j u p d", d=2)[:, u0:u1],
                 MULT,
             )
 
         def turn(words, b, n, at):
             ht = bank[b][:, : 2 * n].rearrange("p (u j) -> p u j", u=2)
             for u in range(2):
-                nc.tensor.transpose(ht[:, u, at : at + P], words[:, u * P : (u + 1) * P], ident[:])
+                nc.tensor.transpose(ht[:, u, at : at + P], words[:, u, :], ident[:])
 
         def turned(b, n, hi4):
             nc.scalar.copy(
@@ -209,13 +209,13 @@ def tile_moe_pre_glu_relu_kernel(
             nc.scalar.copy(y[m][:, lo : lo + n], bank[banks[m]][:, m * n : (m + 1) * n])
 
         gA0, gA1, gA2 = (4608, 512), (3072, 512), (4608, 512)
-        gB0, gB1, gB2 = (3840, 256), (4864, 256), (5632, 256)
-        gZ0, gZ1, gZa, gZb = (5376, 256), (6144, 256), (5376, 128), (5632, 256)
+        gB0, gB1, gB2 = (3840, 256), (4864, 256), (5632, 512)
+        gZ0, gZ1, gZa, gZb = (5120, 256), (5888, 512), (5120, 128), (5504, 256)
         xA0, xA1, xA2a, xA2b, xB0, xB1, xB2, xZ0, xZ1, xZa, xZb = 0, 1024, 11008, 11520, 12032, 12544, 13056, 13568, 18176, 18688, 18944
-        r = [halves(5632), halves(19200), halves(6144), halves(19712), halves(6272, 512)] + [halves(20224 + 512 * j) for j in range(3)]
-        hb = [room(14336 + 256 * j, 256) for j in range(5)]
-        hb = hb + [room(5376, 256), room(15616, 256), room(15872, 256)]
-        hi03, hi4, hi5, hi6, hi7 = room(2048, 1024), room(9984, 256), room(10240, 256), room(10496, 256), room(10752, 256)
+        r = [halves(5632, 512), halves(19200), halves(6656, 512), halves(19712), halves(8192)] + [halves(20224 + 512 * j) for j in range(3)]
+        hb = [halves(14336, 128, 128), halves(14592, 128, 128), halves(5888, 512, 128), halves(7424, 128, 128)]
+        hb = hb + [halves(at, 128, 128) for at in (5136, 4880, 15616, 15872)]
+        hi03, hi45, hi6, hi7 = room(2048, 1024), room(9984, 512), room(10496, 256), room(10752, 256)
         ALL = range(PACK)
 
         gather(0, 0, 512, gA0, ALL)
@@ -239,37 +239,36 @@ def tile_moe_pre_glu_relu_kernel(
         weave(256, gB0, xB0)
         for j in range(4):
             product(j, r[j], hb[j])
-            turn(hb[j], 1 + 4 * (j // 2), 256, (j % 2) * P)
+        for j in range(2):
+            turn(hb[j], 1, 256, j * P)
         quantize_x(0, 512, 256, xB0)
         both((4, 5), [0])
         gather(1, 512, 768, gB1, ALL)
         turned(1, 256, hi03[:, :512])
-        turned(5, 256, hi03[:, 512:])
         weave(256, gB1, xB1)
         quantize_x(1, 512, 256, xB1)
         both((4, 5), [1])
         gather(2, 512, 768, gB2, (1, 2, 3, 0))
         weave(256, gB2, xB2)
-        quantize_h(0, 512, hi03)
+        quantize_h(0, 256, hi03[:, :512])
         quantize_x(2, 512, 256, xB2)
         both((4, 5), [2])
         relu(4, r[4])
         relu(5, r[5])
         results(0, 256, (3, 3))
-        results(256, 256, (7, 7))
+        for j in range(2):
+            turn(hb[2 + j], 0, 256, j * P)
+        turned(0, 256, hi03[:, 512:])
         for m in range(2):
             keep_y(0, 256, (3, 3), m)
-        for m in range(2):
-            keep_y(256, 256, (7, 7), m)
-        product(4, r[4], hb[4])
-        turn(hb[4], 0, P, 0)
         gather(0, 768, S, gZ0, ALL)
         weave(256, gZ0, xZ0)
-        turned(0, P, hi4)
         quantize_x(0, 768, 256, xZ0)
         both((6, 7), [0])
-        quantize_h(512, P, hi4)
-        results(512, P, (0, 0))
+        quantize_h(256, 256, hi03[:, 512:])
+        results(256, 256, (4, 4))
+        for m in range(2):
+            keep_y(256, 256, (4, 4), m)
         gather(1, 768, S, gZ1, (1, 2, 3, 0))
         weave(256, gZ1, xZ1)
         quantize_x(1, 768, 256, xZ1)
@@ -279,42 +278,45 @@ def tile_moe_pre_glu_relu_kernel(
         quantize_x(2, 768, 128, xZa)
         both((6,), [2])
         both((7,), [1])
-        for m in range(2):
-            keep_y(512, P, (0, 0), m)
         gather(2, 896, S, gZb, (1, 2, 3, 0))
         weave(128, gZb, xZb)
         quantize_x(2, 896, 128, xZb)
         both((7,), [2])
         relu(6, r[6])
-        relu(7, r[7])
-        product(7, r[7], hb[7])
+        for u in range(2):
+            relu(7, r[7], u, u + 1)
+        for u in range(2):
+            product(7, r[7], hb[7], u, u + 1)
         turn(hb[7], 1, P, 0)
         turned(1, P, hi7)
         quantize_h(896, P, hi7)
+        second_layer(896, P, 0, bank[5][:, :P])
+        nc.scalar.copy(y[0][:, 896:], bank[5][:, :P])
         product(6, r[6], hb[6])
-        results(896, P, (5, 3))
-        keep_y(896, P, (5, 3), 0)
-        turn(hb[6], 2, P, 0)
-        turned(2, P, hi6)
+        turn(hb[6], 0, P, 0)
+        turned(0, P, hi6)
         quantize_h(768, P, hi6)
-        product(5, r[5], hb[5])
-        results(768, P, (6, 6))
-        keep_y(768, P, (6, 6), 0)
-        turn(hb[5], 4, P, 0)
-        turned(4, P, hi5)
-        quantize_h(640, P, hi5)
-        results(640, P, (0, 0))
-        keep_y(640, P, (0, 0), 0)
-        keep_y(896, P, (5, 3), 1)
-        keep_y(768, P, (6, 6), 1)
-        keep_y(640, P, (0, 0), 1)
+        for j in (4, 5):
+            product(j, r[j], hb[j])
+            turn(hb[j], 4, 256, (j % 2) * P)
+        turned(4, 256, hi45)
+        quantize_h(512, 256, hi45)
+        second_layer(512, 256, 0, bank[2][:, :256])
+        second_layer(768, P, 0, bank[2][:, 256:384])
+        nc.scalar.copy(y[0][:, 512:896], bank[2][:, :384])
+        second_layer(512, 256, 1, bank[6][:, :256])
+        second_layer(768, P, 1, bank[6][:, 256:384])
+        second_layer(896, P, 1, bank[6][:, 384:])
+        nc.scalar.copy(y[1][:, 512:], bank[6][:])
 
         first = [room(16128 + 512 * m, 512) for m in range(2)]
         total = [room(17152 + 512 * m, 512) for m in range(2)]
         for m in range(2):
-            nc.vector.tensor_copy(first[m], y[m][:].indirect(pos1_sb[:]))
-        for m, lo, hi in ((0, 0, T), (1, 0, 384), (1, 384, T)):
-            nc.vector.tensor_tensor(
-                total[m][:, lo:hi], y[m][:].indirect(pos2_sb[:, lo // 16 : hi // 16]), first[m][:, lo:hi], ADD
-            )
-            nc.sync.dma_start(out[m * P : (m + 1) * P, lo:hi], total[m][:, lo:hi])
+            pieces = ((0, 384), (384, T))
+            for lo, hi in pieces:
+                nc.vector.tensor_copy(first[m][:, lo:hi], y[m][:].indirect(pos1_sb[:, lo // 16 : hi // 16]))
+            for lo, hi in pieces:
+                nc.vector.tensor_tensor(
+                    total[m][:, lo:hi], y[m][:].indirect(pos2_sb[:, lo // 16 : hi // 16]), first[m][:, lo:hi], ADD
+                )
+                nc.sync.dma_start(out[m * P : (m + 1) * P, lo:hi], total[m][:, lo:hi])

@@ -212,8 +212,8 @@ def tile_moe_pre_glu_relu_kernel(
         gB0, gB1, gB2 = (3840, 256), (4864, 256), (5632, 512)
         gZ0, gZ1, gZa, gZb = (5120, 256), (5888, 512), (5120, 128), (5504, 256)
         xA0, xA1, xA2a, xA2b, xB0, xB1, xB2, xZ0, xZ1, xZa, xZb = 0, 1024, 11008, 11520, 12032, 12544, 13056, 13568, 18176, 18688, 18944
-        r = [halves(5632, 512), halves(19200), halves(6656, 512), halves(19712), halves(8192)] + [halves(20224 + 512 * j) for j in range(3)]
-        hb = [halves(14336, 128, 128), halves(14592, 128, 128), halves(5888, 512, 128), halves(7424, 128, 128)]
+        r = [halves(5632, 1536), halves(19200), halves(8704), halves(19712), halves(8192)] + [halves(20224 + 512 * j) for j in range(3)]
+        hb = [halves(14336, 128, 128), halves(14592, 128, 128), halves(5888, 128, 128), halves(6400, 1024, 128)]
         hb = hb + [halves(at, 128, 128) for at in (5136, 4880, 15616, 15872)]
         hi03, hi45, hi6, hi7 = room(2048, 1024), room(9984, 512), room(10496, 256), room(10752, 256)
         ALL = range(PACK)
@@ -237,7 +237,7 @@ def tile_moe_pre_glu_relu_kernel(
         for j in range(4):
             relu(j, r[j])
         weave(256, gB0, xB0)
-        for j in range(4):
+        for j in range(3):
             product(j, r[j], hb[j])
         for j in range(2):
             turn(hb[j], 1, 256, j * P)
@@ -252,6 +252,7 @@ def tile_moe_pre_glu_relu_kernel(
         weave(256, gB2, xB2)
         quantize_h(0, 256, hi03[:, :512])
         quantize_x(2, 512, 256, xB2)
+        product(3, r[3], hb[3])
         both((4, 5), [2])
         relu(4, r[4])
         relu(5, r[5])

@@ -24,11 +24,21 @@ MULT = mybir.AluOpType.mult
 ADD = mybir.AluOpType.add
 RELU = mybir.ActivationFunctionType.Relu
 
-GROUPS = ((0, 512), (512, 768), (768, 1024))
 PAD = 32
 HEAD = 128
-ARENA = 21760
+LAST = 128
 AB = ((0, 1), (2, 3), (4, 5), (6, 7), (0, 2), (4, 6), (1, 3), (5, 7))
+
+CELL = 128
+A0, A1, A2 = (12, 4), (0, 4), (12, 4)
+B0, B1, B2 = (4, 2), (12, 2), (18, 4)
+Z0, Z1 = (14, 2), (20, 4)
+Z2A, Z2B = (14, 1), (17, 2)
+RELU0 = (18, 12)
+H2 = (20, 1)
+H3 = (24, 8)
+H4, H5 = (15, 1), (13, 1)
+STAGE_CELLS = 42
 
 
 def tile_moe_pre_glu_relu_kernel(
@@ -43,34 +53,51 @@ def tile_moe_pre_glu_relu_kernel(
         pos1_sb = keep.tile([P, T // 16], U16, name="pos1_sb")
         pos2_sb = keep.tile([P, T // 16], U16, name="pos2_sb")
         gate_sb = keep.tile([P, S], F32, name="gate_sb")
-        planes = [[keep.tile([P, T + PAD], F32, name=f"x{s}{t}") for t in range(PACK)] for s in range(PASSES)]
+        windows = [[keep.tile([P, T + PAD], F32, name=f"x{s}{t}") for t in range(PACK)] for s in range(PASSES)]
         w1c = keep.tile([P, E, PASSES, 2 * H], U8, name="w1c", align_bytes=64)
         w3c = keep.tile([P, E, PASSES, 2 * H], U8, name="w3c", align_bytes=64)
         w2c = keep.tile([P, E, 2 * N], U8, name="w2c", align_bytes=64)
-        w1s = [keep.tile([P, 2 * PASSES, H], U8, name=f"w1s{h}", align_bytes=64) for h in range(2)]
-        w3s = [keep.tile([P, 2 * PASSES, H], U8, name=f"w3s{h}", align_bytes=64) for h in range(2)]
+        w1s = keep.tile([P, E * PASSES, H], U8, name="w1s", align_bytes=64)
+        w3s = keep.tile([P, E * PASSES, H], U8, name="w3s", align_bytes=64)
         w2s = keep.tile([P, E, N], U8, name="w2s", align_bytes=64)
         xq = keep.tile([P, PASSES * S], U32, name="xq", align_bytes=64)
         xs = keep.tile([P, PASSES * S], U8, name="xs", align_bytes=64)
         hq = keep.tile([P, S], U32, name="hq", align_bytes=64)
         hs = keep.tile([P, S], U8, name="hs", align_bytes=64)
+        xb = keep.tile([P, PASSES * S * PACK], BF16, name="xb", align_bytes=64)
+        hb = keep.tile([P, S * PACK], BF16, name="hb", align_bytes=64)
         y = [keep.tile([P, S], F32, name=f"y{m}") for m in range(N // P)]
+        first = keep.tile([P, N // P * T], F32, name="first")
+        total = keep.tile([P, N // P * T], F32, name="total")
         ident = keep.tile([P, P], F32, name="ident")
-        arena = keep.tile([P, ARENA], F32, name="arena", align_bytes=64)
+        stage = keep.tile([P, STAGE_CELLS * CELL], F32, name="stage")
         bank = [psum.tile([P, H], F32, name=f"bank{b}") for b in range(8)]
 
-        nc.vector.memset(w1s[0][:].bitcast(I32), 0)
-        nc.vector.memset(w3s[0][:].bitcast(I32), 0)
-        nc.vector.memset(w1s[1][:].bitcast(I32), 0)
+        def rows(place, count, width):
+            cell, step = place
+            span = stage[:, cell * CELL : (cell + count * step) * CELL]
+            return span.rearrange("p (r c) -> p r c", r=count)[:, :, :width]
+
+        def own_halves(name, width):
+            return keep.tile([P, 2 * width], F32, name=name)[:].rearrange("p (u c) -> p u c", u=2)
+
+        relus = [rows(RELU0, 2, H // 2)]
+        relus.extend(own_halves(f"relu{j}", H // 2) for j in range(1, S // P))
+        pairs = [own_halves(f"pairs{j}", P) for j in (0, 1)]
+        pairs.extend(rows(place, 2, P) for place in (H2, H3, H4, H5))
+        pairs.extend(own_halves(f"pairs{j}", P) for j in (6, 7))
+
+        nc.vector.memset(w1s[:].bitcast(I32), 0)
+        nc.vector.memset(w3s[:, : 2 * PASSES].bitcast(I32), 0)
         make_identity(nc, ident[:])
-        nc.gpsimd.memset(w3s[1][:].bitcast(I32), 0)
+        nc.gpsimd.memset(w3s[:, 2 * PASSES :].bitcast(I32), 0)
         nc.gpsimd.memset(w2s[:].bitcast(I32), 0)
 
         x_rows = xT.rearrange("(s p t) c -> s t p c", p=P, t=PACK)
 
         def load_x(s, ts):
             for t in ts:
-                nc.sync.dma_start(planes[s][t][:, :T], x_rows[s, t])
+                nc.sync.dma_start(windows[s][t][:, :T], x_rows[s, t])
 
         def load_gate(lo, hi):
             nc.sync.dma_start(gate_sb[:, lo:hi], gate[:P, lo:hi])
@@ -89,235 +116,209 @@ def tile_moe_pre_glu_relu_kernel(
         load_x(0, [0])
         nc.sync.dma_start(offs_sb[:], offs)
         load_gate(0, HEAD)
-        load_gate(HEAD, 512)
+        load_gate(HEAD, 2 * C)
         load_x(0, [1, 2, 3])
-        load_x(1, [0, 1, 2, 3])
-        load_x(2, [0, 1, 2, 3])
-        load_gate(512, S)
-        load_scales(w1s[0], w1_scales[:2])
-        load_scales(w3s[0], w3_scales[:2])
+        load_x(1, range(PACK))
+        load_x(2, range(PACK))
+        load_gate(2 * C, S)
+        load_scales(w1s, w1_scales)
+        load_scales(w3s, w3_scales)
+        load_scales(w2s, w2_scales)
         load_words(0)
         load_words(1)
-        load_scales(w1s[1], w1_scales[2:])
-        load_scales(w3s[1], w3_scales[2:])
-        load_scales(w2s, w2_scales)
         load_words(2)
         nc.sync.dma_start(w2c[:].bitcast(I32), w2_words.rearrange("e s p b -> p (e s) b").bitcast(I32))
         load_words(3)
         nc.sync.dma_start(pos1_sb[:], pos1)
         nc.sync.dma_start(pos2_sb[:], pos2)
 
-        def word(s, slot):
-            lo, hi = [g for g in GROUPS if g[0] <= slot < g[1]][0]
-            return PASSES * lo + s * (hi - lo) + slot - lo
-
-        def room(at, words):
-            return arena[:, at : at + words]
-
-        def halves(at, step=256, n=256):
-            return room(at, 2 * step).rearrange("p (u c) -> p u c", u=2)[:, :, :n]
-
         def gather(s, lo, hi, place, ts):
-            base, stride = place
+            dst = rows(place, PACK, hi - lo)
             for t in ts:
                 for a, b in ((0, HEAD), (HEAD, hi)) if (s, t, lo) == (0, 0, 0) else ((lo, hi),):
                     nc.vector.tensor_tensor(
-                        room(base + t * stride + a - lo, b - a),
-                        planes[s][t][:].indirect(offs_sb[:, a // 16 : b // 16]),
+                        dst[:, t, a - lo : b - lo],
+                        windows[s][t][:].indirect(offs_sb[:, a // 16 : b // 16]),
                         gate_sb[:, a:b],
                         MULT,
                     )
 
-        def weave(n, place, at, lo=0):
-            base, stride = place
-            g4 = room(base, PACK * stride).rearrange("p (t c) -> p t c", t=PACK)[:, :, lo : lo + n]
+        def weave(s, lo, hi, place, at=0):
+            src = rows(place, PACK, at + hi - lo)[:, :, at:]
             nc.scalar.copy(
-                room(at, 2 * n).bitcast(BF16).rearrange("p (c i t) -> p c t i", i=4, t=PACK),
-                g4.rearrange("p t (c i) -> p c t i", i=4),
+                xb[:, (S * s + lo) * PACK : (S * s + hi) * PACK].rearrange("p (c i t) -> p c t i", i=4, t=PACK),
+                src.rearrange("p t (c i) -> p c t i", i=4),
             )
 
-        def quantize_x(s, lo, n, at):
-            w = word(s, lo)
-            nc.vector.quantize_mx(out=xq[:, w : w + n].bitcast(FP8X4), scales=xs[:, w : w + n], in_=room(at, 2 * n).bitcast(BF16))
+        def quantize_x(s, lo, hi):
+            a, b = S * s + lo, S * s + hi
+            nc.vector.quantize_mx(out=xq[:, a:b].bitcast(FP8X4), scales=xs[:, a:b], in_=xb[:, a * PACK : b * PACK])
 
-        def first_layer(j, s, which):
-            e = j * P // C
-            cols = slice(word(s, j * P), word(s, j * P) + P)
-            codes, plane = ((w1c, w1s), (w3c, w3s))[which]
-            nc.tensor.matmul_mx(
-                out=bank[AB[j][which]][:],
-                lhsT=xq[:, cols].bitcast(FP8X4),
-                lhsT_scale=xs[:, cols],
-                rhs=codes[:, e, s, :].bitcast(FP4X4),
-                rhs_scale=plane[e // 2][:, (e % 2) * PASSES + s, :],
-                start=(s == 0),
-                stop=(s == PASSES - 1),
-            )
+        def first_layer(tiles, passes):
+            for s in passes:
+                for which, (codes, plane) in enumerate(((w1c, w1s), (w3c, w3s))):
+                    for j in tiles:
+                        e = j * P // C
+                        cols = slice(S * s + j * P, S * s + (j + 1) * P)
+                        nc.tensor.matmul_mx(
+                            out=bank[AB[j][which]][:],
+                            lhsT=xq[:, cols].bitcast(FP8X4),
+                            lhsT_scale=xs[:, cols],
+                            rhs=codes[:, e, s, :].bitcast(FP4X4),
+                            rhs_scale=plane[:, e * PASSES + s, :],
+                            start=(s == 0),
+                            stop=(s == PASSES - 1),
+                        )
 
-        def both(js, ss):
-            for s in ss:
-                for which in range(2):
-                    for j in js:
-                        first_layer(j, s, which)
+        def by_half(b):
+            return bank[b][:].rearrange("j (p u d) -> j u p d", u=2, d=2)
 
-        def relu(j, r, u0=0, u1=2):
-            nc.scalar.activation(
-                r.rearrange("j u (p d) -> j u p d", d=2)[:, u0:u1],
-                bank[AB[j][0]][:].rearrange("j (p u d) -> j u p d", u=2, d=2)[:, u0:u1],
-                RELU,
-            )
+        def relu(j, us=slice(0, 2)):
+            nc.scalar.activation(relus[j].rearrange("j u (p d) -> j u p d", d=2)[:, us], by_half(AB[j][0])[:, us], RELU)
 
-        def product(j, r, words, u0=0, u1=2):
+        def product(j, us=slice(0, 2)):
             nc.vector.tensor_tensor(
-                words.bitcast(BF16).rearrange("j u (p d) -> j u p d", d=2)[:, u0:u1],
-                bank[AB[j][1]][:].rearrange("j (p u d) -> j u p d", u=2, d=2)[:, u0:u1],
-                r.rearrange("j u (p d) -> j u p d", d=2)[:, u0:u1],
+                pairs[j].bitcast(BF16).rearrange("j u (p d) -> j u p d", d=2)[:, us],
+                by_half(AB[j][1])[:, us],
+                relus[j].rearrange("j u (p d) -> j u p d", d=2)[:, us],
                 MULT,
             )
 
-        def turn(words, b, n, at):
-            ht = bank[b][:, : 2 * n].rearrange("p (u j) -> p u j", u=2)
+        def turn(j, b, width, at):
+            dst = bank[b][:, : 2 * width].rearrange("p (u j) -> p u j", u=2)
             for u in range(2):
-                nc.tensor.transpose(ht[:, u, at : at + P], words[:, u, :], ident[:])
+                nc.tensor.transpose(dst[:, u, at : at + P], pairs[j][:, u, :], ident[:])
 
-        def turned(b, n, hi4):
+        def copy_turned(b, lo, hi):
             nc.scalar.copy(
-                hi4.rearrange("p (j u) -> p j u", u=2),
-                bank[b][:, : 2 * n].rearrange("p (u j) -> p j u", u=2),
+                hb[:, lo * PACK : hi * PACK].bitcast(F32).rearrange("p (j u) -> p j u", u=2),
+                bank[b][:, : 2 * (hi - lo)].rearrange("p (u j) -> p j u", u=2),
             )
 
-        def quantize_h(lo, n, hi4):
-            nc.vector.quantize_mx(out=hq[:, lo : lo + n].bitcast(FP8X4), scales=hs[:, lo : lo + n], in_=hi4.bitcast(BF16))
+        def quantize_h(lo, hi):
+            nc.vector.quantize_mx(out=hq[:, lo:hi].bitcast(FP8X4), scales=hs[:, lo:hi], in_=hb[:, lo * PACK : hi * PACK])
 
-        def second_layer(lo, n, m, acc):
+        def second_layer(lo, hi, m, b, at):
             e = lo // C
             nc.tensor.matmul_mx(
-                out=acc,
+                out=bank[b][:, at : at + hi - lo],
                 lhsT=w2c[:, e, 2 * m * P : 2 * (m + 1) * P].bitcast(FP4X4),
                 lhsT_scale=w2s[:, e, m * P : (m + 1) * P],
-                rhs=hq[:, lo : lo + n].bitcast(FP8X4),
-                rhs_scale=hs[:, lo : lo + n],
+                rhs=hq[:, lo:hi].bitcast(FP8X4),
+                rhs_scale=hs[:, lo:hi],
                 start=True,
                 stop=True,
             )
 
-        def results(lo, n, banks):
-            for m in range(2):
-                second_layer(lo, n, m, bank[banks[m]][:, m * n : (m + 1) * n])
+        def copy_y(lo, hi, m, b, at):
+            nc.scalar.copy(y[m][:, lo:hi], bank[b][:, at : at + hi - lo])
 
-        def keep_y(lo, n, banks, m):
-            nc.scalar.copy(y[m][:, lo : lo + n], bank[banks[m]][:, m * n : (m + 1) * n])
+        up = range(PACK)
+        down = (3, 2, 1, 0)
+        wrap = (1, 2, 3, 0)
+        e2, e3, t5, t7 = 2 * C, 3 * C, 5 * P, 7 * P
 
-        gA0, gA1, gA2 = (4608, 512), (3072, 512), (4608, 512)
-        gB0, gB1, gB2 = (3840, 256), (4864, 256), (5632, 512)
-        gZ0, gZ1, gZa, gZb = (5120, 256), (5888, 512), (5120, 128), (5504, 256)
-        xA0, xA1, xA2a, xA2b, xB0, xB1, xB2, xZ0, xZ1, xZa, xZb = 0, 1024, 11008, 11520, 12032, 12544, 13056, 13568, 18176, 18688, 18944
-        r = [halves(5632, 1536), halves(19200), halves(8704), halves(19712), halves(8192)] + [halves(20224 + 512 * j) for j in range(3)]
-        hb = [halves(14336, 128, 128), halves(14592, 128, 128), halves(5888, 128, 128), halves(6400, 1024, 128)]
-        hb = hb + [halves(at, 128, 128) for at in (5136, 4880, 15616, 15872)]
-        hi03, hi45, hi6, hi7 = room(2048, 1024), room(9984, 512), room(10496, 256), room(10752, 256)
-        ALL = range(PACK)
-
-        gather(0, 0, 512, gA0, ALL)
-        weave(512, gA0, xA0)
-        quantize_x(0, 0, 512, xA0)
-        gather(1, 0, 512, gA1, ALL)
-        weave(512, gA1, xA1)
-        quantize_x(1, 0, 512, xA1)
-        both((0, 1), [0, 1])
-        both((2, 3), [0, 1])
-        gather(2, 0, 512, gA2, (3, 2, 1, 0))
-        weave(256, gA2, xA2a)
-        weave(256, gA2, xA2b, 256)
-        quantize_x(2, 0, 256, xA2a)
-        both((0, 1), [2])
-        gather(0, 512, 768, gB0, ALL)
-        quantize_x(2, 256, 256, xA2b)
-        both((2, 3), [2])
+        for s, place in ((0, A0), (1, A1)):
+            gather(s, 0, e2, place, up)
+            weave(s, 0, e2, place)
+            quantize_x(s, 0, e2)
+        first_layer((0, 1), (0, 1))
+        first_layer((2, 3), (0, 1))
+        gather(2, 0, e2, A2, down)
+        weave(2, 0, C, A2)
+        weave(2, C, e2, A2, at=C)
+        quantize_x(2, 0, C)
+        first_layer((0, 1), (2,))
+        gather(0, e2, e3, B0, up)
+        quantize_x(2, C, e2)
+        first_layer((2, 3), (2,))
         for j in range(4):
-            relu(j, r[j])
-        weave(256, gB0, xB0)
-        for j in range(3):
-            product(j, r[j], hb[j])
-        for j in range(2):
-            turn(hb[j], 1, 256, j * P)
-        quantize_x(0, 512, 256, xB0)
-        both((4, 5), [0])
-        gather(1, 512, 768, gB1, ALL)
-        turned(1, 256, hi03[:, :512])
-        weave(256, gB1, xB1)
-        quantize_x(1, 512, 256, xB1)
-        both((4, 5), [1])
-        gather(2, 512, 768, gB2, (1, 2, 3, 0))
-        weave(256, gB2, xB2)
-        quantize_h(0, 256, hi03[:, :512])
-        quantize_x(2, 512, 256, xB2)
-        product(3, r[3], hb[3])
-        both((4, 5), [2])
-        relu(4, r[4])
-        relu(5, r[5])
-        results(0, 256, (3, 3))
-        for j in range(2):
-            turn(hb[2 + j], 0, 256, j * P)
-        turned(0, 256, hi03[:, 512:])
-        for m in range(2):
-            keep_y(0, 256, (3, 3), m)
-        gather(0, 768, S, gZ0, ALL)
-        weave(256, gZ0, xZ0)
-        quantize_x(0, 768, 256, xZ0)
-        both((6, 7), [0])
-        quantize_h(256, 256, hi03[:, 512:])
-        results(256, 256, (4, 4))
-        for m in range(2):
-            keep_y(256, 256, (4, 4), m)
-        gather(1, 768, S, gZ1, (1, 2, 3, 0))
-        weave(256, gZ1, xZ1)
-        quantize_x(1, 768, 256, xZ1)
-        both((6,), [1])
-        gather(2, 768, 896, gZa, ALL)
-        weave(128, gZa, xZa)
-        quantize_x(2, 768, 128, xZa)
-        both((6,), [2])
-        both((7,), [1])
-        gather(2, 896, S, gZb, (1, 2, 3, 0))
-        weave(128, gZb, xZb)
-        quantize_x(2, 896, 128, xZb)
-        both((7,), [2])
-        relu(6, r[6])
-        for u in range(2):
-            relu(7, r[7], u, u + 1)
-        for u in range(2):
-            product(7, r[7], hb[7], u, u + 1)
-        turn(hb[7], 1, P, 0)
-        turned(1, P, hi7)
-        quantize_h(896, P, hi7)
-        second_layer(896, P, 0, bank[5][:, :P])
-        nc.scalar.copy(y[0][:, 896:], bank[5][:, :P])
-        product(6, r[6], hb[6])
-        turn(hb[6], 0, P, 0)
-        turned(0, P, hi6)
-        quantize_h(768, P, hi6)
-        for j in (4, 5):
-            product(j, r[j], hb[j])
-            turn(hb[j], 4, 256, (j % 2) * P)
-        turned(4, 256, hi45)
-        quantize_h(512, 256, hi45)
-        second_layer(512, 256, 0, bank[2][:, :256])
-        second_layer(768, P, 0, bank[2][:, 256:384])
-        nc.scalar.copy(y[0][:, 512:896], bank[2][:, :384])
-        second_layer(512, 256, 1, bank[6][:, :256])
-        second_layer(768, P, 1, bank[6][:, 256:384])
-        second_layer(896, P, 1, bank[6][:, 384:])
-        nc.scalar.copy(y[1][:, 512:], bank[6][:])
+            relu(j)
 
-        first = [room(16128 + 512 * m, 512) for m in range(2)]
-        total = [room(17152 + 512 * m, 512) for m in range(2)]
+        weave(0, e2, e3, B0)
+        for j in range(3):
+            product(j)
+        for j in (0, 1):
+            turn(j, 1, C, j * P)
+        quantize_x(0, e2, e3)
+        first_layer((4, 5), (0,))
+        gather(1, e2, e3, B1, up)
+        copy_turned(1, 0, C)
+        weave(1, e2, e3, B1)
+        quantize_x(1, e2, e3)
+        first_layer((4, 5), (1,))
+        gather(2, e2, e3, B2, wrap)
+        weave(2, e2, e3, B2)
+        quantize_h(0, C)
+        quantize_x(2, e2, e3)
+        product(3)
+        first_layer((4, 5), (2,))
+        relu(4)
+        relu(5)
         for m in range(2):
-            pieces = ((0, 384), (384, T))
+            second_layer(0, C, m, 3, m * C)
+        for j in (2, 3):
+            turn(j, 0, C, (j - 2) * P)
+        copy_turned(0, C, e2)
+        for m in range(2):
+            copy_y(0, C, m, 3, m * C)
+
+        gather(0, e3, S, Z0, up)
+        weave(0, e3, S, Z0)
+        quantize_x(0, e3, S)
+        first_layer((6, 7), (0,))
+        quantize_h(C, e2)
+        for m in range(2):
+            second_layer(C, e2, m, 4, m * C)
+        for m in range(2):
+            copy_y(C, e2, m, 4, m * C)
+        gather(1, e3, S, Z1, wrap)
+        weave(1, e3, S, Z1)
+        quantize_x(1, e3, S)
+        first_layer((6,), (1,))
+        gather(2, e3, t7, Z2A, up)
+        weave(2, e3, t7, Z2A)
+        quantize_x(2, e3, t7)
+        first_layer((6,), (2,))
+        first_layer((7,), (1,))
+        gather(2, t7, S, Z2B, wrap)
+        weave(2, t7, S, Z2B)
+        quantize_x(2, t7, S)
+        first_layer((7,), (2,))
+
+        relu(6)
+        for u in range(2):
+            relu(7, slice(u, u + 1))
+        for u in range(2):
+            product(7, slice(u, u + 1))
+        turn(7, 1, P, 0)
+        copy_turned(1, t7, S)
+        quantize_h(t7, S)
+        second_layer(t7, S, 0, 5, 0)
+        copy_y(t7, S, 0, 5, 0)
+        product(6)
+        turn(6, 0, P, 0)
+        copy_turned(0, e3, t7)
+        quantize_h(e3, t7)
+        for j, at in ((4, 0), (5, t5 - e2)):
+            product(j)
+            turn(j, 4, C, at)
+        copy_turned(4, e2, e3)
+        quantize_h(e2, e3)
+        second_layer(e2, e3, 0, 2, 0)
+        second_layer(e3, t7, 0, 2, e3 - e2)
+        copy_y(e2, t7, 0, 2, 0)
+        for lo, hi in ((e2, e3), (e3, t7), (t7, S)):
+            second_layer(lo, hi, 1, 6, lo - e2)
+        copy_y(e2, S, 1, 6, 0)
+
+        pieces = ((0, T - LAST), (T - LAST, T))
+        for m in range(N // P):
             for lo, hi in pieces:
-                nc.vector.tensor_copy(first[m][:, lo:hi], y[m][:].indirect(pos1_sb[:, lo // 16 : hi // 16]))
+                nc.vector.tensor_copy(first[:, m * T + lo : m * T + hi], y[m][:].indirect(pos1_sb[:, lo // 16 : hi // 16]))
             for lo, hi in pieces:
+                cols = slice(m * T + lo, m * T + hi)
                 nc.vector.tensor_tensor(
-                    total[m][:, lo:hi], y[m][:].indirect(pos2_sb[:, lo // 16 : hi // 16]), first[m][:, lo:hi], ADD
+                    total[:, cols], y[m][:].indirect(pos2_sb[:, lo // 16 : hi // 16]), first[:, cols], ADD
                 )
-                nc.sync.dma_start(out[m * P : (m + 1) * P, lo:hi], total[m][:, lo:hi])
+                nc.sync.dma_start(out[m * P : (m + 1) * P, lo:hi], total[:, cols])

@@ -27,18 +27,17 @@ RELU = mybir.ActivationFunctionType.Relu
 PAD = 32
 HEAD = 128
 LAST = 128
-AB = ((0, 1), (2, 3), (4, 5), (6, 7), (0, 2), (4, 6), (1, 3), (5, 7))
+AB = ((0, 1), (2, 3), (4, 5), (6, 7), (2, 4), (6, 1), (0, 3), (5, 2))
 
 CELL = 128
 A0, A1, A2 = (12, 4), (0, 4), (12, 4)
-B0, B1, B2 = (4, 2), (12, 2), (18, 4)
-Z0, Z1 = (14, 2), (20, 4)
-Z2A, Z2B = (14, 1), (17, 2)
-RELU0 = (18, 12)
-H2 = (20, 1)
-H3 = (24, 8)
-H4, H5 = (15, 1), (13, 1)
-STAGE_CELLS = 42
+C0 = (2, 4)
+B1, B2 = (25, 2), (16, 3)
+Z1 = (25, 2)
+Z2A, Z2B = (17, 2), (23, 1)
+RELU0, RELU1, RELU2 = (14, 2), (29, 2), (19, 3)
+H3, H4, H5 = (17, 1), (19, 1), (21, 1)
+STAGE_CELLS = 33
 
 
 def tile_moe_pre_glu_relu_kernel(
@@ -61,9 +60,10 @@ def tile_moe_pre_glu_relu_kernel(
         w3s = keep.tile([P, E * PASSES, H], U8, name="w3s", align_bytes=64)
         w2s = keep.tile([P, E, N], U8, name="w2s", align_bytes=64)
         xq = keep.tile([P, PASSES * S], U32, name="xq", align_bytes=64)
-        xs = keep.tile([P, PASSES * S], U8, name="xs", align_bytes=64)
+        planes = keep.tile([P, PASSES * S + S - P], U8, name="planes", align_bytes=64)
+        xs = planes[:, : PASSES * S]
         hq = keep.tile([P, S], U32, name="hq", align_bytes=64)
-        hs = keep.tile([P, S], U8, name="hs", align_bytes=64)
+        hs = planes[:, PASSES * S - P :]
         xb = keep.tile([P, PASSES * S * PACK], BF16, name="xb", align_bytes=64)
         hb = keep.tile([P, S * PACK], BF16, name="hb", align_bytes=64)
         y = [keep.tile([P, S], F32, name=f"y{m}") for m in range(N // P)]
@@ -81,10 +81,10 @@ def tile_moe_pre_glu_relu_kernel(
         def own_halves(name, width):
             return keep.tile([P, 2 * width], F32, name=name)[:].rearrange("p (u c) -> p u c", u=2)
 
-        relus = [rows(RELU0, 2, H // 2)]
-        relus.extend(own_halves(f"relu{j}", H // 2) for j in range(1, S // P))
-        pairs = [own_halves(f"pairs{j}", P) for j in (0, 1)]
-        pairs.extend(rows(place, 2, P) for place in (H2, H3, H4, H5))
+        relus = [rows(place, 2, H // 2) for place in (RELU0, RELU1, RELU2)]
+        relus.extend(own_halves(f"relu{j}", H // 2) for j in range(3, S // P))
+        pairs = [own_halves(f"pairs{j}", P) for j in (0, 1, 2)]
+        pairs.extend(rows(place, 2, P) for place in (H3, H4, H5))
         pairs.extend(own_halves(f"pairs{j}", P) for j in (6, 7))
 
         nc.vector.memset(w1s[:].bitcast(I32), 0)
@@ -215,8 +215,8 @@ def tile_moe_pre_glu_relu_kernel(
 
         up = range(PACK)
         down = (3, 2, 1, 0)
-        wrap = (1, 2, 3, 0)
-        e2, e3, t5, t7 = 2 * C, 3 * C, 5 * P, 7 * P
+        e1, e2, e3 = C, 2 * C, 3 * C
+        t3, t7 = 3 * P, 7 * P
 
         for s, place in ((0, A0), (1, A1)):
             gather(s, 0, e2, place, up)
@@ -229,59 +229,50 @@ def tile_moe_pre_glu_relu_kernel(
         weave(2, C, e2, A2, at=C)
         quantize_x(2, 0, C)
         first_layer((0, 1), (2,))
-        gather(0, e2, e3, B0, up)
+        gather(0, e2, S, C0, (0, 1, 2))
         quantize_x(2, C, e2)
         first_layer((2, 3), (2,))
         for j in range(4):
             relu(j)
-
-        weave(0, e2, e3, B0)
-        for j in range(3):
-            product(j)
+        gather(1, e2, e3, B1, (0, 1))
+        product(0)
+        product(1)
+        gather(0, e2, S, C0, (3,))
+        product(2)
         for j in (0, 1):
-            turn(j, 1, C, j * P)
-        quantize_x(0, e2, e3)
-        first_layer((4, 5), (0,))
-        gather(1, e2, e3, B1, up)
-        copy_turned(1, 0, C)
+            turn(j, 0, C, j * P)
+        copy_turned(0, 0, C)
+        weave(0, e2, S, C0)
+        gather(1, e2, e3, B1, (2, 3))
         weave(1, e2, e3, B1)
+        turn(2, 3, P, 0)
+        copy_turned(3, e1, t3)
+        gather(2, e2, e3, B2, (1, 2))
+        quantize_x(0, e2, S)
+        first_layer((4, 5), (0,))
+        gather(2, e2, e3, B2, (0,))
         quantize_x(1, e2, e3)
         first_layer((4, 5), (1,))
-        gather(2, e2, e3, B2, wrap)
+        gather(2, e2, e3, B2, (3,))
         weave(2, e2, e3, B2)
-        quantize_h(0, C)
+        gather(1, e3, S, Z1, (1, 2, 3))
         quantize_x(2, e2, e3)
-        product(3)
         first_layer((4, 5), (2,))
         relu(4)
-        relu(5)
-        for m in range(2):
-            second_layer(0, C, m, 3, m * C)
-        for j in (2, 3):
-            turn(j, 0, C, (j - 2) * P)
-        copy_turned(0, C, e2)
-        for m in range(2):
-            copy_y(0, C, m, 3, m * C)
-
-        gather(0, e3, S, Z0, up)
-        weave(0, e3, S, Z0)
-        quantize_x(0, e3, S)
         first_layer((6, 7), (0,))
-        quantize_h(C, e2)
-        for m in range(2):
-            second_layer(C, e2, m, 4, m * C)
-        for m in range(2):
-            copy_y(C, e2, m, 4, m * C)
-        gather(1, e3, S, Z1, wrap)
+        gather(1, e3, S, Z1, (0,))
         weave(1, e3, S, Z1)
-        quantize_x(1, e3, S)
-        first_layer((6,), (1,))
         gather(2, e3, t7, Z2A, up)
         weave(2, e3, t7, Z2A)
+        relu(5)
+        gather(2, t7, S, Z2B, (1,))
+        quantize_x(1, e3, S)
+        first_layer((6,), (1,))
+        gather(2, t7, S, Z2B, (2, 3))
         quantize_x(2, e3, t7)
         first_layer((6,), (2,))
         first_layer((7,), (1,))
-        gather(2, t7, S, Z2B, wrap)
+        gather(2, t7, S, Z2B, (0,))
         weave(2, t7, S, Z2B)
         quantize_x(2, t7, S)
         first_layer((7,), (2,))
@@ -289,28 +280,42 @@ def tile_moe_pre_glu_relu_kernel(
         relu(6)
         for u in range(2):
             relu(7, slice(u, u + 1))
+        for j in (3, 4, 5):
+            product(j)
         for u in range(2):
             product(7, slice(u, u + 1))
         turn(7, 1, P, 0)
         copy_turned(1, t7, S)
         quantize_h(t7, S)
-        second_layer(t7, S, 0, 5, 0)
-        copy_y(t7, S, 0, 5, 0)
         product(6)
-        turn(6, 0, P, 0)
-        copy_turned(0, e3, t7)
-        quantize_h(e3, t7)
-        for j, at in ((4, 0), (5, t5 - e2)):
-            product(j)
-            turn(j, 4, C, at)
-        copy_turned(4, e2, e3)
+        second_layer(t7, S, 0, 3, 0)
+        copy_y(t7, S, 0, 3, 0)
+        turn(3, 6, P, 0)
+        copy_turned(6, t3, e2)
+        for j in (4, 5):
+            turn(j, 7, C, (j - 4) * P)
+        copy_turned(7, e2, e3)
+        turn(6, 4, P, 0)
+        copy_turned(4, e3, t7)
+        quantize_h(e1, e2)
+        quantize_h(0, e1)
         quantize_h(e2, e3)
-        second_layer(e2, e3, 0, 2, 0)
-        second_layer(e3, t7, 0, 2, e3 - e2)
-        copy_y(e2, t7, 0, 2, 0)
-        for lo, hi in ((e2, e3), (e3, t7), (t7, S)):
-            second_layer(lo, hi, 1, 6, lo - e2)
-        copy_y(e2, S, 1, 6, 0)
+        quantize_h(e3, t7)
+        second_layer(e1, e2, 0, 0, 0)
+        copy_y(e1, e2, 0, 0, 0)
+        second_layer(0, e1, 0, 5, 0)
+        copy_y(0, e1, 0, 5, 0)
+        second_layer(e2, e3, 0, 6, 0)
+        second_layer(e3, t7, 0, 6, C)
+        copy_y(e2, t7, 0, 6, 0)
+        second_layer(e1, e2, 1, 3, 0)
+        second_layer(e2, e3, 1, 3, C)
+        copy_y(e1, e3, 1, 3, 0)
+        second_layer(e3, t7, 1, 2, 0)
+        second_layer(t7, S, 1, 2, P)
+        copy_y(e3, S, 1, 2, 0)
+        second_layer(0, e1, 1, 6, 0)
+        copy_y(0, e1, 1, 6, 0)
 
         pieces = ((0, T - LAST), (T - LAST, T))
         for m in range(N // P):

@@ -35,9 +35,10 @@ C0 = (2, 4)
 B1, B2 = (25, 2), (16, 3)
 Z1 = (25, 2)
 Z2A, Z2B = (17, 2), (23, 1)
-RELU0, RELU1, RELU2 = (14, 2), (29, 2), (19, 3)
+RELU0, RELU1 = (0, 18), (29, 2)
+H1 = (22, 1)
 H3, H4, H5 = (17, 1), (19, 1), (21, 1)
-STAGE_CELLS = 33
+STAGE_CELLS = 36
 
 
 def tile_moe_pre_glu_relu_kernel(
@@ -81,9 +82,12 @@ def tile_moe_pre_glu_relu_kernel(
         def own_halves(name, width):
             return keep.tile([P, 2 * width], F32, name=name)[:].rearrange("p (u c) -> p u c", u=2)
 
-        relus = [rows(place, 2, H // 2) for place in (RELU0, RELU1, RELU2)]
-        relus.extend(own_halves(f"relu{j}", H // 2) for j in range(3, S // P))
-        pairs = [own_halves(f"pairs{j}", P) for j in (0, 1, 2)]
+        relus = [rows(place, 2, H // 2) for place in (RELU0, RELU1)]
+        relus.extend(own_halves(f"relu{j}", H // 2) for j in range(2, S // P))
+        pairs = [own_halves("pairs0", P), rows(H1, 2, P), None]
+        b2 = own_halves("b2", H // 2)
+        last_x = (PASSES * S - P) * PACK
+        pairs2 = (gate_sb[:, S - P :], xb[:, last_x : last_x + 2 * P].bitcast(F32))
         pairs.extend(rows(place, 2, P) for place in (H3, H4, H5))
         pairs.extend(own_halves(f"pairs{j}", P) for j in (6, 7))
 
@@ -187,10 +191,10 @@ def tile_moe_pre_glu_relu_kernel(
         def turn(j, b, width, at):
             dst = bank[b][:, : 2 * width].rearrange("p (u j) -> p u j", u=2)
             for u in range(2):
-                nc.tensor.transpose(dst[:, u, at : at + P], pairs[j][:, u, :], ident[:])
+                nc.tensor.transpose(dst[:, u, at : at + P], pairs2[u] if j == 2 else pairs[j][:, u, :], ident[:])
 
-        def copy_turned(b, lo, hi):
-            nc.scalar.copy(
+        def copy_turned(b, lo, hi, copy=nc.scalar.copy):
+            copy(
                 hb[:, lo * PACK : hi * PACK].bitcast(F32).rearrange("p (j u) -> p j u", u=2),
                 bank[b][:, : 2 * (hi - lo)].rearrange("p (u j) -> p j u", u=2),
             )
@@ -210,8 +214,8 @@ def tile_moe_pre_glu_relu_kernel(
                 stop=True,
             )
 
-        def copy_y(lo, hi, m, b, at):
-            nc.scalar.copy(y[m][:, lo:hi], bank[b][:, at : at + hi - lo])
+        def copy_y(lo, hi, m, b, at, copy=nc.scalar.copy):
+            copy(y[m][:, lo:hi], bank[b][:, at : at + hi - lo])
 
         up = range(PACK)
         down = (3, 2, 1, 0)
@@ -234,19 +238,17 @@ def tile_moe_pre_glu_relu_kernel(
         first_layer((2, 3), (2,))
         for j in range(4):
             relu(j)
+        nc.scalar.copy(b2.rearrange("j u (p d) -> j u p d", d=2), by_half(AB[2][1]))
         gather(1, e2, e3, B1, (0, 1))
-        product(0)
-        product(1)
         gather(0, e2, S, C0, (3,))
-        product(2)
+        product(1)
+        product(0)
         for j in (0, 1):
             turn(j, 0, C, j * P)
-        copy_turned(0, 0, C)
         weave(0, e2, S, C0)
         gather(1, e2, e3, B1, (2, 3))
         weave(1, e2, e3, B1)
-        turn(2, 3, P, 0)
-        copy_turned(3, e1, t3)
+        copy_turned(0, 0, C)
         gather(2, e2, e3, B2, (1, 2))
         quantize_x(0, e2, S)
         first_layer((4, 5), (0,))
@@ -277,6 +279,8 @@ def tile_moe_pre_glu_relu_kernel(
         quantize_x(2, t7, S)
         first_layer((7,), (2,))
 
+        for u in range(2):
+            nc.gpsimd.tensor_tensor(pairs2[u].bitcast(BF16), b2[:, u], relus[2][:, u], MULT)
         relu(6)
         for u in range(2):
             relu(7, slice(u, u + 1))
@@ -295,27 +299,30 @@ def tile_moe_pre_glu_relu_kernel(
         for j in (4, 5):
             turn(j, 7, C, (j - 4) * P)
         copy_turned(7, e2, e3)
+        turn(2, 0, P, 0)
+        copy_turned(0, e1, t3, nc.vector.tensor_copy)
         turn(6, 4, P, 0)
         copy_turned(4, e3, t7)
-        quantize_h(e1, e2)
         quantize_h(0, e1)
         quantize_h(e2, e3)
+        quantize_h(e1, e2)
         quantize_h(e3, t7)
         second_layer(e1, e2, 0, 0, 0)
         copy_y(e1, e2, 0, 0, 0)
         second_layer(0, e1, 0, 5, 0)
         copy_y(0, e1, 0, 5, 0)
         second_layer(e2, e3, 0, 6, 0)
-        second_layer(e3, t7, 0, 6, C)
-        copy_y(e2, t7, 0, 6, 0)
+        copy_y(e2, e3, 0, 6, 0)
+        second_layer(e3, t7, 0, 4, 0)
+        copy_y(e3, t7, 0, 4, 0, nc.vector.tensor_copy)
         second_layer(e1, e2, 1, 3, 0)
         second_layer(e2, e3, 1, 3, C)
         copy_y(e1, e3, 1, 3, 0)
         second_layer(e3, t7, 1, 2, 0)
         second_layer(t7, S, 1, 2, P)
         copy_y(e3, S, 1, 2, 0)
-        second_layer(0, e1, 1, 6, 0)
-        copy_y(0, e1, 1, 6, 0)
+        second_layer(0, e1, 1, 4, 0)
+        copy_y(0, e1, 1, 4, 0)
 
         pieces = ((0, T - LAST), (T - LAST, T))
         for m in range(N // P):

@@ -26,19 +26,19 @@ RELU = mybir.ActivationFunctionType.Relu
 
 PAD = 32
 HEAD = 128
-LAST = 128
+LAST = 160
 AB = ((0, 1), (2, 3), (4, 5), (6, 7), (2, 4), (6, 1), (0, 3), (5, 2))
 
 CELL = 128
-A0, A1, A2 = (12, 4), (0, 4), (12, 4)
-C0 = (2, 4)
-B1, B2 = (25, 2), (16, 3)
-Z1 = (25, 2)
-Z2A, Z2B = (17, 2), (23, 1)
-RELU0, RELU1 = (0, 18), (29, 2)
-H1 = (22, 1)
-H3, H4, H5 = (17, 1), (19, 1), (21, 1)
-STAGE_CELLS = 36
+A0, A1, A2 = (13, 4), (1, 4), (13, 4)
+C0 = (3, 4)
+B1, B2 = (26, 2), (17, 3)
+Z1 = (26, 2)
+Z2A, Z2B = (18, 2), (24, 1)
+RELU0, RELU1 = (1, 18), (31, 5)
+H0 = (23, 1)
+H3, H4, H5 = (18, 1), (20, 1), (22, 1)
+STAGE_CELLS = 41
 
 
 def tile_moe_pre_glu_relu_kernel(
@@ -61,10 +61,9 @@ def tile_moe_pre_glu_relu_kernel(
         w3s = keep.tile([P, E * PASSES, H], U8, name="w3s", align_bytes=64)
         w2s = keep.tile([P, E, N], U8, name="w2s", align_bytes=64)
         xq = keep.tile([P, PASSES * S], U32, name="xq", align_bytes=64)
-        planes = keep.tile([P, PASSES * S + S - P], U8, name="planes", align_bytes=64)
-        xs = planes[:, : PASSES * S]
+        xs = keep.tile([P, PASSES * S], U8, name="xs", align_bytes=64)
         hq = keep.tile([P, S], U32, name="hq", align_bytes=64)
-        hs = planes[:, PASSES * S - P :]
+        hs = keep.tile([P, S], U8, name="hs", align_bytes=64)
         xb = keep.tile([P, PASSES * S * PACK], BF16, name="xb", align_bytes=64)
         hb = keep.tile([P, S * PACK], BF16, name="hb", align_bytes=64)
         y = [keep.tile([P, S], F32, name=f"y{m}") for m in range(N // P)]
@@ -84,12 +83,14 @@ def tile_moe_pre_glu_relu_kernel(
 
         relus = [rows(place, 2, H // 2) for place in (RELU0, RELU1)]
         relus.extend(own_halves(f"relu{j}", H // 2) for j in range(2, S // P))
-        pairs = [own_halves("pairs0", P), rows(H1, 2, P), None]
-        b2 = own_halves("b2", H // 2)
-        last_x = (PASSES * S - P) * PACK
-        pairs2 = (gate_sb[:, S - P :], xb[:, last_x : last_x + 2 * P].bitcast(F32))
+        pairs = [rows(H0, 2, P), own_halves("pairs1", P), own_halves("pairs2", P)]
         pairs.extend(rows(place, 2, P) for place in (H3, H4, H5))
         pairs.extend(own_halves(f"pairs{j}", P) for j in (6, 7))
+        words = [[pairs[j][:, u] for u in range(2)] for j in range(S // P)]
+        for j, slot in ((2, S - 2 * P), (1, S - P)):
+            at = ((PASSES - 1) * S + slot) * PACK
+            words[j][1] = xb[:, at : at + 2 * P].bitcast(F32)
+        b_sb = {key: keep.tile([P, H // 2], F32, name=f"b{key[0]}{key[1]}") for key in ((2, 0), (2, 1), (1, 1))}
 
         nc.vector.memset(w1s[:].bitcast(I32), 0)
         nc.vector.memset(w3s[:, : 2 * PASSES].bitcast(I32), 0)
@@ -188,10 +189,16 @@ def tile_moe_pre_glu_relu_kernel(
                 MULT,
             )
 
+        def copy_b(j, u):
+            nc.scalar.copy(b_sb[j, u][:].rearrange("j (p d) -> j p d", d=2), by_half(AB[j][1])[:, u])
+
+        def product_gpsimd(j, u):
+            nc.gpsimd.tensor_tensor(words[j][u].bitcast(BF16), b_sb[j, u][:], relus[j][:, u], MULT)
+
         def turn(j, b, width, at):
             dst = bank[b][:, : 2 * width].rearrange("p (u j) -> p u j", u=2)
             for u in range(2):
-                nc.tensor.transpose(dst[:, u, at : at + P], pairs2[u] if j == 2 else pairs[j][:, u, :], ident[:])
+                nc.tensor.transpose(dst[:, u, at : at + P], words[j][u], ident[:])
 
         def copy_turned(b, lo, hi, copy=nc.scalar.copy):
             copy(
@@ -220,7 +227,7 @@ def tile_moe_pre_glu_relu_kernel(
         up = range(PACK)
         down = (3, 2, 1, 0)
         e1, e2, e3 = C, 2 * C, 3 * C
-        t3, t7 = 3 * P, 7 * P
+        t7 = 7 * P
 
         for s, place in ((0, A0), (1, A1)):
             gather(s, 0, e2, place, up)
@@ -236,19 +243,22 @@ def tile_moe_pre_glu_relu_kernel(
         gather(0, e2, S, C0, (0, 1, 2))
         quantize_x(2, C, e2)
         first_layer((2, 3), (2,))
-        for j in range(4):
+        for j in range(3):
             relu(j)
-        nc.scalar.copy(b2.rearrange("j u (p d) -> j u p d", d=2), by_half(AB[2][1]))
+        copy_b(2, 0)
+        relu(3)
         gather(1, e2, e3, B1, (0, 1))
         gather(0, e2, S, C0, (3,))
-        product(1)
+        product_gpsimd(2, 0)
+        product(1, slice(0, 1))
         product(0)
-        for j in (0, 1):
-            turn(j, 0, C, j * P)
+        turn(0, 0, P, 0)
         weave(0, e2, S, C0)
         gather(1, e2, e3, B1, (2, 3))
         weave(1, e2, e3, B1)
-        copy_turned(0, 0, C)
+        copy_turned(0, 0, P)
+        copy_b(2, 1)
+        copy_b(1, 1)
         gather(2, e2, e3, B2, (1, 2))
         quantize_x(0, e2, S)
         first_layer((4, 5), (0,))
@@ -276,53 +286,52 @@ def tile_moe_pre_glu_relu_kernel(
         first_layer((7,), (1,))
         gather(2, t7, S, Z2B, (0,))
         weave(2, t7, S, Z2B)
-        quantize_x(2, t7, S)
-        first_layer((7,), (2,))
 
-        for u in range(2):
-            nc.gpsimd.tensor_tensor(pairs2[u].bitcast(BF16), b2[:, u], relus[2][:, u], MULT)
+        product_gpsimd(2, 1)
+        product(3)
+        product(4)
+        quantize_x(2, t7, S)
+        product_gpsimd(1, 1)
         relu(6)
+        for j in (2, 3):
+            turn(j, 6, C, (j - 2) * P)
+        copy_turned(6, e1, e2)
+        turn(4, 7, C, 0)
+        first_layer((7,), (2,))
         for u in range(2):
             relu(7, slice(u, u + 1))
-        for j in (3, 4, 5):
-            product(j)
+        product(5)
+        product(6)
+        quantize_h(e1, e2)
         for u in range(2):
             product(7, slice(u, u + 1))
-        turn(7, 1, P, 0)
-        copy_turned(1, t7, S)
-        quantize_h(t7, S)
-        product(6)
-        second_layer(t7, S, 0, 3, 0)
-        copy_y(t7, S, 0, 3, 0)
-        turn(3, 6, P, 0)
-        copy_turned(6, t3, e2)
-        for j in (4, 5):
-            turn(j, 7, C, (j - 4) * P)
+        turn(5, 7, C, P)
         copy_turned(7, e2, e3)
-        turn(2, 0, P, 0)
-        copy_turned(0, e1, t3, nc.vector.tensor_copy)
+        turn(1, 1, P, 0)
+        copy_turned(1, P, e1)
         turn(6, 4, P, 0)
         copy_turned(4, e3, t7)
-        quantize_h(0, e1)
+        turn(7, 0, P, 0)
+        copy_turned(0, t7, S)
         quantize_h(e2, e3)
-        quantize_h(e1, e2)
+        quantize_h(0, e1)
         quantize_h(e3, t7)
-        second_layer(e1, e2, 0, 0, 0)
-        copy_y(e1, e2, 0, 0, 0)
-        second_layer(0, e1, 0, 5, 0)
-        copy_y(0, e1, 0, 5, 0)
-        second_layer(e2, e3, 0, 6, 0)
-        copy_y(e2, e3, 0, 6, 0)
+        quantize_h(t7, S)
+        for lo, hi, b in ((e1, e2, 2), (e2, e3, 7), (0, e1, 5)):
+            second_layer(lo, hi, 0, b, 0)
+            copy_y(lo, hi, 0, b, 0)
         second_layer(e3, t7, 0, 4, 0)
         copy_y(e3, t7, 0, 4, 0, nc.vector.tensor_copy)
+        second_layer(t7, S, 0, 3, 0)
+        copy_y(t7, S, 0, 3, 0)
+        second_layer(e3, t7, 1, 5, 0)
+        second_layer(t7, S, 1, 5, P)
+        copy_y(e3, S, 1, 5, 0)
+        second_layer(0, e1, 1, 4, 0)
+        copy_y(0, e1, 1, 4, 0)
         second_layer(e1, e2, 1, 3, 0)
         second_layer(e2, e3, 1, 3, C)
         copy_y(e1, e3, 1, 3, 0)
-        second_layer(e3, t7, 1, 2, 0)
-        second_layer(t7, S, 1, 2, P)
-        copy_y(e3, S, 1, 2, 0)
-        second_layer(0, e1, 1, 4, 0)
-        copy_y(0, e1, 1, 4, 0)
 
         pieces = ((0, T - LAST), (T - LAST, T))
         for m in range(N // P):

@@ -34,10 +34,10 @@ A0, A1, A2 = (13, 4), (1, 4), (13, 4)
 C0 = (3, 4)
 B1, B2 = (26, 2), (17, 3)
 Z1 = (26, 2)
-Z2A, Z2B = (18, 2), (24, 1)
+Z2A, Z2B = (17, 2), (23.5, 1)
 RELU0, RELU1 = (1, 18), (31, 5)
 H0 = (23, 1)
-H3, H4, H5 = (18, 1), (20, 1), (22, 1)
+H3, H4, H5 = (17, 1), (19, 5), (25, 1)
 STAGE_CELLS = 41
 
 
@@ -75,7 +75,7 @@ def tile_moe_pre_glu_relu_kernel(
 
         def rows(place, count, width):
             cell, step = place
-            span = stage[:, cell * CELL : (cell + count * step) * CELL]
+            span = stage[:, int(cell * CELL) : int((cell + count * step) * CELL)]
             return span.rearrange("p (r c) -> p r c", r=count)[:, :, :width]
 
         def own_halves(name, width):
@@ -137,10 +137,10 @@ def tile_moe_pre_glu_relu_kernel(
         nc.sync.dma_start(pos1_sb[:], pos1)
         nc.sync.dma_start(pos2_sb[:], pos2)
 
-        def gather(s, lo, hi, place, ts):
+        def gather(s, lo, hi, place, ts, pieces=None):
             dst = rows(place, PACK, hi - lo)
             for t in ts:
-                for a, b in ((0, HEAD), (HEAD, hi)) if (s, t, lo) == (0, 0, 0) else ((lo, hi),):
+                for a, b in pieces or (((0, HEAD), (HEAD, hi)) if (s, t, lo) == (0, 0, 0) else ((lo, hi),)):
                     nc.vector.tensor_tensor(
                         dst[:, t, a - lo : b - lo],
                         windows[s][t][:].indirect(offs_sb[:, a // 16 : b // 16]),
@@ -273,38 +273,44 @@ def tile_moe_pre_glu_relu_kernel(
         relu(4)
         first_layer((6, 7), (0,))
         gather(1, e3, S, Z1, (0,))
-        weave(1, e3, S, Z1)
+        weave(1, e3, t7, Z1)
+        weave(1, t7, S, Z1, at=P)
         gather(2, e3, t7, Z2A, up)
         weave(2, e3, t7, Z2A)
         relu(5)
-        gather(2, t7, S, Z2B, (1,))
-        quantize_x(1, e3, S)
+        quantize_x(1, e3, t7)
         first_layer((6,), (1,))
-        gather(2, t7, S, Z2B, (2, 3))
+        mid = t7 + P // 2
+        gather(2, t7, S, Z2B, (0,), ((mid, S),))
+        gather(2, t7, S, Z2B, (1, 2))
+        quantize_x(1, t7, S)
+        first_layer((7,), (1,))
+        gather(2, t7, S, Z2B, (3,))
+        weave(2, mid, S, Z2B, at=P // 2)
         quantize_x(2, e3, t7)
         first_layer((6,), (2,))
-        first_layer((7,), (1,))
-        gather(2, t7, S, Z2B, (0,))
-        weave(2, t7, S, Z2B)
+        gather(2, t7, S, Z2B, (0,), ((t7, mid),))
+        weave(2, t7, mid, Z2B)
 
         product_gpsimd(2, 1)
         product(3)
-        product(4)
+        product(4, slice(0, 1))
         quantize_x(2, t7, S)
+        product(4, slice(1, 2))
         product_gpsimd(1, 1)
         relu(6)
         for j in (2, 3):
             turn(j, 6, C, (j - 2) * P)
         copy_turned(6, e1, e2)
-        turn(4, 7, C, 0)
         first_layer((7,), (2,))
+        turn(4, 7, C, 0)
         for u in range(2):
             relu(7, slice(u, u + 1))
         product(5)
         product(6)
-        quantize_h(e1, e2)
         for u in range(2):
             product(7, slice(u, u + 1))
+        quantize_h(e1, e2)
         turn(5, 7, C, P)
         copy_turned(7, e2, e3)
         turn(1, 1, P, 0)

@@ -27,17 +27,17 @@ RELU = mybir.ActivationFunctionType.Relu
 PAD = 32
 HEAD = 128
 LAST = 160
-AB = ((0, 1), (2, 3), (4, 5), (6, 7), (2, 4), (6, 1), (0, 3), (5, 2))
+AB = ((0, 1), (2, 3), (4, 5), (6, 7), (2, 4), (6, 1), (0, 3), (5, 6))
 
 CELL = 128
 A0, A1, A2 = (13, 4), (1, 4), (13, 4)
 C0 = (3, 4)
 B1, B2 = (26, 2), (17, 3)
-Z1 = (26, 2)
-Z2A, Z2B = (17, 2), (23.5, 1)
+Z1 = (25, 2)
+Z2A, Z2B = (18.5, 1.5), (23.5, 1)
 RELU0, RELU1 = (1, 18), (31, 5)
 H0 = (23, 1)
-H3, H4, H5 = (17, 1), (19, 5), (25, 1)
+H3, H4, H5 = (19, 1), (21, 3), (25, 1)
 STAGE_CELLS = 41
 
 
@@ -85,7 +85,10 @@ def tile_moe_pre_glu_relu_kernel(
         relus.extend(own_halves(f"relu{j}", H // 2) for j in range(2, S // P))
         pairs = [rows(H0, 2, P), own_halves("pairs1", P), own_halves("pairs2", P)]
         pairs.extend(rows(place, 2, P) for place in (H3, H4, H5))
-        pairs.extend(own_halves(f"pairs{j}", P) for j in (6, 7))
+        pairs6 = keep.tile([P, 2 * P], F32, name="pairs6", tag="held", align_bytes=64)
+        pairs.append(pairs6[:].rearrange("p (u c) -> p u c", u=2))
+        h_planes = {lo: hs[:, lo:hi] for lo, hi in ((0, C), (2 * C, 3 * C), (3 * C, S - P), (S - P, S))}
+        pairs.append(own_halves("pairs7", P))
         words = [[pairs[j][:, u] for u in range(2)] for j in range(S // P)]
         for j, slot in ((2, S - 2 * P), (1, S - P)):
             at = ((PASSES - 1) * S + slot) * PACK
@@ -207,7 +210,7 @@ def tile_moe_pre_glu_relu_kernel(
             )
 
         def quantize_h(lo, hi):
-            nc.vector.quantize_mx(out=hq[:, lo:hi].bitcast(FP8X4), scales=hs[:, lo:hi], in_=hb[:, lo * PACK : hi * PACK])
+            nc.vector.quantize_mx(out=hq[:, lo:hi].bitcast(FP8X4), scales=h_planes[lo], in_=hb[:, lo * PACK : hi * PACK])
 
         def second_layer(lo, hi, m, b, at):
             e = lo // C
@@ -216,7 +219,7 @@ def tile_moe_pre_glu_relu_kernel(
                 lhsT=w2c[:, e, 2 * m * P : 2 * (m + 1) * P].bitcast(FP4X4),
                 lhsT_scale=w2s[:, e, m * P : (m + 1) * P],
                 rhs=hq[:, lo:hi].bitcast(FP8X4),
-                rhs_scale=hs[:, lo:hi],
+                rhs_scale=h_planes[lo],
                 start=True,
                 stop=True,
             )
@@ -227,7 +230,7 @@ def tile_moe_pre_glu_relu_kernel(
         up = range(PACK)
         down = (3, 2, 1, 0)
         e1, e2, e3 = C, 2 * C, 3 * C
-        t7 = 7 * P
+        t5, t7 = 5 * P, 7 * P
 
         for s, place in ((0, A0), (1, A1)):
             gather(s, 0, e2, place, up)
@@ -261,31 +264,36 @@ def tile_moe_pre_glu_relu_kernel(
         copy_b(1, 1)
         gather(2, e2, e3, B2, (1, 2))
         quantize_x(0, e2, S)
-        first_layer((4, 5), (0,))
+        first_layer((5,), (0,))
+        first_layer((4,), (0,))
         gather(2, e2, e3, B2, (0,))
         quantize_x(1, e2, e3)
-        first_layer((4, 5), (1,))
+        first_layer((5,), (1,))
         gather(2, e2, e3, B2, (3,))
-        weave(2, e2, e3, B2)
-        gather(1, e3, S, Z1, (1, 2, 3))
-        quantize_x(2, e2, e3)
-        first_layer((4, 5), (2,))
-        relu(4)
+        weave(2, t5, e3, B2, at=P)
+        weave(2, e2, t5, B2)
+        gather(1, e3, S, Z1, (2, 3))
+        quantize_x(2, t5, e3)
+        first_layer((5,), (2,))
+        relu(5)
+        gather(1, e3, S, Z1, (1,))
+        quantize_x(2, e2, t5)
+        first_layer((4,), (1, 2))
         first_layer((6, 7), (0,))
         gather(1, e3, S, Z1, (0,))
         weave(1, e3, t7, Z1)
         weave(1, t7, S, Z1, at=P)
         gather(2, e3, t7, Z2A, up)
         weave(2, e3, t7, Z2A)
-        relu(5)
-        quantize_x(1, e3, t7)
-        first_layer((6,), (1,))
+        relu(4)
         mid = t7 + P // 2
         gather(2, t7, S, Z2B, (0,), ((mid, S),))
-        gather(2, t7, S, Z2B, (1, 2))
+        quantize_x(1, e3, t7)
+        first_layer((6,), (1,))
+        gather(2, t7, S, Z2B, (1,))
         quantize_x(1, t7, S)
         first_layer((7,), (1,))
-        gather(2, t7, S, Z2B, (3,))
+        gather(2, t7, S, Z2B, (2, 3))
         weave(2, mid, S, Z2B, at=P // 2)
         quantize_x(2, e3, t7)
         first_layer((6,), (2,))
@@ -300,8 +308,8 @@ def tile_moe_pre_glu_relu_kernel(
         product_gpsimd(1, 1)
         relu(6)
         for j in (2, 3):
-            turn(j, 6, C, (j - 2) * P)
-        copy_turned(6, e1, e2)
+            turn(j, 2, C, (j - 2) * P)
+        copy_turned(2, e1, e2)
         first_layer((7,), (2,))
         turn(4, 7, C, 0)
         for u in range(2):
@@ -310,20 +318,21 @@ def tile_moe_pre_glu_relu_kernel(
         product(6)
         for u in range(2):
             product(7, slice(u, u + 1))
-        quantize_h(e1, e2)
         turn(5, 7, C, P)
         copy_turned(7, e2, e3)
         turn(1, 1, P, 0)
         copy_turned(1, P, e1)
         turn(6, 4, P, 0)
         copy_turned(4, e3, t7)
+        h_planes[e1] = keep.tile([P, C], U8, name="hs1", tag="held", align_bytes=64)[:]
+        quantize_h(e1, e2)
         turn(7, 0, P, 0)
         copy_turned(0, t7, S)
         quantize_h(e2, e3)
         quantize_h(0, e1)
         quantize_h(e3, t7)
         quantize_h(t7, S)
-        for lo, hi, b in ((e1, e2, 2), (e2, e3, 7), (0, e1, 5)):
+        for lo, hi, b in ((e1, e2, 6), (e2, e3, 7), (0, e1, 5)):
             second_layer(lo, hi, 0, b, 0)
             copy_y(lo, hi, 0, b, 0)
         second_layer(e3, t7, 0, 4, 0)

@@ -24,21 +24,28 @@ MULT = mybir.AluOpType.mult
 ADD = mybir.AluOpType.add
 RELU = mybir.ActivationFunctionType.Relu
 
+LOW, HIGH, BOTH = slice(0, 1), slice(1, 2), slice(0, 2)
+
 PAD = 32
 HEAD = 128
 LAST = 160
 AB = ((0, 1), (2, 3), (4, 5), (6, 7), (2, 4), (6, 1), (0, 3), (5, 6))
 
-CELL = 128
-A0, A1, A2 = (13, 4), (1, 4), (13, 4)
-C0 = (3, 4)
-B1, B2 = (26, 2), (17, 3)
-Z1 = (25, 2)
-Z2A, Z2B = (18.5, 1.5), (23.5, 1)
-RELU0, RELU1 = (1, 18), (31, 5)
-H0 = (23, 1)
-H3, H4, H5 = (19, 1), (21, 3), (25, 1)
-STAGE_CELLS = 41
+CELL = 64
+X01_0, X01_1, X01_2 = (26, 8), (2, 8), (26, 8)
+X23_0 = (6, 8)
+X2_1 = (52, 4)
+X2_2 = (34, 6)
+X3_1 = (50, 4)
+X6_2 = (37, 3)
+X7_2 = (47, 2)
+RELU0 = (2, 36)
+RELU1 = (62, 10)
+H0 = (46, 2)
+H3 = (38, 2)
+H4 = (42, 6)
+H5 = (50, 2)
+STAGE_CELLS = 82
 
 
 def tile_moe_pre_glu_relu_kernel(
@@ -75,7 +82,7 @@ def tile_moe_pre_glu_relu_kernel(
 
         def rows(place, count, width):
             cell, step = place
-            span = stage[:, int(cell * CELL) : int((cell + count * step) * CELL)]
+            span = stage[:, cell * CELL : (cell + count * step) * CELL]
             return span.rearrange("p (r c) -> p r c", r=count)[:, :, :width]
 
         def own_halves(name, width):
@@ -83,17 +90,17 @@ def tile_moe_pre_glu_relu_kernel(
 
         relus = [rows(place, 2, H // 2) for place in (RELU0, RELU1)]
         relus.extend(own_halves(f"relu{j}", H // 2) for j in range(2, S // P))
-        pairs = [rows(H0, 2, P), own_halves("pairs1", P), own_halves("pairs2", P)]
-        pairs.extend(rows(place, 2, P) for place in (H3, H4, H5))
-        pairs6 = keep.tile([P, 2 * P], F32, name="pairs6", tag="held", align_bytes=64)
-        pairs.append(pairs6[:].rearrange("p (u c) -> p u c", u=2))
-        h_planes = {lo: hs[:, lo:hi] for lo, hi in ((0, C), (2 * C, 3 * C), (3 * C, S - P), (S - P, S))}
-        pairs.append(own_halves("pairs7", P))
-        words = [[pairs[j][:, u] for u in range(2)] for j in range(S // P)]
-        for j, slot in ((2, S - 2 * P), (1, S - P)):
-            at = ((PASSES - 1) * S + slot) * PACK
-            words[j][1] = xb[:, at : at + 2 * P].bitcast(F32)
-        b_sb = {key: keep.tile([P, H // 2], F32, name=f"b{key[0]}{key[1]}") for key in ((2, 0), (2, 1), (1, 1))}
+        pairs = {0: rows(H0, 2, P), 1: own_halves("pairs1", P)}
+        pairs[3], pairs[4], pairs[5] = [rows(place, 2, P) for place in (H3, H4, H5)]
+        words6 = keep.tile([P, 2 * P], F32, name="pairs6", tag="held", align_bytes=64)
+        pairs[6] = words6[:].rearrange("p (u c) -> p u c", u=2)
+        pairs[7] = own_halves("pairs7", P)
+        halves = {(j, u): pairs[j][:, u] for j in pairs for u in range(2)}
+        for u in range(2):
+            at = ((PASSES - 1) * S + (6 + u) * P) * PACK
+            halves[2, u] = xb[:, at : at + 2 * P].bitcast(F32)
+        b_sb = {(j, u): keep.tile([P, H // 2], F32, name=f"b{j}{u}") for j, u in ((1, 1), (2, 0), (2, 1))}
+        h_planes = {lo: hs[:, lo:hi] for lo, hi in ((C, 2 * C), (2 * C, 3 * C), (3 * C, S - P), (S - P, S))}
 
         nc.vector.memset(w1s[:].bitcast(I32), 0)
         nc.vector.memset(w3s[:, : 2 * PASSES].bitcast(I32), 0)
@@ -140,16 +147,15 @@ def tile_moe_pre_glu_relu_kernel(
         nc.sync.dma_start(pos1_sb[:], pos1)
         nc.sync.dma_start(pos2_sb[:], pos2)
 
-        def gather(s, lo, hi, place, ts, pieces=None):
-            dst = rows(place, PACK, hi - lo)
+        def gather(s, lo, hi, place, ts, part=None):
+            a, b = part or (lo, hi)
             for t in ts:
-                for a, b in pieces or (((0, HEAD), (HEAD, hi)) if (s, t, lo) == (0, 0, 0) else ((lo, hi),)):
-                    nc.vector.tensor_tensor(
-                        dst[:, t, a - lo : b - lo],
-                        windows[s][t][:].indirect(offs_sb[:, a // 16 : b // 16]),
-                        gate_sb[:, a:b],
-                        MULT,
-                    )
+                nc.vector.tensor_tensor(
+                    rows(place, PACK, hi - lo)[:, t, a - lo : b - lo],
+                    windows[s][t][:].indirect(offs_sb[:, a // 16 : b // 16]),
+                    gate_sb[:, a:b],
+                    MULT,
+                )
 
         def weave(s, lo, hi, place, at=0):
             src = rows(place, PACK, at + hi - lo)[:, :, at:]
@@ -181,10 +187,10 @@ def tile_moe_pre_glu_relu_kernel(
         def by_half(b):
             return bank[b][:].rearrange("j (p u d) -> j u p d", u=2, d=2)
 
-        def relu(j, us=slice(0, 2)):
+        def relu(j, us=BOTH):
             nc.scalar.activation(relus[j].rearrange("j u (p d) -> j u p d", d=2)[:, us], by_half(AB[j][0])[:, us], RELU)
 
-        def product(j, us=slice(0, 2)):
+        def product(j, us=BOTH):
             nc.vector.tensor_tensor(
                 pairs[j].bitcast(BF16).rearrange("j u (p d) -> j u p d", d=2)[:, us],
                 by_half(AB[j][1])[:, us],
@@ -196,15 +202,15 @@ def tile_moe_pre_glu_relu_kernel(
             nc.scalar.copy(b_sb[j, u][:].rearrange("j (p d) -> j p d", d=2), by_half(AB[j][1])[:, u])
 
         def product_gpsimd(j, u):
-            nc.gpsimd.tensor_tensor(words[j][u].bitcast(BF16), b_sb[j, u][:], relus[j][:, u], MULT)
+            nc.gpsimd.tensor_tensor(halves[j, u].bitcast(BF16), b_sb[j, u][:], relus[j][:, u], MULT)
 
         def turn(j, b, width, at):
             dst = bank[b][:, : 2 * width].rearrange("p (u j) -> p u j", u=2)
             for u in range(2):
-                nc.tensor.transpose(dst[:, u, at : at + P], words[j][u], ident[:])
+                nc.tensor.transpose(dst[:, u, at : at + P], halves[j, u], ident[:])
 
-        def copy_turned(b, lo, hi, copy=nc.scalar.copy):
-            copy(
+        def copy_turned(b, lo, hi):
+            nc.scalar.copy(
                 hb[:, lo * PACK : hi * PACK].bitcast(F32).rearrange("p (j u) -> p j u", u=2),
                 bank[b][:, : 2 * (hi - lo)].rearrange("p (u j) -> p j u", u=2),
             )
@@ -227,112 +233,120 @@ def tile_moe_pre_glu_relu_kernel(
         def copy_y(lo, hi, m, b, at, copy=nc.scalar.copy):
             copy(y[m][:, lo:hi], bank[b][:, at : at + hi - lo])
 
-        up = range(PACK)
-        down = (3, 2, 1, 0)
         e1, e2, e3 = C, 2 * C, 3 * C
-        t5, t7 = 5 * P, 7 * P
+        t3, t5, t7 = 3 * P, 5 * P, 7 * P
+        mid7 = t7 + P // 2
 
-        for s, place in ((0, A0), (1, A1)):
-            gather(s, 0, e2, place, up)
-            weave(s, 0, e2, place)
-            quantize_x(s, 0, e2)
+        gather(0, 0, e2, X01_0, (0,), (0, HEAD))
+        gather(0, 0, e2, X01_0, (0,), (HEAD, e2))
+        gather(0, 0, e2, X01_0, (1, 2, 3))
+        weave(0, 0, e2, X01_0)
+        quantize_x(0, 0, e2)
+        gather(1, 0, e2, X01_1, range(PACK))
+        weave(1, 0, e2, X01_1)
+        quantize_x(1, 0, e2)
         first_layer((0, 1), (0, 1))
         first_layer((2, 3), (0, 1))
-        gather(2, 0, e2, A2, down)
-        weave(2, 0, C, A2)
-        weave(2, C, e2, A2, at=C)
-        quantize_x(2, 0, C)
+        gather(2, 0, e2, X01_2, (3, 2, 1, 0))
+        weave(2, 0, e1, X01_2)
+        weave(2, e1, e2, X01_2, at=C)
+        quantize_x(2, 0, e1)
         first_layer((0, 1), (2,))
-        gather(0, e2, S, C0, (0, 1, 2))
-        quantize_x(2, C, e2)
+        gather(0, e2, S, X23_0, (0, 1, 2))
+        quantize_x(2, e1, e2)
         first_layer((2, 3), (2,))
-        for j in range(3):
-            relu(j)
-        copy_b(2, 0)
-        relu(3)
-        gather(1, e2, e3, B1, (0, 1))
-        gather(0, e2, S, C0, (3,))
-        product_gpsimd(2, 0)
-        product(1, slice(0, 1))
-        product(0)
-        turn(0, 0, P, 0)
-        weave(0, e2, S, C0)
-        gather(1, e2, e3, B1, (2, 3))
-        weave(1, e2, e3, B1)
-        copy_turned(0, 0, P)
-        copy_b(2, 1)
+
+        relu(0)
+        relu(1)
         copy_b(1, 1)
-        gather(2, e2, e3, B2, (1, 2))
+        relu(2)
+        relu(3)
+        gather(1, e2, e3, X2_1, (0, 1))
+        gather(0, e2, S, X23_0, (3,))
+        product_gpsimd(1, 1)
+        product(0, LOW)
+        product(0, HIGH)
+        product(1, LOW)
+        for j in (0, 1):
+            turn(j, 0, C, j * P)
+        weave(0, e2, S, X23_0)
+
+        gather(2, e2, e3, X2_2, (1,))
+        gather(1, e2, e3, X2_1, (2, 3))
+        weave(1, e2, e3, X2_1)
+        copy_turned(0, 0, e1)
+        copy_b(2, 0)
+        copy_b(2, 1)
+        gather(2, e2, e3, X2_2, (2,))
         quantize_x(0, e2, S)
         first_layer((5,), (0,))
         first_layer((4,), (0,))
-        gather(2, e2, e3, B2, (0,))
+        gather(2, e2, e3, X2_2, (0,))
         quantize_x(1, e2, e3)
         first_layer((5,), (1,))
-        gather(2, e2, e3, B2, (3,))
-        weave(2, t5, e3, B2, at=P)
-        weave(2, e2, t5, B2)
-        gather(1, e3, S, Z1, (2, 3))
+        gather(2, e2, e3, X2_2, (3,))
+        weave(2, t5, e3, X2_2, at=P)
+        weave(2, e2, t5, X2_2)
+        gather(1, e3, S, X3_1, (2, 3))
         quantize_x(2, t5, e3)
         first_layer((5,), (2,))
         relu(5)
-        gather(1, e3, S, Z1, (1,))
+        gather(1, e3, S, X3_1, (1,))
         quantize_x(2, e2, t5)
         first_layer((4,), (1, 2))
+
         first_layer((6, 7), (0,))
-        gather(1, e3, S, Z1, (0,))
-        weave(1, e3, t7, Z1)
-        weave(1, t7, S, Z1, at=P)
-        gather(2, e3, t7, Z2A, up)
-        weave(2, e3, t7, Z2A)
+        gather(1, e3, S, X3_1, (0,))
+        weave(1, e3, t7, X3_1)
+        weave(1, t7, S, X3_1, at=P)
+        gather(2, e3, t7, X6_2, range(PACK))
+        weave(2, e3, t7, X6_2)
         relu(4)
-        mid = t7 + P // 2
-        gather(2, t7, S, Z2B, (0,), ((mid, S),))
+        gather(2, t7, S, X7_2, (0,), (mid7, S))
         quantize_x(1, e3, t7)
         first_layer((6,), (1,))
-        gather(2, t7, S, Z2B, (1,))
+        gather(2, t7, S, X7_2, (1,))
         quantize_x(1, t7, S)
         first_layer((7,), (1,))
-        gather(2, t7, S, Z2B, (2, 3))
-        weave(2, mid, S, Z2B, at=P // 2)
+        gather(2, t7, S, X7_2, (2, 3))
+        weave(2, mid7, S, X7_2, at=P // 2)
         quantize_x(2, e3, t7)
         first_layer((6,), (2,))
-        gather(2, t7, S, Z2B, (0,), ((t7, mid),))
-        weave(2, t7, mid, Z2B)
+        gather(2, t7, S, X7_2, (0,), (t7, mid7))
+        weave(2, t7, mid7, X7_2)
 
-        product_gpsimd(2, 1)
+        product_gpsimd(2, 0)
         product(3)
-        product(4, slice(0, 1))
+        product(4, LOW)
         quantize_x(2, t7, S)
-        product(4, slice(1, 2))
-        product_gpsimd(1, 1)
+        product(4, HIGH)
+        product_gpsimd(2, 1)
         relu(6)
-        for j in (2, 3):
-            turn(j, 2, C, (j - 2) * P)
-        copy_turned(2, e1, e2)
+        turn(3, 2, P, 0)
+        copy_turned(2, t3, e2)
         first_layer((7,), (2,))
         turn(4, 7, C, 0)
-        for u in range(2):
-            relu(7, slice(u, u + 1))
+        relu(7, LOW)
+        relu(7, HIGH)
         product(5)
         product(6)
-        for u in range(2):
-            product(7, slice(u, u + 1))
+        product(7, LOW)
+        product(7, HIGH)
         turn(5, 7, C, P)
         copy_turned(7, e2, e3)
-        turn(1, 1, P, 0)
-        copy_turned(1, P, e1)
+        turn(2, 1, P, 0)
+        copy_turned(1, e1, t3)
         turn(6, 4, P, 0)
         copy_turned(4, e3, t7)
-        h_planes[e1] = keep.tile([P, C], U8, name="hs1", tag="held", align_bytes=64)[:]
-        quantize_h(e1, e2)
+        h_planes[0] = keep.tile([P, C], U8, name="hs0", tag="held", align_bytes=64)[:]
+        quantize_h(0, e1)
         turn(7, 0, P, 0)
         copy_turned(0, t7, S)
         quantize_h(e2, e3)
-        quantize_h(0, e1)
+        quantize_h(e1, e2)
         quantize_h(e3, t7)
         quantize_h(t7, S)
-        for lo, hi, b in ((e1, e2, 6), (e2, e3, 7), (0, e1, 5)):
+        for lo, hi, b in ((0, e1, 6), (e2, e3, 7), (e1, e2, 5)):
             second_layer(lo, hi, 0, b, 0)
             copy_y(lo, hi, 0, b, 0)
         second_layer(e3, t7, 0, 4, 0)

@@ -24,28 +24,12 @@ MULT = mybir.AluOpType.mult
 ADD = mybir.AluOpType.add
 RELU = mybir.ActivationFunctionType.Relu
 
+COPY = mybir.ActivationFunctionType.Copy
+
 LOW, HIGH, BOTH = slice(0, 1), slice(1, 2), slice(0, 2)
 
 PAD = 32
-HEAD = 128
-LAST = 160
-AB = ((0, 1), (2, 3), (4, 5), (6, 7), (2, 4), (6, 1), (0, 3), (5, 6))
-
-CELL = 64
-X01_0, X01_1, X01_2 = (26, 8), (2, 8), (26, 8)
-X23_0 = (6, 8)
-X2_1 = (52, 4)
-X2_2 = (34, 6)
-X3_1 = (50, 4)
-X6_2 = (37, 3)
-X7_2 = (47, 2)
-RELU0 = (2, 36)
-RELU1 = (62, 10)
-H0 = (46, 2)
-H3 = (38, 2)
-H4 = (42, 6)
-H5 = (50, 2)
-STAGE_CELLS = 82
+AB = ((0, 1), (2, 3), (4, 5), (6, 7), (0, 2), (1, 3), (6, 5), (7, 4))
 
 
 def tile_moe_pre_glu_relu_kernel(
@@ -60,12 +44,14 @@ def tile_moe_pre_glu_relu_kernel(
         pos1_sb = keep.tile([P, T // 16], U16, name="pos1_sb")
         pos2_sb = keep.tile([P, T // 16], U16, name="pos2_sb")
         gate_sb = keep.tile([P, S], F32, name="gate_sb")
-        windows = [[keep.tile([P, T + PAD], F32, name=f"x{s}{t}") for t in range(PACK)] for s in range(PASSES)]
-        w1c = keep.tile([P, E, PASSES, 2 * H], U8, name="w1c", align_bytes=64)
-        w3c = keep.tile([P, E, PASSES, 2 * H], U8, name="w3c", align_bytes=64)
+        windows = [[keep.tile([P, T + PAD], F32, name=f"x{s}{t}")[:] for t in range(PACK)] for s in range(PASSES - 1)]
+        x_last = keep.tile([P, PACK * T], F32, name="x_last")
+        windows.append([x_last[:, t * T : (t + 1) * T] for t in range(PACK)])
+        w1c = keep.tile([P, E * PASSES * 2 * H], U8, name="w1c", align_bytes=64)
+        w3c = keep.tile([P, E * PASSES * 2 * H], U8, name="w3c", align_bytes=64)
         w2c = keep.tile([P, E, 2 * N], U8, name="w2c", align_bytes=64)
-        w1s = keep.tile([P, E * PASSES, H], U8, name="w1s", align_bytes=64)
-        w3s = keep.tile([P, E * PASSES, H], U8, name="w3s", align_bytes=64)
+        w1s = [keep.tile([P, 2 * PASSES, H], U8, name=f"w1s{g}", align_bytes=64) for g in range(2)]
+        w3s = [keep.tile([P, 2 * PASSES, H], U8, name=f"w3s{g}", align_bytes=64) for g in range(2)]
         w2s = keep.tile([P, E, N], U8, name="w2s", align_bytes=64)
         xq = keep.tile([P, PASSES * S], U32, name="xq", align_bytes=64)
         xs = keep.tile([P, PASSES * S], U8, name="xs", align_bytes=64)
@@ -77,35 +63,44 @@ def tile_moe_pre_glu_relu_kernel(
         first = keep.tile([P, N // P * T], F32, name="first")
         total = keep.tile([P, N // P * T], F32, name="total")
         ident = keep.tile([P, P], F32, name="ident")
-        stage = keep.tile([P, STAGE_CELLS * CELL], F32, name="stage")
+        zeros = keep.tile([P, P], F32, name="zeros")
         bank = [psum.tile([P, H], F32, name=f"bank{b}") for b in range(8)]
+        pairs = [keep.tile([P, 2, P], F32, name=f"pairs{j}") for j in range(S // P)]
 
-        def rows(place, count, width):
-            cell, step = place
-            span = stage[:, cell * CELL : (cell + count * step) * CELL]
-            return span.rearrange("p (r c) -> p r c", r=count)[:, :, :width]
+        e1, e2, e3 = C, 2 * C, 3 * C
+        t5, t7 = 5 * P, 7 * P
 
-        def own_halves(name, width):
-            return keep.tile([P, 2 * width], F32, name=name)[:].rearrange("p (u c) -> p u c", u=2)
+        last_codes = [keep.tile([P, C], U32, name=f"xq_last{e}", tag=f"after{e}", align_bytes=64) for e in range(2)]
 
-        relus = [rows(place, 2, H // 2) for place in (RELU0, RELU1)]
-        relus.extend(own_halves(f"relu{j}", H // 2) for j in range(2, S // P))
-        pairs = {0: rows(H0, 2, P), 1: own_halves("pairs1", P)}
-        pairs[3], pairs[4], pairs[5] = [rows(place, 2, P) for place in (H3, H4, H5)]
-        words6 = keep.tile([P, 2 * P], F32, name="pairs6", tag="held", align_bytes=64)
-        pairs[6] = words6[:].rearrange("p (u c) -> p u c", u=2)
-        pairs[7] = own_halves("pairs7", P)
-        halves = {(j, u): pairs[j][:, u] for j in pairs for u in range(2)}
-        for u in range(2):
-            at = ((PASSES - 1) * S + (6 + u) * P) * PACK
-            halves[2, u] = xb[:, at : at + 2 * P].bitcast(F32)
-        b_sb = {(j, u): keep.tile([P, H // 2], F32, name=f"b{j}{u}") for j, u in ((1, 1), (2, 0), (2, 1))}
-        h_planes = {lo: hs[:, lo:hi] for lo, hi in ((C, 2 * C), (2 * C, 3 * C), (3 * C, S - P), (S - P, S))}
+        last_scales = keep.tile([P, C], U8, name="xs_last", tag="after1s", align_bytes=64)
 
-        nc.vector.memset(w1s[:].bitcast(I32), 0)
-        nc.vector.memset(w3s[:, : 2 * PASSES].bitcast(I32), 0)
-        make_identity(nc, ident[:])
-        nc.gpsimd.memset(w3s[:, 2 * PASSES :].bitcast(I32), 0)
+        def scales_of(s, lo, hi):
+            if s == PASSES - 1 and e1 <= lo < e2:
+                return last_scales[:, lo - e1 : hi - e1]
+            return xs[:, S * s + lo : S * s + hi]
+
+        def codes_of(s, lo, hi):
+            if s == PASSES - 1 and hi <= e2:
+                e = lo // C
+                return last_codes[e][:, lo - e * C : hi - e * C]
+            return xq[:, S * s + lo : S * s + hi]
+
+        stages = {}
+
+        def stage(s, lo, hi, tag=None):
+            name = f"stage{s}_{lo}"
+            stages[s, lo] = keep.tile([P, PACK * (hi - lo)], F32, name=name, tag=tag or name, align_bytes=64)[:]
+
+        def rows(s, lo):
+            return stages[s, lo].rearrange("p (t c) -> p t c", t=PACK)
+
+        nc.vector.memset(zeros[:], 0.0)
+        nc.scalar.activation(ident[:], zeros[:], RELU)
+        make_identity(nc, ident[:], nomemset=True)
+        nc.vector.memset(w1s[0][:].bitcast(I32), 0)
+        nc.vector.memset(w3s[0][:].bitcast(I32), 0)
+        nc.vector.memset(w1s[1][:].bitcast(I32), 0)
+        nc.vector.memset(w3s[1][:].bitcast(I32), 0)
         nc.gpsimd.memset(w2s[:].bitcast(I32), 0)
 
         x_rows = xT.rearrange("(s p t) c -> s t p c", p=P, t=PACK)
@@ -124,62 +119,87 @@ def tile_moe_pre_glu_relu_kernel(
                     scales.rearrange("e s (q r) n -> r q (e s) n", r=4)[r].bitcast(I32),
                 )
 
-        def load_words(e):
+        def words_at(e, s):
+            return slice((e * PASSES + s) * 2 * H, (e * PASSES + s + 1) * 2 * H)
+
+        def load_words(e, lo, hi):
             for codes, words in ((w1c, w1_words), (w3c, w3_words)):
-                nc.sync.dma_start(codes[:, e].bitcast(I32), words[e].rearrange("s p b -> p s b").bitcast(I32))
+                nc.sync.dma_start(
+                    codes[:, words_at(e, lo).start : words_at(e, hi - 1).stop].bitcast(I32).rearrange("p (s b) -> p s b", s=hi - lo),
+                    words[e, lo:hi].rearrange("s p b -> p s b").bitcast(I32),
+                )
 
         load_x(0, [0])
         nc.sync.dma_start(offs_sb[:], offs)
-        load_gate(0, HEAD)
-        load_gate(HEAD, 2 * C)
-        load_x(0, [1, 2, 3])
+        load_gate(e2, S)
+        load_x(0, [1, 2])
+        load_gate(0, e2)
+        load_x(0, [3])
         load_x(1, range(PACK))
-        load_x(2, range(PACK))
-        load_gate(2 * C, S)
-        load_scales(w1s, w1_scales)
-        load_scales(w3s, w3_scales)
+        nc.sync.dma_start(x_last[:], xT[(PASSES - 1) * P * PACK :].rearrange("(p t) c -> p (t c)", t=PACK))
+        load_scales(w1s[0], w1_scales[:2])
+        load_scales(w3s[0], w3_scales[:2])
+        load_words(0, 0, 1)
+        load_words(1, 0, 1)
+        load_words(0, 1, PASSES)
+        load_words(1, 1, 2)
+        load_scales(w1s[1], w1_scales[2:])
+        load_scales(w3s[1], w3_scales[2:])
+        load_words(1, 2, PASSES)
+        load_words(2, 0, 2)
+        load_words(3, 0, 2)
+        load_words(2, 2, PASSES)
+        load_words(3, 2, PASSES)
         load_scales(w2s, w2_scales)
-        load_words(0)
-        load_words(1)
-        load_words(2)
         nc.sync.dma_start(w2c[:].bitcast(I32), w2_words.rearrange("e s p b -> p (e s) b").bitcast(I32))
-        load_words(3)
         nc.sync.dma_start(pos1_sb[:], pos1)
         nc.sync.dma_start(pos2_sb[:], pos2)
 
-        def gather(s, lo, hi, place, ts, part=None):
-            a, b = part or (lo, hi)
+        def gather_scalar(s, lo, hi, ts=range(PACK)):
+            for t in ts:
+                nc.scalar.activation(rows(s, lo)[:, t], windows[s][t].indirect(offs_sb[:, lo // 16 : hi // 16]), COPY)
+
+        def gather_gated(s, lo, hi, ts=range(PACK)):
             for t in ts:
                 nc.vector.tensor_tensor(
-                    rows(place, PACK, hi - lo)[:, t, a - lo : b - lo],
-                    windows[s][t][:].indirect(offs_sb[:, a // 16 : b // 16]),
-                    gate_sb[:, a:b],
-                    MULT,
+                    rows(s, lo)[:, t], windows[s][t].indirect(offs_sb[:, lo // 16 : hi // 16]), gate_sb[:, lo:hi], MULT
                 )
 
-        def weave(s, lo, hi, place, at=0):
-            src = rows(place, PACK, at + hi - lo)[:, :, at:]
-            nc.scalar.copy(
-                xb[:, (S * s + lo) * PACK : (S * s + hi) * PACK].rearrange("p (c i t) -> p c t i", i=4, t=PACK),
-                src.rearrange("p t (c i) -> p c t i", i=4),
+        rounded = {}
+
+        def rounded_x(s, lo, hi):
+            return rounded.get((s, lo), xb[:, (S * s + lo) * PACK : (S * s + hi) * PACK])
+
+        def woven(s, lo, hi, run):
+            return rounded_x(s, lo, hi).rearrange("p (c i t) -> p c t i", i=run, t=PACK)
+
+        def weave(s, lo, hi):
+            nc.vector.tensor_copy(woven(s, lo, hi, 4), rows(s, lo).rearrange("p t (c i) -> p c t i", i=4))
+
+        def weave_gated(s, lo, hi, batch=None):
+            batch = lo if batch is None else batch
+            nc.vector.tensor_tensor(
+                woven(s, lo, hi, 2),
+                rows(s, batch)[:, :, lo - batch : hi - batch].rearrange("p t (c i) -> p c t i", i=2),
+                gate_sb[:, lo:hi].rearrange("p (c i) -> p c i", i=2).unsqueeze(2).to_broadcast([P, (hi - lo) // 2, PACK, 2]),
+                MULT,
             )
 
         def quantize_x(s, lo, hi):
-            a, b = S * s + lo, S * s + hi
-            nc.vector.quantize_mx(out=xq[:, a:b].bitcast(FP8X4), scales=xs[:, a:b], in_=xb[:, a * PACK : b * PACK])
+            nc.vector.quantize_mx(out=codes_of(s, lo, hi).bitcast(FP8X4), scales=scales_of(s, lo, hi), in_=rounded_x(s, lo, hi))
 
-        def first_layer(tiles, passes):
+        def first_layer(tiles, passes, sides=(0, 1)):
             for s in passes:
-                for which, (codes, plane) in enumerate(((w1c, w1s), (w3c, w3s))):
+                for which in sides:
+                    codes, planes = ((w1c, w1s), (w3c, w3s))[which]
                     for j in tiles:
                         e = j * P // C
-                        cols = slice(S * s + j * P, S * s + (j + 1) * P)
                         nc.tensor.matmul_mx(
                             out=bank[AB[j][which]][:],
-                            lhsT=xq[:, cols].bitcast(FP8X4),
-                            lhsT_scale=xs[:, cols],
-                            rhs=codes[:, e, s, :].bitcast(FP4X4),
-                            rhs_scale=plane[:, e * PASSES + s, :],
+                            lhsT=codes_of(s, j * P, (j + 1) * P).bitcast(FP8X4),
+                            lhsT_scale=scales_of(s, j * P, (j + 1) * P),
+                            rhs=codes[:, words_at(e, s)].bitcast(FP4X4),
+                            rhs_scale=planes[e // 2][:, e % 2 * PASSES + s, :],
                             start=(s == 0),
                             stop=(s == PASSES - 1),
                         )
@@ -187,27 +207,23 @@ def tile_moe_pre_glu_relu_kernel(
         def by_half(b):
             return bank[b][:].rearrange("j (p u d) -> j u p d", u=2, d=2)
 
+        relus = {}
+
         def relu(j, us=BOTH):
-            nc.scalar.activation(relus[j].rearrange("j u (p d) -> j u p d", d=2)[:, us], by_half(AB[j][0])[:, us], RELU)
+            nc.scalar.activation(relus[j].rearrange("j (u p d) -> j u p d", u=2, d=2)[:, us], by_half(AB[j][0])[:, us], RELU)
 
         def product(j, us=BOTH):
             nc.vector.tensor_tensor(
-                pairs[j].bitcast(BF16).rearrange("j u (p d) -> j u p d", d=2)[:, us],
+                pairs[j][:].bitcast(BF16).rearrange("j u (p d) -> j u p d", d=2)[:, us],
                 by_half(AB[j][1])[:, us],
-                relus[j].rearrange("j u (p d) -> j u p d", d=2)[:, us],
+                relus[j].rearrange("j (u p d) -> j u p d", u=2, d=2)[:, us],
                 MULT,
             )
-
-        def copy_b(j, u):
-            nc.scalar.copy(b_sb[j, u][:].rearrange("j (p d) -> j p d", d=2), by_half(AB[j][1])[:, u])
-
-        def product_gpsimd(j, u):
-            nc.gpsimd.tensor_tensor(halves[j, u].bitcast(BF16), b_sb[j, u][:], relus[j][:, u], MULT)
 
         def turn(j, b, width, at):
             dst = bank[b][:, : 2 * width].rearrange("p (u j) -> p u j", u=2)
             for u in range(2):
-                nc.tensor.transpose(dst[:, u, at : at + P], halves[j, u], ident[:])
+                nc.tensor.transpose(dst[:, u, at : at + P], pairs[j][:, u], ident[:])
 
         def copy_turned(b, lo, hi):
             nc.scalar.copy(
@@ -216,7 +232,7 @@ def tile_moe_pre_glu_relu_kernel(
             )
 
         def quantize_h(lo, hi):
-            nc.vector.quantize_mx(out=hq[:, lo:hi].bitcast(FP8X4), scales=h_planes[lo], in_=hb[:, lo * PACK : hi * PACK])
+            nc.vector.quantize_mx(out=hq[:, lo:hi].bitcast(FP8X4), scales=hs[:, lo:hi], in_=hb[:, lo * PACK : hi * PACK])
 
         def second_layer(lo, hi, m, b, at):
             e = lo // C
@@ -225,7 +241,7 @@ def tile_moe_pre_glu_relu_kernel(
                 lhsT=w2c[:, e, 2 * m * P : 2 * (m + 1) * P].bitcast(FP4X4),
                 lhsT_scale=w2s[:, e, m * P : (m + 1) * P],
                 rhs=hq[:, lo:hi].bitcast(FP8X4),
-                rhs_scale=h_planes[lo],
+                rhs_scale=hs[:, lo:hi],
                 start=True,
                 stop=True,
             )
@@ -233,142 +249,135 @@ def tile_moe_pre_glu_relu_kernel(
         def copy_y(lo, hi, m, b, at, copy=nc.scalar.copy):
             copy(y[m][:, lo:hi], bank[b][:, at : at + hi - lo])
 
-        e1, e2, e3 = C, 2 * C, 3 * C
-        t3, t5, t7 = 3 * P, 5 * P, 7 * P
-        mid7 = t7 + P // 2
-
-        gather(0, 0, e2, X01_0, (0,), (0, HEAD))
-        gather(0, 0, e2, X01_0, (0,), (HEAD, e2))
-        gather(0, 0, e2, X01_0, (1, 2, 3))
-        weave(0, 0, e2, X01_0)
+        stage(0, 0, e2, "opening")
+        stage(0, e2, S)
+        stage(1, 0, e2, "second")
+        stage(2, 0, e1, "early")
+        stage(2, e1, e2)
+        stage(1, e2, e3, "second")
+        rounded[0, e2] = keep.tile([P, PACK * e2], BF16, name="xb0", tag="opening", align_bytes=64)[:]
+        gather_scalar(0, 0, e2)
+        gather_gated(0, e2, S)
+        gather_scalar(1, 0, e2)
+        weave_gated(0, 0, e2)
         quantize_x(0, 0, e2)
-        gather(1, 0, e2, X01_1, range(PACK))
-        weave(1, 0, e2, X01_1)
-        quantize_x(1, 0, e2)
-        first_layer((0, 1), (0, 1))
-        first_layer((2, 3), (0, 1))
-        gather(2, 0, e2, X01_2, (3, 2, 1, 0))
-        weave(2, 0, e1, X01_2)
-        weave(2, e1, e2, X01_2, at=C)
+        weave(0, e2, S)
+        first_layer((0, 1), (0,))
+        first_layer((2, 3), (0,))
+        gather_scalar(2, 0, e1)
+        gather_scalar(2, e1, e2)
+        weave_gated(1, 0, e1, 0)
+        weave_gated(1, e1, e2, 0)
+        quantize_x(1, 0, e1)
+        weave_gated(2, 0, e1)
+        quantize_x(1, e1, e2)
         quantize_x(2, 0, e1)
-        first_layer((0, 1), (2,))
-        gather(0, e2, S, X23_0, (0, 1, 2))
+        quantize_x(0, e2, S)
+        first_layer((0, 1), (1, 2))
+        first_layer((2, 3), (1,))
+        gather_scalar(1, e2, e3)
+
+        stage(1, e3, S, "early")
+        relus[0] = stages[1, e3][:, 2 * C :]
+        late_x = keep.tile([P, H], F32, name="late_x", align_bytes=64)
+        relus[3] = late_x[:]
+        rounded[2, e2] = late_x[:, : H // 2].bitcast(BF16)
+        for j in (1, 2, 4, 5, 6, 7):
+            relus[j] = keep.tile([P, H], F32, name=f"relu{j}")[:]
+        weave_gated(2, e1, e2)
+        gather_gated(1, e3, S, (0,))
         quantize_x(2, e1, e2)
         first_layer((2, 3), (2,))
-
+        weave_gated(1, e2, e3)
+        gather_gated(1, e3, S, (1,))
+        quantize_x(1, e2, e3)
         relu(0)
         relu(1)
-        copy_b(1, 1)
+        stage(2, e2, t5, "after0")
+        gather_scalar(2, e2, t5)
+        product(0)
+        product(1)
+        first_layer((4,), (0, 1))
+        gather_gated(1, e3, S, (2, 3))
         relu(2)
         relu(3)
-        gather(1, e2, e3, X2_1, (0, 1))
-        gather(0, e2, S, X23_0, (3,))
-        product_gpsimd(1, 1)
-        product(0, LOW)
-        product(0, HIGH)
-        product(1, LOW)
+        first_layer((5,), (0, 1))
         for j in (0, 1):
-            turn(j, 0, C, j * P)
-        weave(0, e2, S, X23_0)
-
-        gather(2, e2, e3, X2_2, (1,))
-        gather(1, e2, e3, X2_1, (2, 3))
-        weave(1, e2, e3, X2_1)
-        copy_turned(0, 0, e1)
-        copy_b(2, 0)
-        copy_b(2, 1)
-        gather(2, e2, e3, X2_2, (2,))
-        quantize_x(0, e2, S)
-        first_layer((5,), (0,))
-        first_layer((4,), (0,))
-        gather(2, e2, e3, X2_2, (0,))
-        quantize_x(1, e2, e3)
-        first_layer((5,), (1,))
-        gather(2, e2, e3, X2_2, (3,))
-        weave(2, t5, e3, X2_2, at=P)
-        weave(2, e2, t5, X2_2)
-        gather(1, e3, S, X3_1, (2, 3))
+            turn(j, 4, C, j * P)
+        late = keep.tile([P, PACK * 3 * P], F32, name="late", tag="after1", align_bytes=64)
+        for i, lo in enumerate((t5, e3, t7)):
+            stages[2, lo] = late[:, i * PACK * P : (i + 1) * PACK * P]
+        rounded[1, e3] = keep.tile([P, PACK * C], BF16, name="xb_e3", tag="after1s", align_bytes=64)[:]
+        gather_scalar(2, t5, e3)
+        copy_turned(4, 0, e1)
+        gather_scalar(2, e3, t7)
+        product(2)
+        weave(1, e3, S)
+        product(3)
+        quantize_x(1, e3, S)
+        first_layer((6,), (0,))
+        first_layer((7,), (0,), (1,))
+        for j in (2, 3):
+            turn(j, 7, C, (j - 2) * P)
+        gather_scalar(2, t7, S)
+        copy_turned(7, e1, e2)
+        first_layer((6,), (1,))
+        first_layer((7,), (1,), (1,))
+        weave_gated(2, e2, t5)
+        weave_gated(2, t5, e3)
+        quantize_x(2, e2, t5)
+        first_layer((4,), (2,))
+        first_layer((7,), (0, 1), (0,))
+        weave_gated(2, e3, t7)
         quantize_x(2, t5, e3)
         first_layer((5,), (2,))
-        relu(5)
-        gather(1, e3, S, X3_1, (1,))
-        quantize_x(2, e2, t5)
-        first_layer((4,), (1, 2))
-
-        first_layer((6, 7), (0,))
-        gather(1, e3, S, X3_1, (0,))
-        weave(1, e3, t7, X3_1)
-        weave(1, t7, S, X3_1, at=P)
-        gather(2, e3, t7, X6_2, range(PACK))
-        weave(2, e3, t7, X6_2)
-        relu(4)
-        gather(2, t7, S, X7_2, (0,), (mid7, S))
-        quantize_x(1, e3, t7)
-        first_layer((6,), (1,))
-        gather(2, t7, S, X7_2, (1,))
-        quantize_x(1, t7, S)
-        first_layer((7,), (1,))
-        gather(2, t7, S, X7_2, (2, 3))
-        weave(2, mid7, S, X7_2, at=P // 2)
+        weave_gated(2, t7, S)
         quantize_x(2, e3, t7)
-        first_layer((6,), (2,))
-        gather(2, t7, S, X7_2, (0,), (t7, mid7))
-        weave(2, t7, mid7, X7_2)
-
-        product_gpsimd(2, 0)
-        product(3)
-        product(4, LOW)
         quantize_x(2, t7, S)
-        product(4, HIGH)
-        product_gpsimd(2, 1)
+        first_layer((6, 7), (2,))
+        relu(4)
+        relu(5)
         relu(6)
-        turn(3, 2, P, 0)
-        copy_turned(2, t3, e2)
-        first_layer((7,), (2,))
-        turn(4, 7, C, 0)
         relu(7, LOW)
         relu(7, HIGH)
+        product(4)
         product(5)
         product(6)
         product(7, LOW)
         product(7, HIGH)
-        turn(5, 7, C, P)
-        copy_turned(7, e2, e3)
-        turn(2, 1, P, 0)
-        copy_turned(1, e1, t3)
-        turn(6, 4, P, 0)
-        copy_turned(4, e3, t7)
-        h_planes[0] = keep.tile([P, C], U8, name="hs0", tag="held", align_bytes=64)[:]
-        quantize_h(0, e1)
-        turn(7, 0, P, 0)
-        copy_turned(0, t7, S)
+        turn(4, 0, C, 0)
+        turn(5, 0, C, P)
+        copy_turned(0, e2, e3)
+        turn(6, 6, P, 0)
+        copy_turned(6, e3, t7)
+        turn(7, 7, P, 0)
+        copy_turned(7, t7, S)
+        quantize_h(0, e2)
         quantize_h(e2, e3)
-        quantize_h(e1, e2)
         quantize_h(e3, t7)
         quantize_h(t7, S)
-        for lo, hi, b in ((0, e1, 6), (e2, e3, 7), (e1, e2, 5)):
-            second_layer(lo, hi, 0, b, 0)
-            copy_y(lo, hi, 0, b, 0)
-        second_layer(e3, t7, 0, 4, 0)
-        copy_y(e3, t7, 0, 4, 0, nc.vector.tensor_copy)
-        second_layer(t7, S, 0, 3, 0)
-        copy_y(t7, S, 0, 3, 0)
-        second_layer(e3, t7, 1, 5, 0)
-        second_layer(t7, S, 1, 5, P)
-        copy_y(e3, S, 1, 5, 0)
-        second_layer(0, e1, 1, 4, 0)
-        copy_y(0, e1, 1, 4, 0)
-        second_layer(e1, e2, 1, 3, 0)
-        second_layer(e2, e3, 1, 3, C)
-        copy_y(e1, e3, 1, 3, 0)
+        second_layer(0, e1, 0, 2, 0)
+        second_layer(e1, e2, 0, 2, C)
+        second_layer(0, e1, 1, 6, 0)
+        second_layer(e1, e2, 1, 6, C)
+        second_layer(e2, e3, 0, 3, 0)
+        second_layer(e3, t7, 0, 3, C)
+        second_layer(t7, S, 0, 4, 0)
+        second_layer(e2, e3, 1, 5, 0)
+        second_layer(e3, S, 1, 5, C)
+        copy_y(0, e2, 0, 2, 0, nc.vector.tensor_copy)
+        copy_y(0, e2, 1, 6, 0)
+        copy_y(e2, t7, 0, 3, 0)
+        copy_y(t7, S, 0, 4, 0, nc.vector.tensor_copy)
+        copy_y(e2, S, 1, 5, 0, nc.vector.tensor_copy)
 
-        pieces = ((0, T - LAST), (T - LAST, T))
+        cuts = (0, 192, 352, T)
         for m in range(N // P):
-            for lo, hi in pieces:
-                nc.vector.tensor_copy(first[:, m * T + lo : m * T + hi], y[m][:].indirect(pos1_sb[:, lo // 16 : hi // 16]))
-            for lo, hi in pieces:
+            for lo, hi in zip(cuts, cuts[1:]):
                 cols = slice(m * T + lo, m * T + hi)
+                nc.scalar.activation(first[:, cols], y[m][:].indirect(pos1_sb[:, lo // 16 : hi // 16]), COPY)
                 nc.vector.tensor_tensor(
                     total[:, cols], y[m][:].indirect(pos2_sb[:, lo // 16 : hi // 16]), first[:, cols], ADD
                 )
-                nc.sync.dma_start(out[m * P : (m + 1) * P, lo:hi], total[:, cols])
+        for m, lo, hi in ((0, 0, T), (1, 0, cuts[2]), (1, cuts[2], T)):
+            nc.sync.dma_start(out[m * P : (m + 1) * P, lo:hi], total[:, m * T + lo : m * T + hi])

@@ -29,7 +29,8 @@ COPY = mybir.ActivationFunctionType.Copy
 LOW, HIGH, BOTH = slice(0, 1), slice(1, 2), slice(0, 2)
 
 PAD = 32
-AB = ((0, 1), (2, 3), (4, 5), (6, 7), (0, 2), (1, 3), (6, 5), (7, 4))
+HEAD = 128
+AB = ((0, 1), (2, 3), (4, 5), (6, 7), (0, 1), (2, 3), (4, 5), (6, 7))
 
 
 def tile_moe_pre_glu_relu_kernel(
@@ -72,11 +73,12 @@ def tile_moe_pre_glu_relu_kernel(
 
         last_codes = [keep.tile([P, C], U32, name=f"xq_last{e}", tag=f"after{e}", align_bytes=64) for e in range(2)]
 
-        last_scales = keep.tile([P, C], U8, name="xs_last", tag="after1s", align_bytes=64)
+        own_scales = {(PASSES - 1, 1): keep.tile([P, C], U8, name="xs_last", tag="after1s", align_bytes=64)}
 
         def scales_of(s, lo, hi):
-            if s == PASSES - 1 and e1 <= lo < e2:
-                return last_scales[:, lo - e1 : hi - e1]
+            e = lo // C
+            if (s, e) in own_scales:
+                return own_scales[s, e][:, lo - e * C : hi - e * C]
             return xs[:, S * s + lo : S * s + hi]
 
         def codes_of(s, lo, hi):
@@ -131,7 +133,8 @@ def tile_moe_pre_glu_relu_kernel(
 
         load_x(0, [0])
         nc.sync.dma_start(offs_sb[:], offs)
-        load_gate(e2, S)
+        load_gate(e2, e2 + HEAD)
+        load_gate(e2 + HEAD, S)
         load_x(0, [1, 2])
         load_gate(0, e2)
         load_x(0, [3])
@@ -159,10 +162,14 @@ def tile_moe_pre_glu_relu_kernel(
             for t in ts:
                 nc.scalar.activation(rows(s, lo)[:, t], windows[s][t].indirect(offs_sb[:, lo // 16 : hi // 16]), COPY)
 
-        def gather_gated(s, lo, hi, ts=range(PACK)):
+        def gather_gated(s, lo, hi, ts, batch=None):
+            batch = lo if batch is None else batch
             for t in ts:
                 nc.vector.tensor_tensor(
-                    rows(s, lo)[:, t], windows[s][t].indirect(offs_sb[:, lo // 16 : hi // 16]), gate_sb[:, lo:hi], MULT
+                    rows(s, batch)[:, t, lo - batch : hi - batch],
+                    windows[s][t].indirect(offs_sb[:, lo // 16 : hi // 16]),
+                    gate_sb[:, lo:hi],
+                    MULT,
                 )
 
         rounded = {}
@@ -225,8 +232,8 @@ def tile_moe_pre_glu_relu_kernel(
             for u in range(2):
                 nc.tensor.transpose(dst[:, u, at : at + P], pairs[j][:, u], ident[:])
 
-        def copy_turned(b, lo, hi):
-            nc.scalar.copy(
+        def copy_turned(b, lo, hi, copy=nc.scalar.copy):
+            copy(
                 hb[:, lo * PACK : hi * PACK].bitcast(F32).rearrange("p (j u) -> p j u", u=2),
                 bank[b][:, : 2 * (hi - lo)].rearrange("p (u j) -> p j u", u=2),
             )
@@ -252,18 +259,25 @@ def tile_moe_pre_glu_relu_kernel(
         stage(0, 0, e2, "opening")
         stage(0, e2, S)
         stage(1, 0, e2, "second")
-        stage(2, 0, e1, "early")
+        stage(2, 0, e1)
         stage(2, e1, e2)
         stage(1, e2, e3, "second")
         rounded[0, e2] = keep.tile([P, PACK * e2], BF16, name="xb0", tag="opening", align_bytes=64)[:]
+        rounded[0, 0] = keep.tile([P, PACK * C], BF16, name="xb00", tag="early", align_bytes=64)[:]
+        stage(1, e3, S, "early")
         gather_scalar(0, 0, e2)
-        gather_gated(0, e2, S)
+        gather_gated(0, e2, e2 + HEAD, (0,))
+        gather_gated(0, e2 + HEAD, S, (0,), e2)
+        gather_gated(0, e2, S, (1, 2, 3))
         gather_scalar(1, 0, e2)
-        weave_gated(0, 0, e2)
-        quantize_x(0, 0, e2)
+        weave_gated(0, 0, e1, 0)
+        weave_gated(0, e1, e2, 0)
+        quantize_x(0, 0, e1)
         weave(0, e2, S)
+        quantize_x(0, e1, e2)
         first_layer((0, 1), (0,))
         first_layer((2, 3), (0,))
+        gather_gated(1, e3, S, (0,))
         gather_scalar(2, 0, e1)
         gather_scalar(2, e1, e2)
         weave_gated(1, 0, e1, 0)
@@ -271,63 +285,56 @@ def tile_moe_pre_glu_relu_kernel(
         quantize_x(1, 0, e1)
         weave_gated(2, 0, e1)
         quantize_x(1, e1, e2)
-        quantize_x(2, 0, e1)
         quantize_x(0, e2, S)
+        quantize_x(2, 0, e1)
         first_layer((0, 1), (1, 2))
         first_layer((2, 3), (1,))
         gather_scalar(1, e2, e3)
 
-        stage(1, e3, S, "early")
-        relus[0] = stages[1, e3][:, 2 * C :]
         late_x = keep.tile([P, H], F32, name="late_x", align_bytes=64)
-        relus[3] = late_x[:]
+        relus[2] = late_x[:]
         rounded[2, e2] = late_x[:, : H // 2].bitcast(BF16)
-        for j in (1, 2, 4, 5, 6, 7):
+        for j in (0, 1, 3, 4, 5, 6, 7):
             relus[j] = keep.tile([P, H], F32, name=f"relu{j}")[:]
         weave_gated(2, e1, e2)
-        gather_gated(1, e3, S, (0,))
+        gather_gated(1, e3, S, (1,))
         quantize_x(2, e1, e2)
         first_layer((2, 3), (2,))
+        gather_gated(1, e3, S, (2,))
         weave_gated(1, e2, e3)
-        gather_gated(1, e3, S, (1,))
+        gather_gated(1, e3, S, (3,))
         quantize_x(1, e2, e3)
+        weave(1, e3, S)
         relu(0)
         relu(1)
         stage(2, e2, t5, "after0")
         gather_scalar(2, e2, t5)
         product(0)
         product(1)
-        first_layer((4,), (0, 1))
-        gather_gated(1, e3, S, (2, 3))
         relu(2)
         relu(3)
-        first_layer((5,), (0, 1))
-        for j in (0, 1):
-            turn(j, 4, C, j * P)
+        first_layer((4, 5), (0, 1), (0,))
+        first_layer((6, 7), (0,), (0,))
+        first_layer((4,), (0, 1), (1,))
+        first_layer((5,), (0, 1), (1,))
         late = keep.tile([P, PACK * 3 * P], F32, name="late", tag="after1", align_bytes=64)
         for i, lo in enumerate((t5, e3, t7)):
             stages[2, lo] = late[:, i * PACK * P : (i + 1) * PACK * P]
-        rounded[1, e3] = keep.tile([P, PACK * C], BF16, name="xb_e3", tag="after1s", align_bytes=64)[:]
+        own_scales[1, 3] = keep.tile([P, C], U8, name="xs_e3", tag="after1s", align_bytes=64)
         gather_scalar(2, t5, e3)
-        copy_turned(4, 0, e1)
         gather_scalar(2, e3, t7)
-        product(2)
-        weave(1, e3, S)
-        product(3)
-        quantize_x(1, e3, S)
-        first_layer((6,), (0,))
-        first_layer((7,), (0,), (1,))
-        for j in (2, 3):
-            turn(j, 7, C, (j - 2) * P)
         gather_scalar(2, t7, S)
-        copy_turned(7, e1, e2)
-        first_layer((6,), (1,))
-        first_layer((7,), (1,), (1,))
+        product(2)
+        quantize_x(1, e3, S)
+        product(3)
+        first_layer((6,), (0,), (1,))
+        first_layer((6, 7), (1,), (0,))
+        first_layer((6,), (1,), (1,))
+        first_layer((7,), (0, 1), (1,))
         weave_gated(2, e2, t5)
         weave_gated(2, t5, e3)
         quantize_x(2, e2, t5)
         first_layer((4,), (2,))
-        first_layer((7,), (0, 1), (0,))
         weave_gated(2, e3, t7)
         quantize_x(2, t5, e3)
         first_layer((5,), (2,))
@@ -345,31 +352,38 @@ def tile_moe_pre_glu_relu_kernel(
         product(6)
         product(7, LOW)
         product(7, HIGH)
-        turn(4, 0, C, 0)
-        turn(5, 0, C, P)
-        copy_turned(0, e2, e3)
-        turn(6, 6, P, 0)
-        copy_turned(6, e3, t7)
-        turn(7, 7, P, 0)
-        copy_turned(7, t7, S)
-        quantize_h(0, e2)
-        quantize_h(e2, e3)
+        for j in range(2):
+            turn(j, 0, C, j * P)
+        for j in range(2):
+            turn(2 + j, 2, C, j * P)
+        for j in range(2):
+            turn(4 + j, 1, C, j * P)
+        turn(6, 4, P, 0)
+        turn(7, 6, P, 0)
+        copy_turned(0, 0, e1)
+        copy_turned(2, e1, e2)
+        copy_turned(1, e2, e3)
+        copy_turned(4, e3, t7, nc.vector.tensor_copy)
+        copy_turned(6, t7, S)
+        quantize_h(0, e1)
+        quantize_h(e1, e2)
         quantize_h(e3, t7)
+        quantize_h(e2, e3)
         quantize_h(t7, S)
-        second_layer(0, e1, 0, 2, 0)
-        second_layer(e1, e2, 0, 2, C)
-        second_layer(0, e1, 1, 6, 0)
-        second_layer(e1, e2, 1, 6, C)
-        second_layer(e2, e3, 0, 3, 0)
-        second_layer(e3, t7, 0, 3, C)
-        second_layer(t7, S, 0, 4, 0)
-        second_layer(e2, e3, 1, 5, 0)
-        second_layer(e3, S, 1, 5, C)
-        copy_y(0, e2, 0, 2, 0, nc.vector.tensor_copy)
-        copy_y(0, e2, 1, 6, 0)
-        copy_y(e2, t7, 0, 3, 0)
-        copy_y(t7, S, 0, 4, 0, nc.vector.tensor_copy)
-        copy_y(e2, S, 1, 5, 0, nc.vector.tensor_copy)
+        second_layer(0, e1, 0, 3, 0)
+        second_layer(0, e1, 1, 0, 0)
+        second_layer(e1, e2, 0, 3, C)
+        second_layer(e1, e2, 1, 0, C)
+        second_layer(e2, e3, 0, 5, 0)
+        second_layer(e3, t7, 0, 5, C)
+        second_layer(t7, S, 0, 7, 0)
+        second_layer(e2, e3, 1, 6, 0)
+        second_layer(e3, S, 1, 6, C)
+        copy_y(0, e2, 0, 3, 0)
+        copy_y(0, e2, 1, 0, 0, nc.vector.tensor_copy)
+        copy_y(e2, t7, 0, 5, 0)
+        copy_y(t7, S, 0, 7, 0, nc.vector.tensor_copy)
+        copy_y(e2, S, 1, 6, 0, nc.vector.tensor_copy)
 
         cuts = (0, 192, 352, T)
         for m in range(N // P):

@@ -30,7 +30,7 @@ LOW, HIGH, BOTH = slice(0, 1), slice(1, 2), slice(0, 2)
 
 PAD = 32
 HEAD = 128
-AB = ((0, 1), (2, 3), (4, 5), (6, 7), (0, 1), (2, 3), (4, 5), (6, 7))
+AB = ((0, 1), (2, 3), (4, 5), (6, 7), (0, 1), (2, 3), (4, 5), (7, 6))
 
 
 def tile_moe_pre_glu_relu_kernel(
@@ -71,9 +71,9 @@ def tile_moe_pre_glu_relu_kernel(
         e1, e2, e3 = C, 2 * C, 3 * C
         t5, t7 = 5 * P, 7 * P
 
-        last_codes = [keep.tile([P, C], U32, name=f"xq_last{e}", tag=f"after{e}", align_bytes=64) for e in range(2)]
-
-        own_scales = {(PASSES - 1, 1): keep.tile([P, C], U8, name="xs_last", tag="after1s", align_bytes=64)}
+        own_scales = {
+            (PASSES - 1, e): keep.tile([P, C], U8, name=f"xs_last{e}", tag=f"after{e}s", align_bytes=64) for e in range(2)
+        }
 
         def scales_of(s, lo, hi):
             e = lo // C
@@ -82,9 +82,6 @@ def tile_moe_pre_glu_relu_kernel(
             return xs[:, S * s + lo : S * s + hi]
 
         def codes_of(s, lo, hi):
-            if s == PASSES - 1 and hi <= e2:
-                e = lo // C
-                return last_codes[e][:, lo - e * C : hi - e * C]
             return xq[:, S * s + lo : S * s + hi]
 
         stages = {}
@@ -102,7 +99,7 @@ def tile_moe_pre_glu_relu_kernel(
         nc.vector.memset(w1s[0][:].bitcast(I32), 0)
         nc.vector.memset(w3s[0][:].bitcast(I32), 0)
         nc.vector.memset(w1s[1][:].bitcast(I32), 0)
-        nc.vector.memset(w3s[1][:].bitcast(I32), 0)
+        nc.gpsimd.memset(w3s[1][:].bitcast(I32), 0)
         nc.gpsimd.memset(w2s[:].bitcast(I32), 0)
 
         x_rows = xT.rearrange("(s p t) c -> s t p c", p=P, t=PACK)
@@ -291,10 +288,7 @@ def tile_moe_pre_glu_relu_kernel(
         first_layer((2, 3), (1,))
         gather_scalar(1, e2, e3)
 
-        late_x = keep.tile([P, H], F32, name="late_x", align_bytes=64)
-        relus[2] = late_x[:]
-        rounded[2, e2] = late_x[:, : H // 2].bitcast(BF16)
-        for j in (0, 1, 3, 4, 5, 6, 7):
+        for j in range(S // P):
             relus[j] = keep.tile([P, H], F32, name=f"relu{j}")[:]
         weave_gated(2, e1, e2)
         gather_gated(1, e3, S, (1,))
@@ -307,41 +301,42 @@ def tile_moe_pre_glu_relu_kernel(
         weave(1, e3, S)
         relu(0)
         relu(1)
-        stage(2, e2, t5, "after0")
-        gather_scalar(2, e2, t5)
-        product(0)
-        product(1)
         relu(2)
         relu(3)
-        first_layer((4, 5), (0, 1), (0,))
-        first_layer((6, 7), (0,), (0,))
-        first_layer((4,), (0, 1), (1,))
-        first_layer((5,), (0, 1), (1,))
-        late = keep.tile([P, PACK * 3 * P], F32, name="late", tag="after1", align_bytes=64)
-        for i, lo in enumerate((t5, e3, t7)):
-            stages[2, lo] = late[:, i * PACK * P : (i + 1) * PACK * P]
-        own_scales[1, 3] = keep.tile([P, C], U8, name="xs_e3", tag="after1s", align_bytes=64)
-        gather_scalar(2, t5, e3)
-        gather_scalar(2, e3, t7)
-        gather_scalar(2, t7, S)
-        product(2)
+        own_scales[1, 3] = keep.tile([P, C], U8, name="xs_e3", tag="after0s", align_bytes=64)
+        late = keep.tile([P, PACK * e2], F32, name="late", tag="after1s", align_bytes=64)
+        for lo, hi in ((e2, e3), (e3, t7), (t7, S)):
+            stages[2, lo] = late[:, (lo - e2) * PACK : (hi - e2) * PACK]
+            gather_scalar(2, lo, hi)
+        product(0)
         quantize_x(1, e3, S)
+        product(1)
+        product(2)
         product(3)
-        first_layer((6,), (0,), (1,))
-        first_layer((6, 7), (1,), (0,))
-        first_layer((6,), (1,), (1,))
-        first_layer((7,), (0, 1), (1,))
-        weave_gated(2, e2, t5)
-        weave_gated(2, t5, e3)
+        first_layer((4, 5), (0, 1), (0,))
+        first_layer((6,), (0,), (0,))
+        first_layer((4,), (0, 1), (1,))
+        first_layer((6,), (1,), (0,))
+        first_layer((5,), (0, 1), (1,))
+        first_layer((6,), (0, 1), (1,))
+        for j in range(2):
+            turn(j, 6, C, j * P)
+        copy_turned(6, 0, e1)
+        first_layer((7,), (0, 1), (0,))
+        weave_gated(2, e2, t5, e2)
+        weave_gated(2, t5, e3, e2)
         quantize_x(2, e2, t5)
         first_layer((4,), (2,))
         weave_gated(2, e3, t7)
         quantize_x(2, t5, e3)
         first_layer((5,), (2,))
+        first_layer((7,), (0,), (1,))
         weave_gated(2, t7, S)
         quantize_x(2, e3, t7)
         quantize_x(2, t7, S)
-        first_layer((6, 7), (2,))
+        first_layer((6, 7), (2,), (0,))
+        first_layer((6,), (2,), (1,))
+        first_layer((7,), (1, 2), (1,))
         relu(4)
         relu(5)
         relu(6)
@@ -353,37 +348,36 @@ def tile_moe_pre_glu_relu_kernel(
         product(7, LOW)
         product(7, HIGH)
         for j in range(2):
-            turn(j, 0, C, j * P)
+            turn(2 + j, 0, C, j * P)
         for j in range(2):
-            turn(2 + j, 2, C, j * P)
-        for j in range(2):
-            turn(4 + j, 1, C, j * P)
+            turn(4 + j, 2, C, j * P)
         turn(6, 4, P, 0)
-        turn(7, 6, P, 0)
-        copy_turned(0, 0, e1)
-        copy_turned(2, e1, e2)
-        copy_turned(1, e2, e3)
-        copy_turned(4, e3, t7, nc.vector.tensor_copy)
-        copy_turned(6, t7, S)
+        turn(7, 7, P, 0)
         quantize_h(0, e1)
+        copy_turned(0, e1, e2)
+        copy_turned(2, e2, e3)
+        copy_turned(4, e3, t7, nc.vector.tensor_copy)
+        copy_turned(7, t7, S)
         quantize_h(e1, e2)
         quantize_h(e3, t7)
         quantize_h(e2, e3)
         quantize_h(t7, S)
-        second_layer(0, e1, 0, 3, 0)
-        second_layer(0, e1, 1, 0, 0)
-        second_layer(e1, e2, 0, 3, C)
-        second_layer(e1, e2, 1, 0, C)
-        second_layer(e2, e3, 0, 5, 0)
-        second_layer(e3, t7, 0, 5, C)
-        second_layer(t7, S, 0, 7, 0)
-        second_layer(e2, e3, 1, 6, 0)
-        second_layer(e3, S, 1, 6, C)
-        copy_y(0, e2, 0, 3, 0)
-        copy_y(0, e2, 1, 0, 0, nc.vector.tensor_copy)
-        copy_y(e2, t7, 0, 5, 0)
-        copy_y(t7, S, 0, 7, 0, nc.vector.tensor_copy)
-        copy_y(e2, S, 1, 6, 0, nc.vector.tensor_copy)
+        second_layer(0, e1, 0, 6, 0)
+        second_layer(0, e1, 1, 6, C)
+        second_layer(e1, e2, 0, 5, 0)
+        second_layer(e2, e3, 0, 1, 0)
+        second_layer(e3, t7, 0, 3, 0)
+        second_layer(t7, S, 0, 3, P)
+        copy_y(0, e1, 0, 6, 0)
+        copy_y(0, e1, 1, 6, C)
+        copy_y(e1, e2, 0, 5, 0)
+        copy_y(e2, e3, 0, 1, 0)
+        copy_y(e3, S, 0, 3, 0, nc.vector.tensor_copy)
+        second_layer(e3, S, 1, 7, 0)
+        second_layer(e1, e2, 1, 6, 0)
+        second_layer(e2, e3, 1, 6, C)
+        copy_y(e3, S, 1, 7, 0, nc.vector.tensor_copy)
+        copy_y(e1, e3, 1, 6, 0, nc.vector.tensor_copy)
 
         cuts = (0, 192, 352, T)
         for m in range(N // P):

@@ -81,7 +81,12 @@ def tile_moe_pre_glu_relu_kernel(
                 return own_scales[s, e][:, lo - e * C : hi - e * C]
             return xs[:, S * s + lo : S * s + hi]
 
+        last_codes = [keep.tile([P, C], U32, name=f"xq_last{e}", tag=f"after{e}", align_bytes=64) for e in range(2)]
+
         def codes_of(s, lo, hi):
+            if s == PASSES - 1 and hi <= e2:
+                e = lo // C
+                return last_codes[e][:, lo - e * C : hi - e * C]
             return xq[:, S * s + lo : S * s + hi]
 
         stages = {}
@@ -282,16 +287,19 @@ def tile_moe_pre_glu_relu_kernel(
         quantize_x(1, 0, e1)
         weave_gated(2, 0, e1)
         quantize_x(1, e1, e2)
-        quantize_x(0, e2, S)
         quantize_x(2, 0, e1)
         first_layer((0, 1), (1, 2))
         first_layer((2, 3), (1,))
         gather_scalar(1, e2, e3)
 
-        for j in range(S // P):
+        late_x = keep.tile([P, H], F32, name="late_x", align_bytes=64)
+        relus[2] = late_x[:]
+        rounded[2, t5] = late_x[:, : H // 2].bitcast(BF16)
+        for j in (0, 1, 3, 4, 5, 6, 7):
             relus[j] = keep.tile([P, H], F32, name=f"relu{j}")[:]
-        weave_gated(2, e1, e2)
         gather_gated(1, e3, S, (1,))
+        weave_gated(2, e1, e2)
+        quantize_x(0, e2, S)
         quantize_x(2, e1, e2)
         first_layer((2, 3), (2,))
         gather_gated(1, e3, S, (2,))
@@ -301,32 +309,34 @@ def tile_moe_pre_glu_relu_kernel(
         weave(1, e3, S)
         relu(0)
         relu(1)
+        stage(2, e2, e3, "after0")
+        gather_scalar(2, e2, e3)
         relu(2)
         relu(3)
         own_scales[1, 3] = keep.tile([P, C], U8, name="xs_e3", tag="after0s", align_bytes=64)
-        late = keep.tile([P, PACK * e2], F32, name="late", tag="after1s", align_bytes=64)
-        for lo, hi in ((e2, e3), (e3, t7), (t7, S)):
-            stages[2, lo] = late[:, (lo - e2) * PACK : (hi - e2) * PACK]
+        own_scales[2, 2] = keep.tile([P, C], U8, name="xs_e2", tag="after1s", align_bytes=64)
+        late = keep.tile([P, PACK * C], F32, name="late", tag="after1", align_bytes=64)
+        for lo, hi in ((e3, t7), (t7, S)):
+            stages[2, lo] = late[:, (lo - e3) * PACK : (hi - e3) * PACK]
             gather_scalar(2, lo, hi)
         product(0)
         quantize_x(1, e3, S)
         product(1)
+        weave_gated(2, e2, t5, e2)
         product(2)
+        quantize_x(2, e2, t5)
         product(3)
         first_layer((4, 5), (0, 1), (0,))
-        first_layer((6,), (0,), (0,))
         first_layer((4,), (0, 1), (1,))
-        first_layer((6,), (1,), (0,))
+        first_layer((6,), (0, 1), (0,))
         first_layer((5,), (0, 1), (1,))
-        first_layer((6,), (0, 1), (1,))
         for j in range(2):
             turn(j, 6, C, j * P)
+        first_layer((6,), (0, 1), (1,))
+        first_layer((4,), (2,))
         copy_turned(6, 0, e1)
         first_layer((7,), (0, 1), (0,))
-        weave_gated(2, e2, t5, e2)
         weave_gated(2, t5, e3, e2)
-        quantize_x(2, e2, t5)
-        first_layer((4,), (2,))
         weave_gated(2, e3, t7)
         quantize_x(2, t5, e3)
         first_layer((5,), (2,))
@@ -365,22 +375,24 @@ def tile_moe_pre_glu_relu_kernel(
         second_layer(0, e1, 0, 6, 0)
         second_layer(0, e1, 1, 6, C)
         second_layer(e1, e2, 0, 5, 0)
+        second_layer(e1, e2, 1, 4, 0)
         second_layer(e2, e3, 0, 1, 0)
         second_layer(e3, t7, 0, 3, 0)
-        second_layer(t7, S, 0, 3, P)
+        second_layer(t7, S, 0, 7, 0)
         copy_y(0, e1, 0, 6, 0)
         copy_y(0, e1, 1, 6, C)
         copy_y(e1, e2, 0, 5, 0)
         copy_y(e2, e3, 0, 1, 0)
-        copy_y(e3, S, 0, 3, 0, nc.vector.tensor_copy)
-        second_layer(e3, S, 1, 7, 0)
-        second_layer(e1, e2, 1, 6, 0)
-        second_layer(e2, e3, 1, 6, C)
-        copy_y(e3, S, 1, 7, 0, nc.vector.tensor_copy)
-        copy_y(e1, e3, 1, 6, 0, nc.vector.tensor_copy)
+        copy_y(e1, e2, 1, 4, 0, nc.vector.tensor_copy)
+        copy_y(e3, t7, 0, 3, 0, nc.vector.tensor_copy)
+        copy_y(t7, S, 0, 7, 0, nc.vector.tensor_copy)
+        second_layer(e2, e3, 1, 4, 0)
+        second_layer(e3, S, 1, 4, C)
+        copy_y(e2, S, 1, 4, 0, nc.vector.tensor_copy)
 
-        cuts = (0, 192, 352, T)
+        all_cuts = ((0, 160, 320, T), (0, 192, 384, T))
         for m in range(N // P):
+            cuts = all_cuts[m]
             for lo, hi in zip(cuts, cuts[1:]):
                 cols = slice(m * T + lo, m * T + hi)
                 nc.scalar.activation(first[:, cols], y[m][:].indirect(pos1_sb[:, lo // 16 : hi // 16]), COPY)

from contextlib import ExitStack

import concourse.mybir as mybir
from concourse.masks import make_identity

K, T, E, C, H, N = 1536, 512, 4, 256, 512, 256
S = E * C
P = 128
PACK = 4
PASSES = K // (P * PACK)

FLOPS = 2 * S * (2 * K * H + H * N)
BYTES = 4 * K * T + E * (2 * K * H + H * N) // 2 + E * (2 * K * H + H * N) // 32 + 4 * P * S + 2 * P * (S + 2 * T) // 16 + 4 * N * T

F32 = mybir.dt.float32
BF16 = mybir.dt.bfloat16
I32 = mybir.dt.int32
U32 = mybir.dt.uint32
U16 = mybir.dt.uint16
U8 = mybir.dt.uint8
FP8X4 = mybir.dt.float8_e4m3fn_x4
FP4X4 = mybir.dt.float4_e2m1fn_x4
MULT = mybir.AluOpType.mult
ADD = mybir.AluOpType.add
RELU = mybir.ActivationFunctionType.Relu

COPY = mybir.ActivationFunctionType.Copy

LOW, HIGH, BOTH = slice(0, 1), slice(1, 2), slice(0, 2)

PAD = 32
HEAD = 128
AB = ((0, 1), (2, 3), (4, 5), (6, 7), (0, 1), (2, 3), (4, 5), (7, 6))


def tile_moe_pre_glu_relu_kernel(
    tc, xT, w1_words, w1_scales, w3_words, w3_scales, w2_words, w2_scales, gate, offs, pos1, pos2, out
):
    nc = tc.nc
    with ExitStack() as ctx:
        keep = ctx.enter_context(tc.tile_pool(name="keep", bufs=1))
        psum = ctx.enter_context(tc.psum_pool(name="psum", bufs=1))

        offs_sb = keep.tile([P, S // 16], U16, name="offs_sb")
        pos1_sb = keep.tile([P, T // 16], U16, name="pos1_sb")
        pos2_sb = keep.tile([P, T // 16], U16, name="pos2_sb")
        gate_sb = keep.tile([P, S], F32, name="gate_sb")
        windows = [[keep.tile([P, T + PAD], F32, name=f"x{s}{t}")[:] for t in range(PACK)] for s in range(PASSES - 1)]
        x_last = keep.tile([P, PACK * T], F32, name="x_last")
        windows.append([x_last[:, t * T : (t + 1) * T] for t in range(PACK)])
        w1c = keep.tile([P, E * PASSES * 2 * H], U8, name="w1c", align_bytes=64)
        w3c = keep.tile([P, E * PASSES * 2 * H], U8, name="w3c", align_bytes=64)
        w2c = keep.tile([P, E, 2 * N], U8, name="w2c", align_bytes=64)
        w1s = [keep.tile([P, 2 * PASSES, H], U8, name=f"w1s{g}", align_bytes=64) for g in range(2)]
        w3s = [keep.tile([P, 2 * PASSES, H], U8, name=f"w3s{g}", align_bytes=64) for g in range(2)]
        w2s = keep.tile([P, E, N], U8, name="w2s", align_bytes=64)
        xq = keep.tile([P, PASSES * S], U32, name="xq", align_bytes=64)
        xs = keep.tile([P, PASSES * S], U8, name="xs", align_bytes=64)
        hq = keep.tile([P, S], U32, name="hq", align_bytes=64)
        hs = keep.tile([P, S], U8, name="hs", align_bytes=64)
        xb = keep.tile([P, PASSES * S * PACK], BF16, name="xb", align_bytes=64)
        hb = keep.tile([P, S * PACK], BF16, name="hb", align_bytes=64)
        y = [keep.tile([P, S], F32, name=f"y{m}") for m in range(N // P)]
        first = keep.tile([P, N // P * T], F32, name="first")
        total = keep.tile([P, N // P * T], F32, name="total")
        ident = keep.tile([P, P], F32, name="ident")
        zeros = keep.tile([P, P], F32, name="zeros")
        bank = [psum.tile([P, H], F32, name=f"bank{b}") for b in range(8)]
        pairs = [keep.tile([P, 2, P], F32, name=f"pairs{j}") for j in range(S // P)]

        e1, e2, e3 = C, 2 * C, 3 * C
        t5, t7 = 5 * P, 7 * P

        own_scales = {
            (PASSES - 1, e): keep.tile([P, C], U8, name=f"xs_last{e}", tag=f"after{e}s", align_bytes=64) for e in range(2)
        }

        def scales_of(s, lo, hi):
            e = lo // C
            if (s, e) in own_scales:
                return own_scales[s, e][:, lo - e * C : hi - e * C]
            return xs[:, S * s + lo : S * s + hi]

        last_codes = [keep.tile([P, C], U32, name=f"xq_last{e}", tag=f"after{e}", align_bytes=64) for e in range(2)]

        def codes_of(s, lo, hi):
            if s == PASSES - 1 and hi <= e2:
                e = lo // C
                return last_codes[e][:, lo - e * C : hi - e * C]
            return xq[:, S * s + lo : S * s + hi]

        stages = {}

        def stage(s, lo, hi, tag=None):
            name = f"stage{s}_{lo}"
            stages[s, lo] = keep.tile([P, PACK * (hi - lo)], F32, name=name, tag=tag or name, align_bytes=64)[:]

        def rows(s, lo):
            return stages[s, lo].rearrange("p (t c) -> p t c", t=PACK)

        nc.vector.memset(zeros[:], 0.0)
        nc.scalar.activation(ident[:], zeros[:], RELU)
        make_identity(nc, ident[:], nomemset=True)
        nc.vector.memset(w1s[0][:].bitcast(I32), 0)
        nc.vector.memset(w3s[0][:].bitcast(I32), 0)
        nc.vector.memset(w1s[1][:].bitcast(I32), 0)
        nc.gpsimd.memset(w3s[1][:].bitcast(I32), 0)
        nc.gpsimd.memset(w2s[:].bitcast(I32), 0)

        x_rows = xT.rearrange("(s p t) c -> s t p c", p=P, t=PACK)

        def load_x(s, ts):
            for t in ts:
                nc.sync.dma_start(windows[s][t][:, :T], x_rows[s, t])

        def load_gate(lo, hi):
            nc.sync.dma_start(gate_sb[:, lo:hi], gate[:P, lo:hi])

        def load_scales(plane, scales):
            for r in range(4):
                nc.sync.dma_start(
                    plane[r:P:32].bitcast(I32),
                    scales.rearrange("e s (q r) n -> r q (e s) n", r=4)[r].bitcast(I32),
                )

        def words_at(e, s):
            return slice((e * PASSES + s) * 2 * H, (e * PASSES + s + 1) * 2 * H)

        def load_words(e, lo, hi):
            for codes, words in ((w1c, w1_words), (w3c, w3_words)):
                nc.sync.dma_start(
                    codes[:, words_at(e, lo).start : words_at(e, hi - 1).stop].bitcast(I32).rearrange("p (s b) -> p s b", s=hi - lo),
                    words[e, lo:hi].rearrange("s p b -> p s b").bitcast(I32),
                )

        load_x(0, [0])
        nc.sync.dma_start(offs_sb[:], offs)
        load_gate(e2, e2 + HEAD)
        load_gate(e2 + HEAD, S)
        load_x(0, [1, 2])
        load_gate(0, e2)
        load_x(0, [3])
        load_x(1, range(PACK))
        nc.sync.dma_start(x_last[:], xT[(PASSES - 1) * P * PACK :].rearrange("(p t) c -> p (t c)", t=PACK))
        load_scales(w1s[0], w1_scales[:2])
        load_scales(w3s[0], w3_scales[:2])
        load_words(0, 0, 1)
        load_words(1, 0, 1)
        load_words(0, 1, PASSES)
        load_words(1, 1, 2)
        load_scales(w1s[1], w1_scales[2:])
        load_scales(w3s[1], w3_scales[2:])
        load_words(1, 2, PASSES)
        load_words(2, 0, 2)
        load_words(3, 0, 2)
        load_words(2, 2, PASSES)
        load_words(3, 2, PASSES)
        load_scales(w2s, w2_scales)
        nc.sync.dma_start(w2c[:].bitcast(I32), w2_words.rearrange("e s p b -> p (e s) b").bitcast(I32))
        nc.sync.dma_start(pos1_sb[:], pos1)
        nc.sync.dma_start(pos2_sb[:], pos2)

        def gather_scalar(s, lo, hi, ts=range(PACK)):
            for t in ts:
                nc.scalar.activation(rows(s, lo)[:, t], windows[s][t].indirect(offs_sb[:, lo // 16 : hi // 16]), COPY)

        def gather_gated(s, lo, hi, ts, batch=None):
            batch = lo if batch is None else batch
            for t in ts:
                nc.vector.tensor_tensor(
                    rows(s, batch)[:, t, lo - batch : hi - batch],
                    windows[s][t].indirect(offs_sb[:, lo // 16 : hi // 16]),
                    gate_sb[:, lo:hi],
                    MULT,
                )

        rounded = {}

        def rounded_x(s, lo, hi):
            return rounded.get((s, lo), xb[:, (S * s + lo) * PACK : (S * s + hi) * PACK])

        def woven(s, lo, hi, run):
            return rounded_x(s, lo, hi).rearrange("p (c i t) -> p c t i", i=run, t=PACK)

        def weave(s, lo, hi):
            nc.vector.tensor_copy(woven(s, lo, hi, 4), rows(s, lo).rearrange("p t (c i) -> p c t i", i=4))

        def weave_gated(s, lo, hi, batch=None):
            batch = lo if batch is None else batch
            nc.vector.tensor_tensor(
                woven(s, lo, hi, 2),
                rows(s, batch)[:, :, lo - batch : hi - batch].rearrange("p t (c i) -> p c t i", i=2),
                gate_sb[:, lo:hi].rearrange("p (c i) -> p c i", i=2).unsqueeze(2).to_broadcast([P, (hi - lo) // 2, PACK, 2]),
                MULT,
            )

        def quantize_x(s, lo, hi):
            nc.vector.quantize_mx(out=codes_of(s, lo, hi).bitcast(FP8X4), scales=scales_of(s, lo, hi), in_=rounded_x(s, lo, hi))

        def first_layer(tiles, passes, sides=(0, 1)):
            for s in passes:
                for which in sides:
                    codes, planes = ((w1c, w1s), (w3c, w3s))[which]
                    for j in tiles:
                        e = j * P // C
                        nc.tensor.matmul_mx(
                            out=bank[AB[j][which]][:],
                            lhsT=codes_of(s, j * P, (j + 1) * P).bitcast(FP8X4),
                            lhsT_scale=scales_of(s, j * P, (j + 1) * P),
                            rhs=codes[:, words_at(e, s)].bitcast(FP4X4),
                            rhs_scale=planes[e // 2][:, e % 2 * PASSES + s, :],
                            start=(s == 0),
                            stop=(s == PASSES - 1),
                        )

        def by_half(b):
            return bank[b][:].rearrange("j (p u d) -> j u p d", u=2, d=2)

        relus = {}

        def relu(j, us=BOTH):
            nc.scalar.activation(relus[j].rearrange("j (u p d) -> j u p d", u=2, d=2)[:, us], by_half(AB[j][0])[:, us], RELU)

        def product(j, us=BOTH):
            nc.vector.tensor_tensor(
                pairs[j][:].bitcast(BF16).rearrange("j u (p d) -> j u p d", d=2)[:, us],
                by_half(AB[j][1])[:, us],
                relus[j].rearrange("j (u p d) -> j u p d", u=2, d=2)[:, us],
                MULT,
            )

        def turn(j, b, width, at):
            dst = bank[b][:, : 2 * width].rearrange("p (u j) -> p u j", u=2)
            for u in range(2):
                nc.tensor.transpose(dst[:, u, at : at + P], pairs[j][:, u], ident[:])

        def copy_turned(b, lo, hi, copy=nc.scalar.copy):
            copy(
                hb[:, lo * PACK : hi * PACK].bitcast(F32).rearrange("p (j u) -> p j u", u=2),
                bank[b][:, : 2 * (hi - lo)].rearrange("p (u j) -> p j u", u=2),
            )

        def quantize_h(lo, hi):
            nc.vector.quantize_mx(out=hq[:, lo:hi].bitcast(FP8X4), scales=hs[:, lo:hi], in_=hb[:, lo * PACK : hi * PACK])

        def second_layer(lo, hi, m, b, at):
            e = lo // C
            nc.tensor.matmul_mx(
                out=bank[b][:, at : at + hi - lo],
                lhsT=w2c[:, e, 2 * m * P : 2 * (m + 1) * P].bitcast(FP4X4),
                lhsT_scale=w2s[:, e, m * P : (m + 1) * P],
                rhs=hq[:, lo:hi].bitcast(FP8X4),
                rhs_scale=hs[:, lo:hi],
                start=True,
                stop=True,
            )

        def copy_y(lo, hi, m, b, at, copy=nc.scalar.copy):
            copy(y[m][:, lo:hi], bank[b][:, at : at + hi - lo])

        stage(0, 0, e2, "opening")
        stage(0, e2, S)
        stage(1, 0, e2, "second")
        stage(2, 0, e1)
        stage(2, e1, e2)
        stage(1, e2, e3, "second")
        rounded[0, e2] = keep.tile([P, PACK * e2], BF16, name="xb0", tag="opening", align_bytes=64)[:]
        rounded[0, 0] = keep.tile([P, PACK * C], BF16, name="xb00", tag="early", align_bytes=64)[:]
        stage(1, e3, S, "early")
        gather_scalar(0, 0, e2)
        gather_gated(0, e2, e2 + HEAD, (0,))
        gather_gated(0, e2 + HEAD, S, (0,), e2)
        gather_gated(0, e2, S, (1, 2, 3))
        gather_scalar(1, 0, e2)
        weave_gated(0, 0, e1, 0)
        weave_gated(0, e1, e2, 0)
        quantize_x(0, 0, e1)
        weave(0, e2, S)
        quantize_x(0, e1, e2)
        first_layer((0, 1), (0,))
        first_layer((2, 3), (0,))
        gather_gated(1, e3, S, (0,))
        gather_scalar(2, 0, e1)
        gather_scalar(2, e1, e2)
        weave_gated(1, 0, e1, 0)
        weave_gated(1, e1, e2, 0)
        quantize_x(1, 0, e1)
        weave_gated(2, 0, e1)
        quantize_x(1, e1, e2)
        quantize_x(2, 0, e1)
        first_layer((0, 1), (1, 2))
        first_layer((2, 3), (1,))
        gather_scalar(1, e2, e3)

        late_x = keep.tile([P, H], F32, name="late_x", align_bytes=64)
        relus[2] = late_x[:]
        rounded[2, t5] = late_x[:, : H // 2].bitcast(BF16)
        for j in (0, 1, 3, 4, 5, 6, 7):
            relus[j] = keep.tile([P, H], F32, name=f"relu{j}")[:]
        gather_gated(1, e3, S, (1,))
        weave_gated(2, e1, e2)
        quantize_x(0, e2, S)
        quantize_x(2, e1, e2)
        first_layer((2, 3), (2,))
        gather_gated(1, e3, S, (2,))
        weave_gated(1, e2, e3)
        gather_gated(1, e3, S, (3,))
        quantize_x(1, e2, e3)
        weave(1, e3, S)
        relu(0)
        relu(1)
        stage(2, e2, e3, "after0")
        gather_scalar(2, e2, e3)
        relu(2)
        relu(3)
        own_scales[1, 3] = keep.tile([P, C], U8, name="xs_e3", tag="after0s", align_bytes=64)
        own_scales[2, 2] = keep.tile([P, C], U8, name="xs_e2", tag="after1s", align_bytes=64)
        late = keep.tile([P, PACK * C], F32, name="late", tag="after1", align_bytes=64)
        for lo, hi in ((e3, t7), (t7, S)):
            stages[2, lo] = late[:, (lo - e3) * PACK : (hi - e3) * PACK]
            gather_scalar(2, lo, hi)
        product(0)
        quantize_x(1, e3, S)
        product(1)
        weave_gated(2, e2, t5, e2)
        product(2)
        quantize_x(2, e2, t5)
        product(3)
        first_layer((4, 5), (0, 1), (0,))
        first_layer((4,), (0, 1), (1,))
        first_layer((6,), (0, 1), (0,))
        first_layer((5,), (0, 1), (1,))
        for j in range(2):
            turn(j, 6, C, j * P)
        first_layer((6,), (0, 1), (1,))
        first_layer((4,), (2,))
        copy_turned(6, 0, e1)
        first_layer((7,), (0, 1), (0,))
        weave_gated(2, t5, e3, e2)
        weave_gated(2, e3, t7)
        quantize_x(2, t5, e3)
        first_layer((5,), (2,))
        first_layer((7,), (0,), (1,))
        weave_gated(2, t7, S)
        quantize_x(2, e3, t7)
        quantize_x(2, t7, S)
        first_layer((6, 7), (2,), (0,))
        first_layer((6,), (2,), (1,))
        first_layer((7,), (1, 2), (1,))
        relu(4)
        relu(5)
        relu(6)
        relu(7, LOW)
        relu(7, HIGH)
        product(4)
        product(5)
        product(6)
        product(7, LOW)
        product(7, HIGH)
        for j in range(2):
            turn(2 + j, 0, C, j * P)
        for j in range(2):
            turn(4 + j, 2, C, j * P)
        turn(6, 4, P, 0)
        turn(7, 7, P, 0)
        quantize_h(0, e1)
        copy_turned(0, e1, e2)
        copy_turned(2, e2, e3)
        copy_turned(4, e3, t7, nc.vector.tensor_copy)
        copy_turned(7, t7, S)
        quantize_h(e1, e2)
        quantize_h(e3, t7)
        quantize_h(e2, e3)
        quantize_h(t7, S)
        second_layer(0, e1, 0, 6, 0)
        second_layer(0, e1, 1, 6, C)
        second_layer(e1, e2, 0, 5, 0)
        second_layer(e1, e2, 1, 4, 0)
        second_layer(e2, e3, 0, 1, 0)
        second_layer(e3, t7, 0, 3, 0)
        second_layer(t7, S, 0, 7, 0)
        copy_y(0, e1, 0, 6, 0)
        copy_y(0, e1, 1, 6, C)
        copy_y(e1, e2, 0, 5, 0)
        copy_y(e2, e3, 0, 1, 0)
        copy_y(e1, e2, 1, 4, 0, nc.vector.tensor_copy)
        copy_y(e3, t7, 0, 3, 0, nc.vector.tensor_copy)
        copy_y(t7, S, 0, 7, 0, nc.vector.tensor_copy)
        second_layer(e2, e3, 1, 4, 0)
        second_layer(e3, S, 1, 4, C)
        copy_y(e2, S, 1, 4, 0, nc.vector.tensor_copy)

        all_cuts = ((0, 160, 320, T), (0, 192, 384, T))
        for m in range(N // P):
            cuts = all_cuts[m]
            for lo, hi in zip(cuts, cuts[1:]):
                cols = slice(m * T + lo, m * T + hi)
                nc.scalar.activation(first[:, cols], y[m][:].indirect(pos1_sb[:, lo // 16 : hi // 16]), COPY)
                nc.vector.tensor_tensor(
                    total[:, cols], y[m][:].indirect(pos2_sb[:, lo // 16 : hi // 16]), first[:, cols], ADD
                )
        for m, lo, hi in ((0, 0, T), (1, 0, cuts[2]), (1, cuts[2], T)):
            nc.sync.dma_start(out[m * P : (m + 1) * P, lo:hi], total[:, m * T + lo : m * T + hi])
